import numpy as np
import ml_dtypes


def mxq(x, axis, fmt="e4m3"):
    dtype, down = {"e4m3": (ml_dtypes.float8_e4m3fn, 7), "e5m2": (ml_dtypes.float8_e5m2, 14)}[fmt]
    v = np.moveaxis(np.asarray(x, np.float32).astype(ml_dtypes.bfloat16).astype(np.float64), axis, -1)
    blocks = v.reshape(v.shape[:-1] + (-1, 32))
    amax = np.abs(blocks).max(-1, keepdims=True)
    byte = np.maximum(np.where(amax > 0, np.frexp(amax)[1] - 1 + 127, 0) - down, 1)
    scale = np.exp2(byte - 127.0)
    codes = (blocks / scale).astype(np.float32).astype(dtype).astype(np.float64)
    return np.moveaxis((codes * scale).reshape(v.shape), -1, axis)


WIDE = False


def mx_kscale(k):
    if not WIDE:
        return np.ones(k)
    levels = np.array([10, -10, 5, -5, 0])
    if k % 512:
        return np.exp2(np.random.permutation(np.resize(levels, k // 32))).repeat(32)
    a = np.empty((k // 512, 16))
    for p in range(k // 512):
        a[p, :8] = np.random.permutation(np.resize(levels, 8))
        for g in range(8):
            far = levels[np.abs(levels - a[p, g]) >= 10]
            a[p, g + 8] = far[np.random.randint(len(far))]
    return np.exp2(a.ravel()).repeat(32)


def f64(x):
    return np.asarray(x).astype(np.float64)


def striped(idx):
    return np.tile(idx.reshape(-1, 16).T, (8, 1)).astype(np.uint16)


def unstriped(offs):
    return offs[:16].T.reshape(-1).astype(np.int64)


E2M1 = np.array([0.0, 0.5, 1.0, 1.5, 2.0, 3.0, 4.0, 6.0, -0.0, -0.5, -1.0, -1.5, -2.0, -3.0, -4.0, -6.0])


def pack_weight(w, fmt):
    k, n = w.shape
    w = f64(np.asarray(w, np.float32).astype(ml_dtypes.bfloat16)).reshape(k // 32, 32, n)
    amax = np.abs(w).max(1)
    if fmt == "e4m3":
        byte = np.frexp(amax)[1] - 1 + 127 - 7
    else:
        mant, ex = np.frexp(amax / 6.0)
        byte = np.where(mant > 0.5, ex, ex - 1) + 127
    byte = np.clip(np.where(amax > 0, byte, 1), 1, 254)
    scaled = (w * np.exp2(127.0 - byte)[:, None, :]).reshape(k, n).astype(np.float32)
    by_word = np.ascontiguousarray(scaled.reshape(k // 512, 128, 4, n).transpose(0, 1, 3, 2))
    if fmt == "e4m3":
        words = by_word.astype(ml_dtypes.float8_e4m3fn).view(np.uint8)
    else:
        c = by_word.astype(ml_dtypes.float4_e2m1fn).view(np.uint8) & 0xF
        words = (c[..., 0::2] | (c[..., 1::2] << 4)).reshape(k // 512, 128, 2 * n)
    return np.ascontiguousarray(words), np.ascontiguousarray(byte.astype(np.uint8).reshape(k // 512, 16, n))


def unpack_weight(words, scales, fmt):
    g, _, n = scales.shape
    words = np.ascontiguousarray(words).reshape(g, 128, n, -1)
    if fmt == "e4m3":
        vals = words.view(ml_dtypes.float8_e4m3fn).astype(np.float64)
    else:
        nib = np.empty((g, 128, n, 4), np.uint8)
        nib[..., 0::2] = words & 0xF
        nib[..., 1::2] = words >> 4
        vals = E2M1[nib]
    vals = vals * np.repeat(np.exp2(scales.astype(np.float64) - 127.0), 8, axis=1)[..., None]
    return vals.transpose(0, 1, 3, 2).reshape(g * 512, n)


def gelu(v):
    return 0.5 * v * (1.0 + np.tanh(np.sqrt(2.0 / np.pi) * (v + 0.044715 * v**3)))


T, S, K, H, N = 2048, 1024, 1024, 512, 512

def setup_inputs():
    n = np.random.standard_normal
    s = mx_kscale(K)[:, None]
    u = mx_kscale(H)[:, None]
    tab_words, tab_scales = pack_weight(n((K, T)) * s, "e4m3")
    w2_words, w2_scales = pack_weight(n((K, H)) / np.sqrt(K) / s, "e2m1")
    w3_words, w3_scales = pack_weight(n((K, H)) / np.sqrt(K) / s * u.T, "e4m3")
    o2_words, o2_scales = pack_weight(n((H, N)) / np.sqrt(H) / u, "e4m3")
    return {
        "tab_words": tab_words, "tab_scales": tab_scales,
        "offs": striped(np.random.permutation(T)[:S]),
        "gT": n((N, T)).astype(np.float32),
        "w1": (n((K, H)) / np.sqrt(K) / s).astype(np.float32),
        "w2_words": w2_words, "w2_scales": w2_scales,
        "w3_words": w3_words, "w3_scales": w3_scales,
        "gain1": (np.exp(0.3 * n(H)) * u[:, 0]).astype(np.float32),
        "gain2": (1.5 * np.exp(0.3 * n(H)) * u[:, 0]).astype(np.float32),
        "b3": (0.5 * n(H) * u[:, 0]).astype(np.float32),
        "o1": (n((H, N)) / np.sqrt(H) / u).astype(np.float32),
        "o2_words": o2_words, "o2_scales": o2_scales,
        "o3": (n((H, N)) / np.sqrt(H) / u).astype(np.float32),
    }

def reference(tab_words, tab_scales, offs, gT, w1, w2_words, w2_scales, w3_words, w3_scales,
              gain1, gain2, b3, o1, o2_words, o2_scales, o3):
    v = unpack_weight(tab_words, tab_scales, "e4m3")[:, unstriped(offs)]
    h1 = np.tanh(mxq(f64(w1), 0, "e4m3").T @ v) * f64(gain1)[:, None]
    x2 = unpack_weight(w2_words, w2_scales, "e2m1").T @ v
    h2 = 1.0 / (1.0 + np.exp(-x2)) * f64(gain2)[:, None]
    h3 = (unpack_weight(w3_words, w3_scales, "e4m3").T @ v) + f64(b3)[:, None]
    y = (mxq(f64(o1), 0, "e4m3").T @ mxq(h1, 0, "e4m3")
              + unpack_weight(o2_words, o2_scales, "e4m3").T @ mxq(h2, 0, "e4m3")
              + mxq(f64(o3), 0, "e4m3").T @ mxq(h3, 0, "e4m3"))
    g = f64(gT)[:, unstriped(offs)]
    new = g * y
    out = f64(gT).copy()
    out[:, unstriped(offs)] = new
    return out

@@ -1,0 +1,271 @@
+from contextlib import ExitStack
+
+import concourse.mybir as mybir
+
+T, S, K, H, N = 2048, 1024, 1024, 512, 512
+FLOPS = 2 * S * (3 * K * H + 3 * H * N)
+
+F32 = mybir.dt.float32
+BF16 = mybir.dt.bfloat16
+I32 = mybir.dt.int32
+U32 = mybir.dt.uint32
+U16 = mybir.dt.uint16
+U8 = mybir.dt.uint8
+FP8X4 = mybir.dt.float8_e4m3fn_x4
+FP4X4 = mybir.dt.float4_e2m1fn_x4
+ALU = mybir.AluOpType
+ACT = mybir.ActivationFunctionType
+
+P = 128
+PACK = 4
+PASSES = K // (P * PACK)
+QUADS = 4
+CH = 256
+CHUNKS = S // CH
+NT = N // P
+ON_VECTOR = 4
+
+
+def tile_list_fader_balance_mix_kernel(tc, tab_words, tab_scales, offs, gT, w1, w2_words, w2_scales,
+                                                 w3_words, w3_scales, gain1, gain2, b3, o1, o2_words, o2_scales,
+                                                 o3, out):
+    nc = tc.nc
+    with ExitStack() as ctx:
+        keep = ctx.enter_context(tc.tile_pool(name="keep", bufs=1))
+        work = ctx.enter_context(tc.tile_pool(name="work", bufs=2))
+        psum = ctx.enter_context(tc.psum_pool(name="psum", bufs=1))
+
+        def held(shape, dtype, name):
+            return keep.tile(shape, dtype, name=name, align_bytes=64)
+
+        offsets = keep.tile([P, S // 16], U16, name="offsets")
+        nc.sync.dma_start(offsets[:], offs)
+
+        tab_sc = keep.tile([P, T], U8, name="tab_sc", tag="plane_slot", align_bytes=64)
+        w_sc_raw = keep.tile([P, PASSES * H], U8, name="w_sc_raw", tag="w_sc_slot", align_bytes=64)
+        v_sc_low = held([P, S], U8, "v_sc_low")
+        o2_sc = held([P, N], U8, "o2_sc")
+        for plane in (tab_sc, w_sc_raw, v_sc_low, o2_sc):
+            nc.vector.memset(plane[:].bitcast(I32), 0)
+        for q in range(QUADS):
+            nc.scalar.dma_start(out=tab_sc[32 * q : 32 * q + 8, :].bitcast(I32),
+                              in_=tab_scales[:, 4 * q : 4 * q + 4, :].bitcast(I32))
+        for first, scales in ((0, w2_scales), (4, w3_scales)):
+            for q in range(QUADS):
+                queue = nc.scalar if first == 0 and q < 2 else nc.gpsimd
+                rows = slice(32 * q + first, 32 * q + first + 4)
+                queue.dma_start(out=w_sc_raw[rows, :].bitcast(I32).rearrange("r (a c) -> r a c", a=PASSES),
+                                    in_=scales[:, 4 * q : 4 * q + 4, :].bitcast(I32).rearrange("a r c -> r a c"))
+        b3_t = held([P, PACK], F32, "b3_t")
+        nc.gpsimd.dma_start(out=b3_t[:], in_=b3.rearrange("(p t) -> p t", t=PACK))
+
+        def ring(shape, dtype, name):
+            return keep.tile(shape, dtype, name=name, tag="ring", bufs=3, align_bytes=64)
+
+        tab_w = [ring([P, T], I32, f"tab_w{a}") for a in range(PASSES)]
+        w1_raw = [ring([P, PACK, H], F32, "w1_raw0")]
+        warm = held([P, 2], F32, "warm")
+        nc.vector.memset(warm[:, 0:1], 0.0)
+        nc.scalar.activation(warm[:, 1:2], warm[:, 0:1], ACT.Sigmoid)
+
+        def load_tab(a):
+            nc.sync.dma_start(out=tab_w[a][:], in_=tab_words[a].rearrange("p t i -> p (t i)").bitcast(I32))
+
+        def load_rows(tile, rows):
+            nc.sync.dma_start(out=tile[:], in_=rows.rearrange("(p j) c -> p j c", j=PACK))
+
+        load_tab(0)
+        load_tab(1)
+        load_rows(w1_raw[0], w1[0 : P * PACK, :])
+
+        v_w = [held([P, S], U32, f"v_w{a}") for a in range(PASSES)]
+        for a in range(PASSES):
+            nc.vector.tensor_copy(v_w[a][:], tab_w[a][:].bitcast(U32).indirect(offsets[:]))
+        v_sc = held([P, S], U8, "v_sc")
+        nc.vector.tensor_copy(v_sc[:], tab_sc[:].indirect(offsets[:]))
+        for q in range(QUADS):
+            nc.scalar.dma_start(out=v_sc_low[32 * q : 32 * q + 4, :].bitcast(I32),
+                                in_=v_sc[32 * q + 4 : 32 * q + 8, :].bitcast(I32))
+        w1_raw.append(ring([P, PACK, H], F32, "w1_raw1"))
+        load_rows(w1_raw[1], w1[P * PACK : K, :])
+        w23_raw = ring([P, PASSES * 6 * H], U8, "w23_raw")
+        w3_raw = w23_raw[:, 0 : PASSES * 4 * H].bitcast(I32)
+        w2_raw = w23_raw[:, PASSES * 4 * H : PASSES * 6 * H]
+        nc.sync.dma_start(out=w3_raw.rearrange("p (a c) -> p a c", a=PASSES),
+                          in_=w3_words.rearrange("a p c i -> p a (c i)").bitcast(I32))
+        nc.sync.dma_start(out=w2_raw.bitcast(I32).rearrange("p (a c) -> p a c", a=PASSES),
+                          in_=w2_words.bitcast(I32).rearrange("a p c -> p a c"))
+
+        w2_codes = held([P, PASSES * 2 * H], U8, "w2_codes")
+        w3_codes = held([P, PASSES * H], I32, "w3_codes")
+        w_sc = held([P, PASSES * H], U8, "w_sc")
+
+        def permute(dst, src):
+            nc.vector.tensor_copy(dst.rearrange("p (a t m) -> p a m t", a=PASSES, t=PACK),
+                                  src.rearrange("p (a m t) -> p a m t", a=PASSES, t=PACK))
+
+        permute(w3_codes[:], w3_raw)
+        permute(w_sc[:], w_sc_raw[:])
+        permute(w2_codes[:].bitcast(U16), w2_raw.bitcast(U16))
+
+        vecs = keep.tile([P, 2, 8], F32, name="vecs", tag="plane_slot", align_bytes=64)
+        gain2_t, gain1_t = (vecs[:, i, 0:PACK] for i in range(2))
+        for tile, vec in ((gain1_t, gain1), (gain2_t, gain2)):
+            nc.gpsimd.dma_start(out=tile, in_=vec.rearrange("(p t) -> p t", t=PACK))
+        for q in range(QUADS):
+            nc.gpsimd.dma_start(out=o2_sc[32 * q : 32 * q + 4, :].bitcast(I32),
+                                in_=o2_scales[0, 4 * q : 4 * q + 4, :].bitcast(I32))
+
+        w1_codes = [held([P, H], U32, f"w1_codes{a}") for a in range(PASSES)]
+        w1_sc = [held([P, H], U8, f"w1_sc{a}") for a in range(PASSES)]
+        for a in range(PASSES):
+            w1_bf = keep.tile([P, PACK * H], BF16, name="w1_bf", tag=f"w1_slot{a}", align_bytes=64)
+            nc.scalar.copy(w1_bf[:].rearrange("p (t m j) -> p m j t", t=PACK, j=PACK),
+                           w1_raw[a][:].rearrange("p j (m t) -> p m j t", t=PACK))
+            nc.vector.quantize_mx(out=w1_codes[a][:].bitcast(FP8X4), scales=w1_sc[a][:], in_=w1_bf[:])
+
+        o1_raw = ring([P, PACK, N], F32, "o1_raw")
+        load_rows(o1_raw, o1)
+        o3_raw = ring([P, PACK, N], F32, "o3_raw")
+        load_rows(o3_raw, o3)
+        o2_codes = keep.tile([P, N], I32, name="o2_codes", tag="w1_slot0", align_bytes=64)
+        nc.sync.dma_start(out=o2_codes[:], in_=o2_words[0].rearrange("p c i -> p (c i)").bitcast(I32))
+        state = [ring([P, T], F32, "state0"),
+                 keep.tile([P, T], F32, name="state1", tag="w1_slot1", align_bytes=64)]
+        for n in range(2):
+            nc.sync.dma_start(out=state[n][:], in_=gT[n * P : (n + 1) * P, :])
+
+        o_q = []
+        for name, raw in (("o1", o1_raw), ("o3", o3_raw)):
+            o_bf = held([P, N, PACK], BF16, f"{name}_bf")
+            for n in range(NT):
+                cols = slice(n * P, (n + 1) * P)
+                nc.gpsimd.tensor_scalar(o_bf[:, cols, :], raw[:, :, cols].rearrange("p j c -> p c j"), 1.0, 0.0,
+                                        ALU.mult, ALU.add)
+            codes = held([P, N], U32, f"{name}_codes")
+            scales = held([P, N], U8, f"{name}_sc")
+            for h in range(2):
+                cols = slice(h * N // 2, (h + 1) * N // 2)
+                nc.vector.quantize_mx(out=codes[:, cols].bitcast(FP8X4), scales=scales[:, cols],
+                                      in_=o_bf[:, cols, :].rearrange("p c j -> p (c j)"))
+            o_q.append((codes, scales))
+        for n in range(2, NT):
+            state.append(ring([P, T], F32, f"state{n}"))
+            nc.sync.dma_start(out=state[n][:], in_=gT[n * P : (n + 1) * P, :])
+        o_ops = (o_q[0], (o2_codes, o2_sc), o_q[1])
+
+        picked = [held([P, S], F32, f"picked{n}") for n in range(NT)]
+
+        def gather_state(n):
+            nc.vector.tensor_copy(picked[n][:], state[n][:].indirect(offsets[:]))
+
+        def w1_side(a, t):
+            cols = slice(t * P, (t + 1) * P)
+            return w1_codes[a][:, cols].bitcast(FP8X4), w1_sc[a][:, cols]
+
+        def w2_side(a, t):
+            first = a * H + t * P
+            return w2_codes[:, 2 * first : 2 * (first + P)].bitcast(FP4X4), w_sc[:, first : first + P]
+
+        def w3_side(a, t):
+            first = a * H + t * P
+            return w3_codes[:, first : first + P].bitcast(FP8X4), w_sc[4:P, first : first + P]
+
+        def first_product(dst, side, t, tokens, low):
+            for a in range(PASSES):
+                codes, scales = side(a, t)
+                if a == 0:
+                    plane = v_sc[:, tokens]
+                else:
+                    plane = v_sc_low[:, tokens] if low else v_sc[4:P, tokens]
+                nc.tensor.matmul_mx(out=dst, lhsT=codes, lhsT_scale=scales, rhs=v_w[a][:, tokens].bitcast(FP8X4),
+                                    rhs_scale=plane, start=(a == 0), stop=(a == PASSES - 1))
+
+        h_q = {name: (held([P, S], U32, f"{name}_codes"), held([P, S], U8, f"{name}_sc")) for name in ("h1", "h2", "h3")}
+
+        def quantize_h(name, c, h_bf):
+            codes, scales = h_q[name]
+            tokens = slice(c * CH, (c + 1) * CH)
+            nc.vector.quantize_mx(out=codes[:, tokens].bitcast(FP8X4), scales=scales[:, tokens], in_=h_bf[:])
+
+        def gated_branch(name, c, side, func, gain, width, low):
+            act = work.tile([P, PACK, CH], F32, name="act")
+            for pair in range(2):
+                bank = psum.tile([P, 2, CH], F32, name="x_bank", bufs=4)
+                for e in range(2):
+                    for s in range(0, CH, width):
+                        first_product(bank[:, e, s : s + width], side, 2 * pair + e,
+                                      slice(c * CH + s, c * CH + s + width), low)
+                nc.scalar.activation(act[:, 2 * pair : 2 * pair + 2, :], bank[:], func)
+            planes = keep.tile([P, PACK, CH], BF16, name="planes", tag=f"{name}_slot{c}")
+            for t in range(PACK):
+                nc.scalar.activation(planes[:, t, :], act[:, t, :], ACT.Copy, scale=gain[:, t : t + 1])
+            h_bf = work.tile([P, CH * PACK], BF16, name="h_bf", align_bytes=64, bufs=4)
+            nc.scalar.copy(h_bf[:].rearrange("p (c i t) -> p c t i", i=4, t=PACK),
+                           planes[:].rearrange("p t (c i) -> p c t i", i=4))
+            quantize_h(name, c, h_bf)
+
+        def affine_branch(c):
+            h_bf = work.tile([P, CH * PACK], BF16, name="h3_bf", align_bytes=64)
+            for s in range(0, CH, P):
+                bank = psum.tile([P, PACK, P], F32, name="x3_bank", bufs=2)
+                for t in range(PACK):
+                    first_product(bank[:, t, :], w3_side, t, slice(c * CH + s, c * CH + s + P), False)
+                nc.vector.tensor_tensor(h_bf[:, s * PACK : (s + P) * PACK].rearrange("p (n t) -> p n t", t=PACK),
+                                        bank[:].rearrange("p t n -> p n t"),
+                                        b3_t[:].unsqueeze(1).to_broadcast([P, P, PACK]), ALU.add)
+            quantize_h("h3", c, h_bf)
+
+        def affine_on_scalar(c):
+            planes = keep.tile([P, PACK, CH], BF16, name="planes", tag=f"h3_slot{c}")
+            for pair in range(2):
+                bank = psum.tile([P, 2, CH], F32, name="x_bank", bufs=4)
+                for e in range(2):
+                    first_product(bank[:, e, :], w3_side, 2 * pair + e, slice(c * CH, (c + 1) * CH), False)
+                for e in range(2):
+                    t = 2 * pair + e
+                    nc.scalar.activation(planes[:, t, :], bank[:, e, :], ACT.Identity, bias=b3_t[:, t : t + 1])
+            h_bf = work.tile([P, CH * PACK], BF16, name="h_bf", align_bytes=64, bufs=4)
+            nc.scalar.copy(h_bf[:].rearrange("p (c i t) -> p c t i", i=4, t=PACK),
+                           planes[:].rearrange("p t (c i) -> p c t i", i=4))
+            quantize_h("h3", c, h_bf)
+
+        def second_product(first, count, slot):
+            width = count * CH
+            tokens = slice(first * CH, first * CH + width)
+            per_bank = 512 // width
+            y = keep.tile([P, NT, width], F32, name="y", tag=slot)
+            for n0 in range(0, NT, per_bank):
+                bank = psum.tile([P, per_bank, width], F32, name="y_bank", bufs=2)
+                for e in range(per_bank):
+                    cols = slice((n0 + e) * P, (n0 + e + 1) * P)
+                    for b, name in enumerate(("h1", "h2", "h3")):
+                        nc.tensor.matmul_mx(out=bank[:, e, :], lhsT=o_ops[b][0][:, cols].bitcast(FP8X4),
+                                            lhsT_scale=o_ops[b][1][:, cols],
+                                            rhs=h_q[name][0][:, tokens].bitcast(FP8X4),
+                                            rhs_scale=h_q[name][1][:, tokens], start=(b == 0), stop=(b == 2))
+                nc.scalar.copy(y[:, n0 : n0 + per_bank, :], bank[:])
+                for n in range(n0, n0 + per_bank):
+                    if first == 0:
+                        gather_state(n)
+                    nc.vector.tensor_tensor(state[n][:].indirect(offsets[:, tokens.start // 16 : tokens.stop // 16]),
+                                            y[:, n, :], picked[n][:, tokens], ALU.mult)
+                    if tokens.stop == S:
+                        nc.sync.dma_start(out=out[n * P : (n + 1) * P, :], in_=state[n][:])
+
+        def gated(c):
+            gated_branch("h1", c, w1_side, ACT.Tanh, gain1_t, CH, False)
+            if c >= ON_VECTOR:
+                affine_on_scalar(c)
+            gated_branch("h2", c, w2_side, ACT.Sigmoid, gain2_t, P, True)
+
+        for c in range(ON_VECTOR):
+            affine_branch(c)
+        gated(0)
+        gated(1)
+        second_product(0, 1, "h2_slot1")
+        gated(2)
+        second_product(1, 1, "h2_slot2")
+        gated(3)
+        second_product(2, 1, "h2_slot3")
+        second_product(3, 1, "y_last")

@@ -24,6 +24,8 @@ CH = 256
 CHUNKS = S // CH
 NT = N // P
 ON_VECTOR = 4
+GP = 256
+ON_G = ()
 
 
 def tile_list_fader_balance_mix_kernel(tc, tab_words, tab_scales, offs, gT, w1, w2_words, w2_scales,
@@ -41,118 +43,112 @@ def tile_list_fader_balance_mix_kernel(tc, tab_words, tab_scales, offs, gT, w1, 
         offsets = keep.tile([P, S // 16], U16, name="offsets")
         nc.sync.dma_start(offsets[:], offs)
 
-        tab_sc = keep.tile([P, T], U8, name="tab_sc", tag="plane_slot", align_bytes=64)
-        w_sc_raw = keep.tile([P, PASSES * H], U8, name="w_sc_raw", tag="w_sc_slot", align_bytes=64)
+        def shared(shape, dtype, name, slot):
+            return keep.tile(shape, dtype, name=name, tag=slot, align_bytes=64)
+
+        tab_sc = held([P, T], U8, "tab_sc")
+        w_sc_raw = held([P, PASSES * H], U8, "w_sc_raw")
         v_sc_low = held([P, S], U8, "v_sc_low")
         o2_sc = held([P, N], U8, "o2_sc")
         for plane in (tab_sc, w_sc_raw, v_sc_low, o2_sc):
             nc.vector.memset(plane[:].bitcast(I32), 0)
         for q in range(QUADS):
-            nc.scalar.dma_start(out=tab_sc[32 * q : 32 * q + 8, :].bitcast(I32),
+            nc.sync.dma_start(out=tab_sc[32 * q : 32 * q + 8, :].bitcast(I32),
                               in_=tab_scales[:, 4 * q : 4 * q + 4, :].bitcast(I32))
         for first, scales in ((0, w2_scales), (4, w3_scales)):
             for q in range(QUADS):
                 queue = nc.scalar if first == 0 and q < 2 else nc.gpsimd
                 rows = slice(32 * q + first, 32 * q + first + 4)
                 queue.dma_start(out=w_sc_raw[rows, :].bitcast(I32).rearrange("r (a c) -> r a c", a=PASSES),
-                                    in_=scales[:, 4 * q : 4 * q + 4, :].bitcast(I32).rearrange("a r c -> r a c"))
-        b3_t = held([P, PACK], F32, "b3_t")
-        nc.gpsimd.dma_start(out=b3_t[:], in_=b3.rearrange("(p t) -> p t", t=PACK))
-
-        def ring(shape, dtype, name):
-            return keep.tile(shape, dtype, name=name, tag="ring", bufs=3, align_bytes=64)
-
-        tab_w = [ring([P, T], I32, f"tab_w{a}") for a in range(PASSES)]
-        w1_raw = [ring([P, PACK, H], F32, "w1_raw0")]
+                                in_=scales[:, 4 * q : 4 * q + 4, :].bitcast(I32).rearrange("a r c -> r a c"))
+        vecs = held([P, 3, 8], F32, "vecs")
+        b3_t, gain2_t, gain1_t = (vecs[:, i, 0:PACK] for i in range(3))
+        for tile, vec in ((b3_t, b3), (gain2_t, gain2), (gain1_t, gain1)):
+            nc.gpsimd.dma_start(out=tile, in_=vec.rearrange("(p t) -> p t", t=PACK))
+        for q in range(QUADS):
+            nc.gpsimd.dma_start(out=o2_sc[32 * q : 32 * q + 4, :].bitcast(I32),
+                                in_=o2_scales[0, 4 * q : 4 * q + 4, :].bitcast(I32))
         warm = held([P, 2], F32, "warm")
         nc.vector.memset(warm[:, 0:1], 0.0)
         nc.scalar.activation(warm[:, 1:2], warm[:, 0:1], ACT.Sigmoid)
 
-        def load_tab(a):
-            nc.sync.dma_start(out=tab_w[a][:], in_=tab_words[a].rearrange("p t i -> p (t i)").bitcast(I32))
+        tab_w = [shared([P, T], I32, f"tab_w{a}", f"tab_slot{a}") for a in range(PASSES)]
+        w3_raw = held([P, PASSES * H], I32, "w3_raw")
+        w2_raw = shared([P, PASSES * 2 * H], U8, "w2_raw", "w2_slot")
+        w1_raw = [held([P, PACK, H], F32, f"w1_raw{a}") for a in range(PASSES)]
+        o1_raw = held([P, PACK, N], F32, "o1_raw")
+        o3_raw = shared([P, PACK, N], F32, "o3_raw", "o3_slot")
+        o2_codes = held([P, N], I32, "o2_codes")
+        state = [held([P, T], F32, f"state{n}") for n in range(NT)]
 
         def load_rows(tile, rows):
             nc.sync.dma_start(out=tile[:], in_=rows.rearrange("(p j) c -> p j c", j=PACK))
 
-        load_tab(0)
-        load_tab(1)
-        load_rows(w1_raw[0], w1[0 : P * PACK, :])
+        def load_state(n):
+            nc.sync.dma_start(out=state[n][:], in_=gT[n * P : (n + 1) * P, :])
 
-        v_w = [held([P, S], U32, f"v_w{a}") for a in range(PASSES)]
         for a in range(PASSES):
-            nc.vector.tensor_copy(v_w[a][:], tab_w[a][:].bitcast(U32).indirect(offsets[:]))
+            nc.sync.dma_start(out=tab_w[a][:], in_=tab_words[a].rearrange("p t i -> p (t i)").bitcast(I32))
+        load_rows(w1_raw[0], w1[0 : P * PACK, :])
+        load_rows(w1_raw[1], w1[P * PACK : K, :])
+        nc.sync.dma_start(out=w3_raw[:].rearrange("p (a c) -> p a c", a=PASSES),
+                          in_=w3_words.rearrange("a p c i -> p a (c i)").bitcast(I32))
+        nc.sync.dma_start(out=w2_raw[:].bitcast(I32).rearrange("p (a c) -> p a c", a=PASSES),
+                          in_=w2_words.bitcast(I32).rearrange("a p c -> p a c"))
+        load_rows(o1_raw, o1)
+        load_state(0)
+        load_rows(o3_raw, o3)
+        nc.sync.dma_start(out=o2_codes[:], in_=o2_words[0].rearrange("p c i -> p (c i)").bitcast(I32))
+        load_state(1)
+        load_state(2)
+        load_state(3)
+
         v_sc = held([P, S], U8, "v_sc")
         nc.vector.tensor_copy(v_sc[:], tab_sc[:].indirect(offsets[:]))
         for q in range(QUADS):
             nc.scalar.dma_start(out=v_sc_low[32 * q : 32 * q + 4, :].bitcast(I32),
                                 in_=v_sc[32 * q + 4 : 32 * q + 8, :].bitcast(I32))
-        w1_raw.append(ring([P, PACK, H], F32, "w1_raw1"))
-        load_rows(w1_raw[1], w1[P * PACK : K, :])
-        w23_raw = ring([P, PASSES * 6 * H], U8, "w23_raw")
-        w3_raw = w23_raw[:, 0 : PASSES * 4 * H].bitcast(I32)
-        w2_raw = w23_raw[:, PASSES * 4 * H : PASSES * 6 * H]
-        nc.sync.dma_start(out=w3_raw.rearrange("p (a c) -> p a c", a=PASSES),
-                          in_=w3_words.rearrange("a p c i -> p a (c i)").bitcast(I32))
-        nc.sync.dma_start(out=w2_raw.bitcast(I32).rearrange("p (a c) -> p a c", a=PASSES),
-                          in_=w2_words.bitcast(I32).rearrange("a p c -> p a c"))
-
-        w2_codes = held([P, PASSES * 2 * H], U8, "w2_codes")
-        w3_codes = held([P, PASSES * H], I32, "w3_codes")
-        w_sc = held([P, PASSES * H], U8, "w_sc")
+        v_w = [held([P, S], U32, f"v_w{a}") for a in range(PASSES)]
+        for a in range(PASSES):
+            nc.vector.tensor_copy(v_w[a][:], tab_w[a][:].bitcast(U32).indirect(offsets[:]))
 
         def permute(dst, src):
             nc.vector.tensor_copy(dst.rearrange("p (a t m) -> p a m t", a=PASSES, t=PACK),
                                   src.rearrange("p (a m t) -> p a m t", a=PASSES, t=PACK))
 
-        permute(w3_codes[:], w3_raw)
+        w3_codes = held([P, PASSES * H], I32, "w3_codes")
+        w2_codes = held([P, PASSES * 2 * H], U8, "w2_codes")
+        w_sc = shared([P, PASSES * H], U8, "w_sc", "tab_slot1")
         permute(w_sc[:], w_sc_raw[:])
-        permute(w2_codes[:].bitcast(U16), w2_raw.bitcast(U16))
-
-        vecs = keep.tile([P, 2, 8], F32, name="vecs", tag="plane_slot", align_bytes=64)
-        gain2_t, gain1_t = (vecs[:, i, 0:PACK] for i in range(2))
-        for tile, vec in ((gain1_t, gain1), (gain2_t, gain2)):
-            nc.gpsimd.dma_start(out=tile, in_=vec.rearrange("(p t) -> p t", t=PACK))
-        for q in range(QUADS):
-            nc.gpsimd.dma_start(out=o2_sc[32 * q : 32 * q + 4, :].bitcast(I32),
-                                in_=o2_scales[0, 4 * q : 4 * q + 4, :].bitcast(I32))
+        permute(w3_codes[:], w3_raw[:])
+        permute(w2_codes[:].bitcast(U16), w2_raw[:].bitcast(U16))
 
         w1_codes = [held([P, H], U32, f"w1_codes{a}") for a in range(PASSES)]
         w1_sc = [held([P, H], U8, f"w1_sc{a}") for a in range(PASSES)]
         for a in range(PASSES):
-            w1_bf = keep.tile([P, PACK * H], BF16, name="w1_bf", tag=f"w1_slot{a}", align_bytes=64)
+            w1_bf = shared([P, PACK * H], BF16, "w1_bf", f"w1_slot{a}")
             nc.scalar.copy(w1_bf[:].rearrange("p (t m j) -> p m j t", t=PACK, j=PACK),
                            w1_raw[a][:].rearrange("p j (m t) -> p m j t", t=PACK))
             nc.vector.quantize_mx(out=w1_codes[a][:].bitcast(FP8X4), scales=w1_sc[a][:], in_=w1_bf[:])
 
-        o1_raw = ring([P, PACK, N], F32, "o1_raw")
-        load_rows(o1_raw, o1)
-        o3_raw = ring([P, PACK, N], F32, "o3_raw")
-        load_rows(o3_raw, o3)
-        o2_codes = keep.tile([P, N], I32, name="o2_codes", tag="w1_slot0", align_bytes=64)
-        nc.sync.dma_start(out=o2_codes[:], in_=o2_words[0].rearrange("p c i -> p (c i)").bitcast(I32))
-        state = [ring([P, T], F32, "state0"),
-                 keep.tile([P, T], F32, name="state1", tag="w1_slot1", align_bytes=64)]
-        for n in range(2):
-            nc.sync.dma_start(out=state[n][:], in_=gT[n * P : (n + 1) * P, :])
+        def cast_o(name, raw, slot):
+            o_bf = shared([P, N * PACK], BF16, f"{name}_bf", slot)
+            nc.gpsimd.tensor_scalar(o_bf[:].rearrange("p (c j) -> p c j", j=PACK), raw[:].rearrange("p j c -> p c j"),
+                                    1.0, 0.0, ALU.mult, ALU.add)
+            return o_bf
 
-        o_q = []
-        for name, raw in (("o1", o1_raw), ("o3", o3_raw)):
-            o_bf = held([P, N, PACK], BF16, f"{name}_bf")
-            for n in range(NT):
-                cols = slice(n * P, (n + 1) * P)
-                nc.gpsimd.tensor_scalar(o_bf[:, cols, :], raw[:, :, cols].rearrange("p j c -> p c j"), 1.0, 0.0,
-                                        ALU.mult, ALU.add)
-            codes = held([P, N], U32, f"{name}_codes")
+        o1_bf = cast_o("o1", o1_raw, "w1_slot1")
+        o3_bf = cast_o("o3", o3_raw, "w1_slot0")
+        late_codes = shared([P, 3 * S + 2 * N], U32, "late_codes", "o3_slot")
+        h_codes = late_codes[:, 0 : 3 * S]
+
+        def quantize_o(name, o_bf, first):
+            codes = late_codes[:, first : first + N]
             scales = held([P, N], U8, f"{name}_sc")
-            for h in range(2):
-                cols = slice(h * N // 2, (h + 1) * N // 2)
-                nc.vector.quantize_mx(out=codes[:, cols].bitcast(FP8X4), scales=scales[:, cols],
-                                      in_=o_bf[:, cols, :].rearrange("p c j -> p (c j)"))
-            o_q.append((codes, scales))
-        for n in range(2, NT):
-            state.append(ring([P, T], F32, f"state{n}"))
-            nc.sync.dma_start(out=state[n][:], in_=gT[n * P : (n + 1) * P, :])
-        o_ops = (o_q[0], (o2_codes, o2_sc), o_q[1])
+            nc.vector.quantize_mx(out=codes.bitcast(FP8X4), scales=scales[:], in_=o_bf[:])
+            return codes, scales
+
+        o_ops = (quantize_o("o1", o1_bf, 3 * S), (o2_codes, o2_sc), quantize_o("o3", o3_bf, 3 * S + N))
 
         picked = [held([P, S], F32, f"picked{n}") for n in range(NT)]
 
@@ -181,17 +177,30 @@ def tile_list_fader_balance_mix_kernel(tc, tab_words, tab_scales, offs, gT, w1, 
                 nc.tensor.matmul_mx(out=dst, lhsT=codes, lhsT_scale=scales, rhs=v_w[a][:, tokens].bitcast(FP8X4),
                                     rhs_scale=plane, start=(a == 0), stop=(a == PASSES - 1))
 
-        h_q = {name: (held([P, S], U32, f"{name}_codes"), held([P, S], U8, f"{name}_sc")) for name in ("h1", "h2", "h3")}
+        h_q = {name: (h_codes[:, b * S : (b + 1) * S], held([P, S], U8, f"{name}_sc"))
+               for b, name in enumerate(("h1", "h2", "h3"))}
 
         def quantize_h(name, c, h_bf):
             codes, scales = h_q[name]
             tokens = slice(c * CH, (c + 1) * CH)
             nc.vector.quantize_mx(out=codes[:, tokens].bitcast(FP8X4), scales=scales[:, tokens], in_=h_bf[:])
 
+        def interleave(name, c, planes, on_gpsimd):
+            h_bf = work.tile([P, CH * PACK], BF16, name="h_bf", align_bytes=64, bufs=6)
+            if on_gpsimd:
+                for s in range(0, CH, GP):
+                    nc.gpsimd.tensor_scalar(h_bf[:, s * PACK : (s + GP) * PACK].rearrange("p (n t) -> p n t", t=PACK),
+                                            planes[:, :, s : s + GP].rearrange("p t n -> p n t"), 1.0, 0.0,
+                                            ALU.mult, ALU.add)
+            else:
+                nc.scalar.copy(h_bf[:].rearrange("p (c i t) -> p c t i", i=4, t=PACK),
+                               planes[:].rearrange("p t (c i) -> p c t i", i=4))
+            quantize_h(name, c, h_bf)
+
         def gated_branch(name, c, side, func, gain, width, low):
             act = work.tile([P, PACK, CH], F32, name="act")
             for pair in range(2):
-                bank = psum.tile([P, 2, CH], F32, name="x_bank", bufs=4)
+                bank = psum.tile([P, 2, CH], F32, name="x_bank", bufs=5)
                 for e in range(2):
                     for s in range(0, CH, width):
                         first_product(bank[:, e, s : s + width], side, 2 * pair + e,
@@ -200,72 +209,83 @@ def tile_list_fader_balance_mix_kernel(tc, tab_words, tab_scales, offs, gT, w1, 
             planes = keep.tile([P, PACK, CH], BF16, name="planes", tag=f"{name}_slot{c}")
             for t in range(PACK):
                 nc.scalar.activation(planes[:, t, :], act[:, t, :], ACT.Copy, scale=gain[:, t : t + 1])
-            h_bf = work.tile([P, CH * PACK], BF16, name="h_bf", align_bytes=64, bufs=4)
-            nc.scalar.copy(h_bf[:].rearrange("p (c i t) -> p c t i", i=4, t=PACK),
-                           planes[:].rearrange("p t (c i) -> p c t i", i=4))
-            quantize_h(name, c, h_bf)
+            interleave(name, c, planes, (name, c) in ON_G)
 
         def affine_branch(c):
-            h_bf = work.tile([P, CH * PACK], BF16, name="h3_bf", align_bytes=64)
+            h_bf = work.tile([P, CH * PACK], BF16, name="h3_bf", align_bytes=64, bufs=4)
             for s in range(0, CH, P):
                 bank = psum.tile([P, PACK, P], F32, name="x3_bank", bufs=2)
                 for t in range(PACK):
                     first_product(bank[:, t, :], w3_side, t, slice(c * CH + s, c * CH + s + P), False)
                 nc.vector.tensor_tensor(h_bf[:, s * PACK : (s + P) * PACK].rearrange("p (n t) -> p n t", t=PACK),
                                         bank[:].rearrange("p t n -> p n t"),
-                                        b3_t[:].unsqueeze(1).to_broadcast([P, P, PACK]), ALU.add)
+                                        b3_t.unsqueeze(1).to_broadcast([P, P, PACK]), ALU.add)
             quantize_h("h3", c, h_bf)
 
         def affine_on_scalar(c):
             planes = keep.tile([P, PACK, CH], BF16, name="planes", tag=f"h3_slot{c}")
             for pair in range(2):
-                bank = psum.tile([P, 2, CH], F32, name="x_bank", bufs=4)
+                bank = psum.tile([P, 2, CH], F32, name="x_bank", bufs=5)
                 for e in range(2):
                     first_product(bank[:, e, :], w3_side, 2 * pair + e, slice(c * CH, (c + 1) * CH), False)
                 for e in range(2):
                     t = 2 * pair + e
                     nc.scalar.activation(planes[:, t, :], bank[:, e, :], ACT.Identity, bias=b3_t[:, t : t + 1])
-            h_bf = work.tile([P, CH * PACK], BF16, name="h_bf", align_bytes=64, bufs=4)
-            nc.scalar.copy(h_bf[:].rearrange("p (c i t) -> p c t i", i=4, t=PACK),
-                           planes[:].rearrange("p t (c i) -> p c t i", i=4))
-            quantize_h("h3", c, h_bf)
+            interleave("h3", c, planes, ("h3", c) in ON_G)
 
-        def second_product(first, count, slot):
-            width = count * CH
-            tokens = slice(first * CH, first * CH + width)
-            per_bank = 512 // width
-            y = keep.tile([P, NT, width], F32, name="y", tag=slot)
-            for n0 in range(0, NT, per_bank):
-                bank = psum.tile([P, per_bank, width], F32, name="y_bank", bufs=2)
-                for e in range(per_bank):
-                    cols = slice((n0 + e) * P, (n0 + e + 1) * P)
-                    for b, name in enumerate(("h1", "h2", "h3")):
-                        nc.tensor.matmul_mx(out=bank[:, e, :], lhsT=o_ops[b][0][:, cols].bitcast(FP8X4),
-                                            lhsT_scale=o_ops[b][1][:, cols],
-                                            rhs=h_q[name][0][:, tokens].bitcast(FP8X4),
-                                            rhs_scale=h_q[name][1][:, tokens], start=(b == 0), stop=(b == 2))
-                nc.scalar.copy(y[:, n0 : n0 + per_bank, :], bank[:])
-                for n in range(n0, n0 + per_bank):
-                    if first == 0:
-                        gather_state(n)
-                    nc.vector.tensor_tensor(state[n][:].indirect(offsets[:, tokens.start // 16 : tokens.stop // 16]),
-                                            y[:, n, :], picked[n][:, tokens], ALU.mult)
-                    if tokens.stop == S:
-                        nc.sync.dma_start(out=out[n * P : (n + 1) * P, :], in_=state[n][:])
+        def second_product(c, pair, slot):
+            tokens = slice(c * CH, (c + 1) * CH)
+            y = keep.tile([P, 2, CH], F32, name="y", tag=slot)
+            bank = psum.tile([P, 2, CH], F32, name="y_bank")
+            for e in range(2):
+                cols = slice((2 * pair + e) * P, (2 * pair + e + 1) * P)
+                for b, name in enumerate(("h1", "h2", "h3")):
+                    nc.tensor.matmul_mx(out=bank[:, e, :], lhsT=o_ops[b][0][:, cols].bitcast(FP8X4),
+                                        lhsT_scale=o_ops[b][1][:, cols],
+                                        rhs=h_q[name][0][:, tokens].bitcast(FP8X4),
+                                        rhs_scale=h_q[name][1][:, tokens], start=(b == 0), stop=(b == 2))
+            nc.scalar.copy(y[:], bank[:])
+            for e in range(2):
+                n = 2 * pair + e
+                if c == 0:
+                    gather_state(n)
+                nc.vector.tensor_tensor(state[n][:].indirect(offsets[:, tokens.start // 16 : tokens.stop // 16]),
+                                        y[:, e, :], picked[n][:, tokens], ALU.mult)
+                if c == CHUNKS - 1:
+                    nc.sync.dma_start(out=out[n * P : (n + 1) * P, :], in_=state[n][:])
+
+        def wide_product(n):
+            tokens = slice(2 * CH, S)
+            cols = slice(n * P, (n + 1) * P)
+            y = held([P, 2 * CH], F32, f"y_wide{n}")
+            bank = psum.tile([P, 2 * CH], F32, name="y_bank")
+            for b, name in enumerate(("h1", "h2", "h3")):
+                nc.tensor.matmul_mx(out=bank[:], lhsT=o_ops[b][0][:, cols].bitcast(FP8X4),
+                                    lhsT_scale=o_ops[b][1][:, cols],
+                                    rhs=h_q[name][0][:, tokens].bitcast(FP8X4),
+                                    rhs_scale=h_q[name][1][:, tokens], start=(b == 0), stop=(b == 2))
+            nc.scalar.copy(y[:], bank[:])
+            nc.vector.tensor_tensor(state[n][:].indirect(offsets[:, tokens.start // 16 : tokens.stop // 16]),
+                                    y[:], picked[n][:, tokens], ALU.mult)
+            nc.sync.dma_start(out=out[n * P : (n + 1) * P, :], in_=state[n][:])
 
         def gated(c):
-            gated_branch("h1", c, w1_side, ACT.Tanh, gain1_t, CH, False)
-            if c >= ON_VECTOR:
-                affine_on_scalar(c)
             gated_branch("h2", c, w2_side, ACT.Sigmoid, gain2_t, P, True)
+            gated_branch("h1", c, w1_side, ACT.Tanh, gain1_t, CH, False)
 
-        for c in range(ON_VECTOR):
-            affine_branch(c)
+        affine_branch(0)
+        affine_branch(1)
         gated(0)
+        affine_branch(2)
+        affine_branch(3)
         gated(1)
-        second_product(0, 1, "h2_slot1")
+        second_product(0, 0, "h1_slot1")
+        second_product(0, 1, "y01")
         gated(2)
-        second_product(1, 1, "h2_slot2")
+        second_product(1, 0, "h1_slot2")
+        second_product(1, 1, "y11")
         gated(3)
-        second_product(2, 1, "h2_slot3")
-        second_product(3, 1, "y_last")
+        second_product(2, 0, "h1_slot3")
+        second_product(3, 0, "y30")
+        for n in range(2, NT):
+            wide_product(n)

@@ -20,12 +20,12 @@ P = 128
 PACK = 4
 PASSES = K // (P * PACK)
 QUADS = 4
+LOW = 4
+GROUP = 16
 CH = 256
 CHUNKS = S // CH
 NT = N // P
-ON_VECTOR = 4
-GP = 256
-ON_G = ()
+O3_ON_SCALAR = 256
 
 
 def tile_list_fader_balance_mix_kernel(tc, tab_words, tab_scales, offs, gT, w1, w2_words, w2_scales,
@@ -40,46 +40,37 @@ def tile_list_fader_balance_mix_kernel(tc, tab_words, tab_scales, offs, gT, w1, 
         def held(shape, dtype, name):
             return keep.tile(shape, dtype, name=name, align_bytes=64)
 
-        offsets = keep.tile([P, S // 16], U16, name="offsets")
-        nc.sync.dma_start(offsets[:], offs)
-
         def shared(shape, dtype, name, slot):
             return keep.tile(shape, dtype, name=name, tag=slot, align_bytes=64)
 
+        def listed(entries):
+            return offsets[:, entries.start // GROUP : entries.stop // GROUP]
+
+        offsets = keep.tile([P, S // GROUP], U16, name="offsets")
+        nc.sync.dma_start(offsets[:], offs)
+
         tab_sc = held([P, T], U8, "tab_sc")
         w_sc_raw = held([P, PASSES * H], U8, "w_sc_raw")
-        v_sc_low = held([P, S], U8, "v_sc_low")
+        v_sc_raised = held([P, S], U8, "v_sc_raised")
         o2_sc = held([P, N], U8, "o2_sc")
-        for plane in (tab_sc, w_sc_raw, v_sc_low, o2_sc):
+        for plane in (tab_sc, w_sc_raw, v_sc_raised, o2_sc):
             nc.vector.memset(plane[:].bitcast(I32), 0)
-        for q in range(QUADS):
-            nc.sync.dma_start(out=tab_sc[32 * q : 32 * q + 8, :].bitcast(I32),
-                              in_=tab_scales[:, 4 * q : 4 * q + 4, :].bitcast(I32))
-        for first, scales in ((0, w2_scales), (4, w3_scales)):
-            for q in range(QUADS):
-                queue = nc.scalar if first == 0 and q < 2 else nc.gpsimd
+
+        b3_t, gain2_t, gain1_t = (held([P, PACK], F32, name) for name in ("b3_t", "gain2_t", "gain1_t"))
+        tab_w = [held([P, T], I32, f"tab_w{a}") for a in range(PASSES)]
+        w3_raw = shared([P, PASSES * H], I32, "w3_raw", "w3_slot")
+        w2_raw = held([P, PASSES * 2 * H], U8, "w2_raw")
+        w1_raw = [held([P, PACK, H], F32, f"w1_raw{a}") for a in range(PASSES)]
+        o1_raw = held([P, PACK, N], F32, "o1_raw")
+        o3_raw = held([P, PACK, N], F32, "o3_raw")
+        o2_codes = held([P, N], I32, "o2_codes")
+        state = [held([P, T], F32, f"state{n}") for n in range(NT)]
+
+        def load_w_scales(queue, scales, first, quads):
+            for q in quads:
                 rows = slice(32 * q + first, 32 * q + first + 4)
                 queue.dma_start(out=w_sc_raw[rows, :].bitcast(I32).rearrange("r (a c) -> r a c", a=PASSES),
                                 in_=scales[:, 4 * q : 4 * q + 4, :].bitcast(I32).rearrange("a r c -> r a c"))
-        vecs = held([P, 3, 8], F32, "vecs")
-        b3_t, gain2_t, gain1_t = (vecs[:, i, 0:PACK] for i in range(3))
-        for tile, vec in ((b3_t, b3), (gain2_t, gain2), (gain1_t, gain1)):
-            nc.gpsimd.dma_start(out=tile, in_=vec.rearrange("(p t) -> p t", t=PACK))
-        for q in range(QUADS):
-            nc.gpsimd.dma_start(out=o2_sc[32 * q : 32 * q + 4, :].bitcast(I32),
-                                in_=o2_scales[0, 4 * q : 4 * q + 4, :].bitcast(I32))
-        warm = held([P, 2], F32, "warm")
-        nc.vector.memset(warm[:, 0:1], 0.0)
-        nc.scalar.activation(warm[:, 1:2], warm[:, 0:1], ACT.Sigmoid)
-
-        tab_w = [shared([P, T], I32, f"tab_w{a}", f"tab_slot{a}") for a in range(PASSES)]
-        w3_raw = held([P, PASSES * H], I32, "w3_raw")
-        w2_raw = shared([P, PASSES * 2 * H], U8, "w2_raw", "w2_slot")
-        w1_raw = [held([P, PACK, H], F32, f"w1_raw{a}") for a in range(PASSES)]
-        o1_raw = held([P, PACK, N], F32, "o1_raw")
-        o3_raw = shared([P, PACK, N], F32, "o3_raw", "o3_slot")
-        o2_codes = held([P, N], I32, "o2_codes")
-        state = [held([P, T], F32, f"state{n}") for n in range(NT)]
 
         def load_rows(tile, rows):
             nc.sync.dma_start(out=tile[:], in_=rows.rearrange("(p j) c -> p j c", j=PACK))
@@ -87,77 +78,66 @@ def tile_list_fader_balance_mix_kernel(tc, tab_words, tab_scales, offs, gT, w1, 
         def load_state(n):
             nc.sync.dma_start(out=state[n][:], in_=gT[n * P : (n + 1) * P, :])
 
+        for tile, vec in ((b3_t, b3), (gain2_t, gain2), (gain1_t, gain1)):
+            nc.gpsimd.dma_start(out=tile[:], in_=vec.rearrange("(p t) -> p t", t=PACK))
+        load_w_scales(nc.scalar, w2_scales, 0, range(QUADS // 2))
+        for q in range(QUADS):
+            nc.sync.dma_start(out=tab_sc[32 * q : 32 * q + PASSES * LOW, :].bitcast(I32),
+                              in_=tab_scales[:, 4 * q : 4 * q + 4, :].bitcast(I32))
         for a in range(PASSES):
             nc.sync.dma_start(out=tab_w[a][:], in_=tab_words[a].rearrange("p t i -> p (t i)").bitcast(I32))
-        load_rows(w1_raw[0], w1[0 : P * PACK, :])
-        load_rows(w1_raw[1], w1[P * PACK : K, :])
-        nc.sync.dma_start(out=w3_raw[:].rearrange("p (a c) -> p a c", a=PASSES),
-                          in_=w3_words.rearrange("a p c i -> p a (c i)").bitcast(I32))
+        load_w_scales(nc.sync, w2_scales, 0, range(QUADS // 2, QUADS))
+        load_w_scales(nc.sync, w3_scales, LOW, range(QUADS))
+        for a in range(PASSES):
+            load_rows(w1_raw[a], w1[a * P * PACK : (a + 1) * P * PACK, :])
         nc.sync.dma_start(out=w2_raw[:].bitcast(I32).rearrange("p (a c) -> p a c", a=PASSES),
                           in_=w2_words.bitcast(I32).rearrange("a p c -> p a c"))
-        load_rows(o1_raw, o1)
-        load_state(0)
-        load_rows(o3_raw, o3)
-        nc.sync.dma_start(out=o2_codes[:], in_=o2_words[0].rearrange("p c i -> p (c i)").bitcast(I32))
-        load_state(1)
-        load_state(2)
-        load_state(3)
 
         v_sc = held([P, S], U8, "v_sc")
         nc.vector.tensor_copy(v_sc[:], tab_sc[:].indirect(offsets[:]))
         for q in range(QUADS):
-            nc.scalar.dma_start(out=v_sc_low[32 * q : 32 * q + 4, :].bitcast(I32),
-                                in_=v_sc[32 * q + 4 : 32 * q + 8, :].bitcast(I32))
+            nc.sync.dma_start(out=v_sc_raised[32 * q : 32 * q + 4, :].bitcast(I32),
+                              in_=v_sc[32 * q + LOW : 32 * q + LOW + 4, :].bitcast(I32))
+
+        nc.sync.dma_start(out=w3_raw[:].rearrange("p (a c) -> p a c", a=PASSES),
+                          in_=w3_words.rearrange("a p c i -> p a (c i)").bitcast(I32))
+        load_state(0)
+        load_rows(o1_raw, o1)
+        load_rows(o3_raw, o3)
+        nc.sync.dma_start(out=o2_codes[:], in_=o2_words[0].rearrange("p c i -> p (c i)").bitcast(I32))
+        for q in range(QUADS):
+            nc.gpsimd.dma_start(out=o2_sc[32 * q : 32 * q + 4, :].bitcast(I32),
+                                in_=o2_scales[0, 4 * q : 4 * q + 4, :].bitcast(I32))
+        for n in range(1, NT):
+            load_state(n)
+
         v_w = [held([P, S], U32, f"v_w{a}") for a in range(PASSES)]
         for a in range(PASSES):
             nc.vector.tensor_copy(v_w[a][:], tab_w[a][:].bitcast(U32).indirect(offsets[:]))
 
-        def permute(dst, src):
-            nc.vector.tensor_copy(dst.rearrange("p (a t m) -> p a m t", a=PASSES, t=PACK),
-                                  src.rearrange("p (a m t) -> p a m t", a=PASSES, t=PACK))
+        def reorder(dst, src, walk):
+            nc.vector.tensor_copy(dst.rearrange(f"p (a t m) -> p {walk}", a=PASSES, t=PACK),
+                                  src.rearrange(f"p (a m t) -> p {walk}", a=PASSES, t=PACK))
 
         w3_codes = held([P, PASSES * H], I32, "w3_codes")
         w2_codes = held([P, PASSES * 2 * H], U8, "w2_codes")
-        w_sc = shared([P, PASSES * H], U8, "w_sc", "tab_slot1")
-        permute(w_sc[:], w_sc_raw[:])
-        permute(w3_codes[:], w3_raw[:])
-        permute(w2_codes[:].bitcast(U16), w2_raw[:].bitcast(U16))
+        w_sc = held([P, PASSES * H], U8, "w_sc")
+        reorder(w_sc[:], w_sc_raw[:], "a t m")
+        reorder(w3_codes[:], w3_raw[:], "a m t")
+        reorder(w2_codes[:].bitcast(U16), w2_raw[:].bitcast(U16), "a t m")
 
-        w1_codes = [held([P, H], U32, f"w1_codes{a}") for a in range(PASSES)]
-        w1_sc = [held([P, H], U8, f"w1_sc{a}") for a in range(PASSES)]
+        w1_bf = held([P, PASSES * PACK * H], BF16, "w1_bf")
         for a in range(PASSES):
-            w1_bf = shared([P, PACK * H], BF16, "w1_bf", f"w1_slot{a}")
-            nc.scalar.copy(w1_bf[:].rearrange("p (t m j) -> p m j t", t=PACK, j=PACK),
+            dst = w1_bf[:, a * PACK * H : (a + 1) * PACK * H]
+            nc.scalar.copy(dst.rearrange("p (t m j) -> p m j t", t=PACK, j=PACK),
                            w1_raw[a][:].rearrange("p j (m t) -> p m j t", t=PACK))
-            nc.vector.quantize_mx(out=w1_codes[a][:].bitcast(FP8X4), scales=w1_sc[a][:], in_=w1_bf[:])
-
-        def cast_o(name, raw, slot):
-            o_bf = shared([P, N * PACK], BF16, f"{name}_bf", slot)
-            nc.gpsimd.tensor_scalar(o_bf[:].rearrange("p (c j) -> p c j", j=PACK), raw[:].rearrange("p j c -> p c j"),
-                                    1.0, 0.0, ALU.mult, ALU.add)
-            return o_bf
-
-        o1_bf = cast_o("o1", o1_raw, "w1_slot1")
-        o3_bf = cast_o("o3", o3_raw, "w1_slot0")
-        late_codes = shared([P, 3 * S + 2 * N], U32, "late_codes", "o3_slot")
-        h_codes = late_codes[:, 0 : 3 * S]
-
-        def quantize_o(name, o_bf, first):
-            codes = late_codes[:, first : first + N]
-            scales = held([P, N], U8, f"{name}_sc")
-            nc.vector.quantize_mx(out=codes.bitcast(FP8X4), scales=scales[:], in_=o_bf[:])
-            return codes, scales
-
-        o_ops = (quantize_o("o1", o1_bf, 3 * S), (o2_codes, o2_sc), quantize_o("o3", o3_bf, 3 * S + N))
-
-        picked = [held([P, S], F32, f"picked{n}") for n in range(NT)]
-
-        def gather_state(n):
-            nc.vector.tensor_copy(picked[n][:], state[n][:].indirect(offsets[:]))
+        w1_codes = shared([P, PASSES * H], U32, "w1_codes", "w3_slot")
+        w1_sc = held([P, PASSES * H], U8, "w1_sc")
+        nc.vector.quantize_mx(out=w1_codes[:].bitcast(FP8X4), scales=w1_sc[:], in_=w1_bf[:])
 
         def w1_side(a, t):
-            cols = slice(t * P, (t + 1) * P)
-            return w1_codes[a][:, cols].bitcast(FP8X4), w1_sc[a][:, cols]
+            first = a * H + t * P
+            return w1_codes[:, first : first + P].bitcast(FP8X4), w1_sc[:, first : first + P]
 
         def w2_side(a, t):
             first = a * H + t * P
@@ -165,127 +145,107 @@ def tile_list_fader_balance_mix_kernel(tc, tab_words, tab_scales, offs, gT, w1, 
 
         def w3_side(a, t):
             first = a * H + t * P
-            return w3_codes[:, first : first + P].bitcast(FP8X4), w_sc[4:P, first : first + P]
+            return w3_codes[:, first : first + P].bitcast(FP8X4), w_sc[LOW:P, first : first + P]
 
-        def first_product(dst, side, t, tokens, low):
+        planes_e4m3 = (v_sc[:], v_sc[LOW:P, :])
+        planes_e2m1 = (v_sc[:], v_sc_raised[:])
+
+        def first_product(dst, side, planes, t, entries):
             for a in range(PASSES):
                 codes, scales = side(a, t)
-                if a == 0:
-                    plane = v_sc[:, tokens]
-                else:
-                    plane = v_sc_low[:, tokens] if low else v_sc[4:P, tokens]
-                nc.tensor.matmul_mx(out=dst, lhsT=codes, lhsT_scale=scales, rhs=v_w[a][:, tokens].bitcast(FP8X4),
-                                    rhs_scale=plane, start=(a == 0), stop=(a == PASSES - 1))
+                nc.tensor.matmul_mx(out=dst, lhsT=codes, lhsT_scale=scales, rhs=v_w[a][:, entries].bitcast(FP8X4),
+                                    rhs_scale=planes[a][:, entries], start=(a == 0), stop=(a == PASSES - 1))
 
-        h_q = {name: (h_codes[:, b * S : (b + 1) * S], held([P, S], U8, f"{name}_sc"))
-               for b, name in enumerate(("h1", "h2", "h3"))}
+        h_codes = {name: held([P, S], U32, f"{name}_codes") for name in ("h1", "h2", "h3")}
+        h_sc = {name: held([P, S], U8, f"{name}_sc") for name in ("h1", "h2", "h3")}
 
         def quantize_h(name, c, h_bf):
-            codes, scales = h_q[name]
-            tokens = slice(c * CH, (c + 1) * CH)
-            nc.vector.quantize_mx(out=codes[:, tokens].bitcast(FP8X4), scales=scales[:, tokens], in_=h_bf[:])
+            entries = slice(c * CH, (c + 1) * CH)
+            nc.vector.quantize_mx(out=h_codes[name][:, entries].bitcast(FP8X4), scales=h_sc[name][:, entries],
+                                  in_=h_bf[:])
 
-        def interleave(name, c, planes, on_gpsimd):
-            h_bf = work.tile([P, CH * PACK], BF16, name="h_bf", align_bytes=64, bufs=6)
-            if on_gpsimd:
-                for s in range(0, CH, GP):
-                    nc.gpsimd.tensor_scalar(h_bf[:, s * PACK : (s + GP) * PACK].rearrange("p (n t) -> p n t", t=PACK),
-                                            planes[:, :, s : s + GP].rearrange("p t n -> p n t"), 1.0, 0.0,
-                                            ALU.mult, ALU.add)
-            else:
-                nc.scalar.copy(h_bf[:].rearrange("p (c i t) -> p c t i", i=4, t=PACK),
-                               planes[:].rearrange("p t (c i) -> p c t i", i=4))
-            quantize_h(name, c, h_bf)
-
-        def gated_branch(name, c, side, func, gain, width, low):
+        def gated_branch(name, c, side, planes, width, func, gain):
             act = work.tile([P, PACK, CH], F32, name="act")
-            for pair in range(2):
-                bank = psum.tile([P, 2, CH], F32, name="x_bank", bufs=5)
+            for pair in range(PACK // 2):
+                bank = psum.tile([P, 2, CH], F32, name="x_bank", bufs=4)
                 for e in range(2):
                     for s in range(0, CH, width):
-                        first_product(bank[:, e, s : s + width], side, 2 * pair + e,
-                                      slice(c * CH + s, c * CH + s + width), low)
+                        first_product(bank[:, e, s : s + width], side, planes, 2 * pair + e,
+                                      slice(c * CH + s, c * CH + s + width))
                 nc.scalar.activation(act[:, 2 * pair : 2 * pair + 2, :], bank[:], func)
-            planes = keep.tile([P, PACK, CH], BF16, name="planes", tag=f"{name}_slot{c}")
+            slices = shared([P, PACK, CH], BF16, "slices", f"{name}_slot{c}")
             for t in range(PACK):
-                nc.scalar.activation(planes[:, t, :], act[:, t, :], ACT.Copy, scale=gain[:, t : t + 1])
-            interleave(name, c, planes, (name, c) in ON_G)
-
-        def affine_branch(c):
-            h_bf = work.tile([P, CH * PACK], BF16, name="h3_bf", align_bytes=64, bufs=4)
-            for s in range(0, CH, P):
-                bank = psum.tile([P, PACK, P], F32, name="x3_bank", bufs=2)
-                for t in range(PACK):
-                    first_product(bank[:, t, :], w3_side, t, slice(c * CH + s, c * CH + s + P), False)
-                nc.vector.tensor_tensor(h_bf[:, s * PACK : (s + P) * PACK].rearrange("p (n t) -> p n t", t=PACK),
-                                        bank[:].rearrange("p t n -> p n t"),
-                                        b3_t.unsqueeze(1).to_broadcast([P, P, PACK]), ALU.add)
-            quantize_h("h3", c, h_bf)
-
-        def affine_on_scalar(c):
-            planes = keep.tile([P, PACK, CH], BF16, name="planes", tag=f"h3_slot{c}")
-            for pair in range(2):
-                bank = psum.tile([P, 2, CH], F32, name="x_bank", bufs=5)
-                for e in range(2):
-                    first_product(bank[:, e, :], w3_side, 2 * pair + e, slice(c * CH, (c + 1) * CH), False)
-                for e in range(2):
-                    t = 2 * pair + e
-                    nc.scalar.activation(planes[:, t, :], bank[:, e, :], ACT.Identity, bias=b3_t[:, t : t + 1])
-            interleave("h3", c, planes, ("h3", c) in ON_G)
-
-        def second_product(c, pair, slot):
-            tokens = slice(c * CH, (c + 1) * CH)
-            y = keep.tile([P, 2, CH], F32, name="y", tag=slot)
-            bank = psum.tile([P, 2, CH], F32, name="y_bank")
-            for e in range(2):
-                cols = slice((2 * pair + e) * P, (2 * pair + e + 1) * P)
-                for b, name in enumerate(("h1", "h2", "h3")):
-                    nc.tensor.matmul_mx(out=bank[:, e, :], lhsT=o_ops[b][0][:, cols].bitcast(FP8X4),
-                                        lhsT_scale=o_ops[b][1][:, cols],
-                                        rhs=h_q[name][0][:, tokens].bitcast(FP8X4),
-                                        rhs_scale=h_q[name][1][:, tokens], start=(b == 0), stop=(b == 2))
-            nc.scalar.copy(y[:], bank[:])
-            for e in range(2):
-                n = 2 * pair + e
-                if c == 0:
-                    gather_state(n)
-                nc.vector.tensor_tensor(state[n][:].indirect(offsets[:, tokens.start // 16 : tokens.stop // 16]),
-                                        y[:, e, :], picked[n][:, tokens], ALU.mult)
-                if c == CHUNKS - 1:
-                    nc.sync.dma_start(out=out[n * P : (n + 1) * P, :], in_=state[n][:])
-
-        def wide_product(n):
-            tokens = slice(2 * CH, S)
-            cols = slice(n * P, (n + 1) * P)
-            y = held([P, 2 * CH], F32, f"y_wide{n}")
-            bank = psum.tile([P, 2 * CH], F32, name="y_bank")
-            for b, name in enumerate(("h1", "h2", "h3")):
-                nc.tensor.matmul_mx(out=bank[:], lhsT=o_ops[b][0][:, cols].bitcast(FP8X4),
-                                    lhsT_scale=o_ops[b][1][:, cols],
-                                    rhs=h_q[name][0][:, tokens].bitcast(FP8X4),
-                                    rhs_scale=h_q[name][1][:, tokens], start=(b == 0), stop=(b == 2))
-            nc.scalar.copy(y[:], bank[:])
-            nc.vector.tensor_tensor(state[n][:].indirect(offsets[:, tokens.start // 16 : tokens.stop // 16]),
-                                    y[:], picked[n][:, tokens], ALU.mult)
-            nc.sync.dma_start(out=out[n * P : (n + 1) * P, :], in_=state[n][:])
+                nc.scalar.activation(slices[:, t, :], act[:, t, :], ACT.Copy, scale=gain[:, t : t + 1])
+            h_bf = work.tile([P, CH * PACK], BF16, name="h_bf", align_bytes=64, bufs=4)
+            nc.scalar.copy(h_bf[:].rearrange("p (c i t) -> p c t i", i=4, t=PACK),
+                           slices[:].rearrange("p t (c i) -> p c t i", i=4))
+            quantize_h(name, c, h_bf)
 
         def gated(c):
-            gated_branch("h2", c, w2_side, ACT.Sigmoid, gain2_t, P, True)
-            gated_branch("h1", c, w1_side, ACT.Tanh, gain1_t, CH, False)
+            gated_branch("h2", c, w2_side, planes_e2m1, P, ACT.Sigmoid, gain2_t)
+            gated_branch("h1", c, w1_side, planes_e4m3, CH, ACT.Tanh, gain1_t)
 
-        affine_branch(0)
-        affine_branch(1)
+        def affine(c):
+            h_bf = held([P, CH * PACK], BF16, f"h3_bf{c}")
+            for s in range(0, CH, P):
+                bank = psum.tile([P, PACK, P], F32, name="x3_bank", bufs=3)
+                for t in range(PACK):
+                    first_product(bank[:, t, :], w3_side, planes_e4m3, t, slice(c * CH + s, c * CH + s + P))
+                nc.vector.tensor_tensor(h_bf[:, s * PACK : (s + P) * PACK].rearrange("p (n t) -> p n t", t=PACK),
+                                        bank[:].rearrange("p t n -> p n t"),
+                                        b3_t[:].unsqueeze(1).to_broadcast([P, P, PACK]), ALU.add)
+            quantize_h("h3", c, h_bf)
+
+        def quantize_o(name, raw, on_scalar):
+            o_bf = held([P, N, PACK], BF16, f"{name}_bf")
+            for copy, cols in ((nc.scalar.copy, slice(0, on_scalar)), (nc.vector.tensor_copy, slice(on_scalar, N))):
+                if cols.start < cols.stop:
+                    copy(o_bf[:, cols, :].rearrange("p (c i) j -> p c j i", i=4),
+                         raw[:, :, cols].rearrange("p j (c i) -> p c j i", i=4))
+            codes = held([P, N], U32, f"{name}_codes")
+            scales = held([P, N], U8, f"{name}_sc")
+            nc.vector.quantize_mx(out=codes[:].bitcast(FP8X4), scales=scales[:],
+                                  in_=o_bf[:].rearrange("p c j -> p (c j)"))
+            return codes, scales
+
+        picked = [held([P, S], F32, f"picked{n}") for n in range(NT)]
+
+        def second_stage(tiles, entries, slot):
+            width = entries.stop - entries.start
+            y = shared([P, len(tiles), width], F32, "y", slot)
+            bank = psum.tile([P, len(tiles), width], F32, name="y_bank")
+            for e, n in enumerate(tiles):
+                cols = slice(n * P, (n + 1) * P)
+                for b, name in enumerate(("h1", "h2", "h3")):
+                    nc.tensor.matmul_mx(out=bank[:, e, :], lhsT=o_sides[b][0][:, cols].bitcast(FP8X4),
+                                        lhsT_scale=o_sides[b][1][:, cols],
+                                        rhs=h_codes[name][:, entries].bitcast(FP8X4),
+                                        rhs_scale=h_sc[name][:, entries], start=(b == 0), stop=(b == 2))
+            nc.scalar.copy(y[:], bank[:])
+            for e, n in enumerate(tiles):
+                if entries.start == 0:
+                    nc.vector.tensor_copy(picked[n][:], state[n][:].indirect(offsets[:]))
+                nc.vector.tensor_tensor(state[n][:].indirect(listed(entries)), y[:, e, :], picked[n][:, entries],
+                                        ALU.mult)
+                if entries.stop == S:
+                    nc.sync.dma_start(out=out[n * P : (n + 1) * P, :], in_=state[n][:])
+
+        def chunk(c):
+            return slice(c * CH, (c + 1) * CH)
+
         gated(0)
-        affine_branch(2)
-        affine_branch(3)
-        gated(1)
-        second_product(0, 0, "h1_slot1")
-        second_product(0, 1, "y01")
-        gated(2)
-        second_product(1, 0, "h1_slot2")
-        second_product(1, 1, "y11")
-        gated(3)
-        second_product(2, 0, "h1_slot3")
-        second_product(3, 0, "y30")
-        for n in range(2, NT):
-            wide_product(n)
+        affine(0)
+        affine(1)
+        o_sides = (quantize_o("o1", o1_raw, N), (o2_codes, o2_sc), quantize_o("o3", o3_raw, O3_ON_SCALAR))
+        affine(2)
+        affine(3)
+
+        upper, lower = (0, 1), (2, 3)
+        for c in range(CHUNKS - 1):
+            gated(c + 1)
+            second_stage(upper, chunk(c), f"h1_slot{c + 1}")
+            if c < CHUNKS - 2:
+                second_stage(lower, chunk(c), f"y_lower{c}")
+        second_stage(upper, chunk(CHUNKS - 1), "y_upper_last")
+        for n in lower:
+            second_stage((n,), slice((CHUNKS - 2) * CH, S), f"y_last{n}")

@@ -25,7 +25,8 @@ GROUP = 16
 CH = 256
 CHUNKS = S // CH
 NT = N // P
-O3_ON_SCALAR = 256
+BRANCHES = ("h1", "h2", "h3")
+RUN = 4
 
 
 def tile_list_fader_balance_mix_kernel(tc, tab_words, tab_scales, offs, gT, w1, w2_words, w2_scales,
@@ -62,7 +63,7 @@ def tile_list_fader_balance_mix_kernel(tc, tab_words, tab_scales, offs, gT, w1, 
         w2_raw = held([P, PASSES * 2 * H], U8, "w2_raw")
         w1_raw = [held([P, PACK, H], F32, f"w1_raw{a}") for a in range(PASSES)]
         o1_raw = held([P, PACK, N], F32, "o1_raw")
-        o3_raw = held([P, PACK, N], F32, "o3_raw")
+        o3_raw = shared([P, PACK, N], F32, "o3_raw", "o3_slot")
         o2_codes = held([P, N], I32, "o2_codes")
         state = [held([P, T], F32, f"state{n}") for n in range(NT)]
 
@@ -101,8 +102,8 @@ def tile_list_fader_balance_mix_kernel(tc, tab_words, tab_scales, offs, gT, w1, 
 
         nc.sync.dma_start(out=w3_raw[:].rearrange("p (a c) -> p a c", a=PASSES),
                           in_=w3_words.rearrange("a p c i -> p a (c i)").bitcast(I32))
-        load_state(0)
         load_rows(o1_raw, o1)
+        load_state(0)
         load_rows(o3_raw, o3)
         nc.sync.dma_start(out=o2_codes[:], in_=o2_words[0].rearrange("p c i -> p (c i)").bitcast(I32))
         for q in range(QUADS):
@@ -126,11 +127,12 @@ def tile_list_fader_balance_mix_kernel(tc, tab_words, tab_scales, offs, gT, w1, 
         reorder(w3_codes[:], w3_raw[:], "a m t")
         reorder(w2_codes[:].bitcast(U16), w2_raw[:].bitcast(U16), "a t m")
 
-        w1_bf = held([P, PASSES * PACK * H], BF16, "w1_bf")
-        for a in range(PASSES):
+        w1_bf = shared([P, PASSES * PACK * H], BF16, "w1_bf", "w1_slot")
+        for a, copy, ts in ((0, nc.scalar.copy, slice(0, PACK)), (1, nc.scalar.copy, slice(0, PACK // 2)),
+                            (1, nc.vector.tensor_copy, slice(PACK // 2, PACK))):
             dst = w1_bf[:, a * PACK * H : (a + 1) * PACK * H]
-            nc.scalar.copy(dst.rearrange("p (t m j) -> p m j t", t=PACK, j=PACK),
-                           w1_raw[a][:].rearrange("p j (m t) -> p m j t", t=PACK))
+            copy(dst.rearrange("p (t m j) -> p m j t", t=PACK, j=PACK)[:, :, :, ts],
+                 w1_raw[a][:].rearrange("p j (m t) -> p m j t", t=PACK)[:, :, :, ts])
         w1_codes = shared([P, PASSES * H], U32, "w1_codes", "w3_slot")
         w1_sc = held([P, PASSES * H], U8, "w1_sc")
         nc.vector.quantize_mx(out=w1_codes[:].bitcast(FP8X4), scales=w1_sc[:], in_=w1_bf[:])
@@ -156,18 +158,26 @@ def tile_list_fader_balance_mix_kernel(tc, tab_words, tab_scales, offs, gT, w1, 
                 nc.tensor.matmul_mx(out=dst, lhsT=codes, lhsT_scale=scales, rhs=v_w[a][:, entries].bitcast(FP8X4),
                                     rhs_scale=planes[a][:, entries], start=(a == 0), stop=(a == PASSES - 1))
 
-        h_codes = {name: held([P, S], U32, f"{name}_codes") for name in ("h1", "h2", "h3")}
-        h_sc = {name: held([P, S], U8, f"{name}_sc") for name in ("h1", "h2", "h3")}
+        o_bf = shared([P, 2, N * PACK], BF16, "o_bf", "w1_slot")
+        for i, raw in enumerate((o1_raw, o3_raw)):
+            nc.gpsimd.tensor_scalar(o_bf[:, i, :].rearrange("p (c j) -> p c j", j=PACK),
+                                    raw[:].rearrange("p j c -> p c j"), 1.0, 0.0, ALU.mult, ALU.add)
+        late_codes = shared([P, 2 * N + 3 * S], U32, "late_codes", "o3_slot")
+        o_sc = held([P, 2 * N], U8, "o_sc")
+        nc.vector.quantize_mx(out=late_codes[:, 0 : 2 * N].bitcast(FP8X4), scales=o_sc[:],
+                              in_=o_bf[:].rearrange("p i c -> p (i c)"))
+        o_sides = ((late_codes[:, 0:N], o_sc[:, 0:N]), (o2_codes, o2_sc),
+                   (late_codes[:, N : 2 * N], o_sc[:, N : 2 * N]))
+        h_codes = {name: late_codes[:, 2 * N + b * S : 2 * N + (b + 1) * S] for b, name in enumerate(BRANCHES)}
+        h_sc = {name: held([P, S], U8, f"{name}_sc") for name in BRANCHES}
 
-        def quantize_h(name, c, h_bf):
-            entries = slice(c * CH, (c + 1) * CH)
-            nc.vector.quantize_mx(out=h_codes[name][:, entries].bitcast(FP8X4), scales=h_sc[name][:, entries],
-                                  in_=h_bf[:])
+        def chunk(c):
+            return slice(c * CH, (c + 1) * CH)
 
         def gated_branch(name, c, side, planes, width, func, gain):
             act = work.tile([P, PACK, CH], F32, name="act")
             for pair in range(PACK // 2):
-                bank = psum.tile([P, 2, CH], F32, name="x_bank", bufs=4)
+                bank = psum.tile([P, 2, CH], F32, name="x_bank", bufs=3)
                 for e in range(2):
                     for s in range(0, CH, width):
                         first_product(bank[:, e, s : s + width], side, planes, 2 * pair + e,
@@ -177,36 +187,25 @@ def tile_list_fader_balance_mix_kernel(tc, tab_words, tab_scales, offs, gT, w1, 
             for t in range(PACK):
                 nc.scalar.activation(slices[:, t, :], act[:, t, :], ACT.Copy, scale=gain[:, t : t + 1])
             h_bf = work.tile([P, CH * PACK], BF16, name="h_bf", align_bytes=64, bufs=4)
-            nc.scalar.copy(h_bf[:].rearrange("p (c i t) -> p c t i", i=4, t=PACK),
-                           slices[:].rearrange("p t (c i) -> p c t i", i=4))
-            quantize_h(name, c, h_bf)
+            nc.scalar.copy(h_bf[:].rearrange("p (c i t) -> p c t i", i=RUN, t=PACK),
+                           slices[:].rearrange("p t (c i) -> p c t i", i=RUN))
+            nc.vector.quantize_mx(out=h_codes[name][:, chunk(c)].bitcast(FP8X4), scales=h_sc[name][:, chunk(c)],
+                                  in_=h_bf[:])
 
         def gated(c):
             gated_branch("h2", c, w2_side, planes_e2m1, P, ACT.Sigmoid, gain2_t)
             gated_branch("h1", c, w1_side, planes_e4m3, CH, ACT.Tanh, gain1_t)
 
+        h3_bf = held([P, S * PACK], BF16, "h3_bf")
+
         def affine(c):
-            h_bf = held([P, CH * PACK], BF16, f"h3_bf{c}")
-            for s in range(0, CH, P):
-                bank = psum.tile([P, PACK, P], F32, name="x3_bank", bufs=3)
+            for s in range(c * CH, (c + 1) * CH, P):
+                bank = psum.tile([P, PACK, P], F32, name="x3_bank", bufs=4)
                 for t in range(PACK):
-                    first_product(bank[:, t, :], w3_side, planes_e4m3, t, slice(c * CH + s, c * CH + s + P))
-                nc.vector.tensor_tensor(h_bf[:, s * PACK : (s + P) * PACK].rearrange("p (n t) -> p n t", t=PACK),
+                    first_product(bank[:, t, :], w3_side, planes_e4m3, t, slice(s, s + P))
+                nc.vector.tensor_tensor(h3_bf[:, s * PACK : (s + P) * PACK].rearrange("p (n t) -> p n t", t=PACK),
                                         bank[:].rearrange("p t n -> p n t"),
                                         b3_t[:].unsqueeze(1).to_broadcast([P, P, PACK]), ALU.add)
-            quantize_h("h3", c, h_bf)
-
-        def quantize_o(name, raw, on_scalar):
-            o_bf = held([P, N, PACK], BF16, f"{name}_bf")
-            for copy, cols in ((nc.scalar.copy, slice(0, on_scalar)), (nc.vector.tensor_copy, slice(on_scalar, N))):
-                if cols.start < cols.stop:
-                    copy(o_bf[:, cols, :].rearrange("p (c i) j -> p c j i", i=4),
-                         raw[:, :, cols].rearrange("p j (c i) -> p c j i", i=4))
-            codes = held([P, N], U32, f"{name}_codes")
-            scales = held([P, N], U8, f"{name}_sc")
-            nc.vector.quantize_mx(out=codes[:].bitcast(FP8X4), scales=scales[:],
-                                  in_=o_bf[:].rearrange("p c j -> p (c j)"))
-            return codes, scales
 
         picked = [held([P, S], F32, f"picked{n}") for n in range(NT)]
 
@@ -216,7 +215,7 @@ def tile_list_fader_balance_mix_kernel(tc, tab_words, tab_scales, offs, gT, w1, 
             bank = psum.tile([P, len(tiles), width], F32, name="y_bank")
             for e, n in enumerate(tiles):
                 cols = slice(n * P, (n + 1) * P)
-                for b, name in enumerate(("h1", "h2", "h3")):
+                for b, name in enumerate(BRANCHES):
                     nc.tensor.matmul_mx(out=bank[:, e, :], lhsT=o_sides[b][0][:, cols].bitcast(FP8X4),
                                         lhsT_scale=o_sides[b][1][:, cols],
                                         rhs=h_codes[name][:, entries].bitcast(FP8X4),
@@ -230,15 +229,10 @@ def tile_list_fader_balance_mix_kernel(tc, tab_words, tab_scales, offs, gT, w1, 
                 if entries.stop == S:
                     nc.sync.dma_start(out=out[n * P : (n + 1) * P, :], in_=state[n][:])
 
-        def chunk(c):
-            return slice(c * CH, (c + 1) * CH)
-
         gated(0)
-        affine(0)
-        affine(1)
-        o_sides = (quantize_o("o1", o1_raw, N), (o2_codes, o2_sc), quantize_o("o3", o3_raw, O3_ON_SCALAR))
-        affine(2)
-        affine(3)
+        for c in range(CHUNKS):
+            affine(c)
+        nc.vector.quantize_mx(out=h_codes["h3"].bitcast(FP8X4), scales=h_sc["h3"][:], in_=h3_bf[:])
 
         upper, lower = (0, 1), (2, 3)
         for c in range(CHUNKS - 1):

@@ -102,8 +102,8 @@ def tile_list_fader_balance_mix_kernel(tc, tab_words, tab_scales, offs, gT, w1, 
 
         nc.sync.dma_start(out=w3_raw[:].rearrange("p (a c) -> p a c", a=PASSES),
                           in_=w3_words.rearrange("a p c i -> p a (c i)").bitcast(I32))
-        load_rows(o1_raw, o1)
         load_state(0)
+        load_rows(o1_raw, o1)
         load_rows(o3_raw, o3)
         nc.sync.dma_start(out=o2_codes[:], in_=o2_words[0].rearrange("p c i -> p (c i)").bitcast(I32))
         for q in range(QUADS):
@@ -128,11 +128,10 @@ def tile_list_fader_balance_mix_kernel(tc, tab_words, tab_scales, offs, gT, w1, 
         reorder(w2_codes[:].bitcast(U16), w2_raw[:].bitcast(U16), "a t m")
 
         w1_bf = shared([P, PASSES * PACK * H], BF16, "w1_bf", "w1_slot")
-        for a, copy, ts in ((0, nc.scalar.copy, slice(0, PACK)), (1, nc.scalar.copy, slice(0, PACK // 2)),
-                            (1, nc.vector.tensor_copy, slice(PACK // 2, PACK))):
+        for a in range(PASSES):
             dst = w1_bf[:, a * PACK * H : (a + 1) * PACK * H]
-            copy(dst.rearrange("p (t m j) -> p m j t", t=PACK, j=PACK)[:, :, :, ts],
-                 w1_raw[a][:].rearrange("p j (m t) -> p m j t", t=PACK)[:, :, :, ts])
+            nc.scalar.copy(dst.rearrange("p (t m j) -> p m j t", t=PACK, j=PACK),
+                           w1_raw[a][:].rearrange("p j (m t) -> p m j t", t=PACK))
         w1_codes = shared([P, PASSES * H], U32, "w1_codes", "w3_slot")
         w1_sc = held([P, PASSES * H], U8, "w1_sc")
         nc.vector.quantize_mx(out=w1_codes[:].bitcast(FP8X4), scales=w1_sc[:], in_=w1_bf[:])
@@ -168,13 +167,21 @@ def tile_list_fader_balance_mix_kernel(tc, tab_words, tab_scales, offs, gT, w1, 
                               in_=o_bf[:].rearrange("p i c -> p (i c)"))
         o_sides = ((late_codes[:, 0:N], o_sc[:, 0:N]), (o2_codes, o2_sc),
                    (late_codes[:, N : 2 * N], o_sc[:, N : 2 * N]))
-        h_codes = {name: late_codes[:, 2 * N + b * S : 2 * N + (b + 1) * S] for b, name in enumerate(BRANCHES)}
-        h_sc = {name: held([P, S], U8, f"{name}_sc") for name in BRANCHES}
+        h3_codes = late_codes[:, 2 * N : 2 * N + S]
+        h21_codes = late_codes[:, 2 * N + S : 2 * N + 3 * S]
+        h3_sc = held([P, S], U8, "h3_sc")
+        h21_sc = held([P, 2 * S], U8, "h21_sc")
+
+        def h_side(name, c):
+            if name == "h3":
+                return h3_codes[:, chunk(c)], h3_sc[:, chunk(c)]
+            cols = chunk(2 * c + (name == "h1"))
+            return h21_codes[:, cols], h21_sc[:, cols]
 
         def chunk(c):
             return slice(c * CH, (c + 1) * CH)
 
-        def gated_branch(name, c, side, planes, width, func, gain):
+        def gated_branch(name, c, side, planes, width, func, gain, dst):
             act = work.tile([P, PACK, CH], F32, name="act")
             for pair in range(PACK // 2):
                 bank = psum.tile([P, 2, CH], F32, name="x_bank", bufs=3)
@@ -186,15 +193,16 @@ def tile_list_fader_balance_mix_kernel(tc, tab_words, tab_scales, offs, gT, w1, 
             slices = shared([P, PACK, CH], BF16, "slices", f"{name}_slot{c}")
             for t in range(PACK):
                 nc.scalar.activation(slices[:, t, :], act[:, t, :], ACT.Copy, scale=gain[:, t : t + 1])
-            h_bf = work.tile([P, CH * PACK], BF16, name="h_bf", align_bytes=64, bufs=4)
-            nc.scalar.copy(h_bf[:].rearrange("p (c i t) -> p c t i", i=RUN, t=PACK),
+            nc.scalar.copy(dst.rearrange("p (c i t) -> p c t i", i=RUN, t=PACK),
                            slices[:].rearrange("p t (c i) -> p c t i", i=RUN))
-            nc.vector.quantize_mx(out=h_codes[name][:, chunk(c)].bitcast(FP8X4), scales=h_sc[name][:, chunk(c)],
-                                  in_=h_bf[:])
 
         def gated(c):
-            gated_branch("h2", c, w2_side, planes_e2m1, P, ACT.Sigmoid, gain2_t)
-            gated_branch("h1", c, w1_side, planes_e4m3, CH, ACT.Tanh, gain1_t)
+            h_bf = work.tile([P, 2, CH * PACK], BF16, name="h_bf", align_bytes=64)
+            gated_branch("h2", c, w2_side, planes_e2m1, P, ACT.Sigmoid, gain2_t, h_bf[:, 0, :])
+            gated_branch("h1", c, w1_side, planes_e4m3, CH, ACT.Tanh, gain1_t, h_bf[:, 1, :])
+            cols = slice(2 * c * CH, 2 * (c + 1) * CH)
+            nc.vector.quantize_mx(out=h21_codes[:, cols].bitcast(FP8X4), scales=h21_sc[:, cols],
+                                  in_=h_bf[:].rearrange("p b c -> p (b c)"))
 
         h3_bf = held([P, S * PACK], BF16, "h3_bf")
 
@@ -215,11 +223,14 @@ def tile_list_fader_balance_mix_kernel(tc, tab_words, tab_scales, offs, gT, w1, 
             bank = psum.tile([P, len(tiles), width], F32, name="y_bank")
             for e, n in enumerate(tiles):
                 cols = slice(n * P, (n + 1) * P)
-                for b, name in enumerate(BRANCHES):
-                    nc.tensor.matmul_mx(out=bank[:, e, :], lhsT=o_sides[b][0][:, cols].bitcast(FP8X4),
-                                        lhsT_scale=o_sides[b][1][:, cols],
-                                        rhs=h_codes[name][:, entries].bitcast(FP8X4),
-                                        rhs_scale=h_sc[name][:, entries], start=(b == 0), stop=(b == 2))
+                for c in range(entries.start // CH, entries.stop // CH):
+                    first = c * CH - entries.start
+                    for b, name in enumerate(BRANCHES):
+                        codes, scales = h_side(name, c)
+                        nc.tensor.matmul_mx(out=bank[:, e, first : first + CH],
+                                            lhsT=o_sides[b][0][:, cols].bitcast(FP8X4),
+                                            lhsT_scale=o_sides[b][1][:, cols], rhs=codes.bitcast(FP8X4),
+                                            rhs_scale=scales, start=(b == 0), stop=(b == 2))
             nc.scalar.copy(y[:], bank[:])
             for e, n in enumerate(tiles):
                 if entries.start == 0:
@@ -232,7 +243,7 @@ def tile_list_fader_balance_mix_kernel(tc, tab_words, tab_scales, offs, gT, w1, 
         gated(0)
         for c in range(CHUNKS):
             affine(c)
-        nc.vector.quantize_mx(out=h_codes["h3"].bitcast(FP8X4), scales=h_sc["h3"][:], in_=h3_bf[:])
+        nc.vector.quantize_mx(out=h3_codes.bitcast(FP8X4), scales=h3_sc[:], in_=h3_bf[:])
 
         upper, lower = (0, 1), (2, 3)
         for c in range(CHUNKS - 1):

@@ -67,11 +67,10 @@ def tile_list_fader_balance_mix_kernel(tc, tab_words, tab_scales, offs, gT, w1, 
         o2_codes = held([P, N], I32, "o2_codes")
         state = [held([P, T], F32, f"state{n}") for n in range(NT)]
 
-        def load_w_scales(queue, scales, first, quads):
-            for q in quads:
-                rows = slice(32 * q + first, 32 * q + first + 4)
-                queue.dma_start(out=w_sc_raw[rows, :].bitcast(I32).rearrange("r (a c) -> r a c", a=PASSES),
-                                in_=scales[:, 4 * q : 4 * q + 4, :].bitcast(I32).rearrange("a r c -> r a c"))
+        def load_w_scales(queue, scales, first, rows):
+            for r in rows:
+                queue.dma_start(out=w_sc_raw[first + r : P : 32, :].bitcast(I32).rearrange("q (a c) -> q a c", a=PASSES),
+                                in_=scales.bitcast(I32).rearrange("a (q r) c -> r q a c", r=4)[r])
 
         def load_rows(tile, rows):
             nc.sync.dma_start(out=tile[:], in_=rows.rearrange("(p j) c -> p j c", j=PACK))
@@ -82,9 +81,9 @@ def tile_list_fader_balance_mix_kernel(tc, tab_words, tab_scales, offs, gT, w1, 
         for tile, vec in ((b3_t, b3), (gain2_t, gain2), (gain1_t, gain1)):
             nc.gpsimd.dma_start(out=tile[:], in_=vec.rearrange("(p t) -> p t", t=PACK))
         load_w_scales(nc.scalar, w2_scales, 0, range(QUADS // 2))
-        for q in range(QUADS):
-            nc.sync.dma_start(out=tab_sc[32 * q : 32 * q + PASSES * LOW, :].bitcast(I32),
-                              in_=tab_scales[:, 4 * q : 4 * q + 4, :].bitcast(I32))
+        for r in range(4):
+            nc.sync.dma_start(out=tab_sc[r:P:16, :].bitcast(I32),
+                              in_=tab_scales.bitcast(I32).rearrange("a (q r) t -> r q a t", r=4)[r])
         for a in range(PASSES):
             nc.sync.dma_start(out=tab_w[a][:], in_=tab_words[a].rearrange("p t i -> p (t i)").bitcast(I32))
         load_w_scales(nc.sync, w2_scales, 0, range(QUADS // 2, QUADS))
@@ -96,9 +95,8 @@ def tile_list_fader_balance_mix_kernel(tc, tab_words, tab_scales, offs, gT, w1, 
 
         v_sc = held([P, S], U8, "v_sc")
         nc.vector.tensor_copy(v_sc[:], tab_sc[:].indirect(offsets[:]))
-        for q in range(QUADS):
-            nc.sync.dma_start(out=v_sc_raised[32 * q : 32 * q + 4, :].bitcast(I32),
-                              in_=v_sc[32 * q + LOW : 32 * q + LOW + 4, :].bitcast(I32))
+        for r in range(4):
+            nc.sync.dma_start(out=v_sc_raised[r:P:32, :].bitcast(I32), in_=v_sc[16 + r : P : 32, :].bitcast(I32))
 
         nc.sync.dma_start(out=w3_raw[:].rearrange("p (a c) -> p a c", a=PASSES),
                           in_=w3_words.rearrange("a p c i -> p a (c i)").bitcast(I32))
@@ -106,9 +104,9 @@ def tile_list_fader_balance_mix_kernel(tc, tab_words, tab_scales, offs, gT, w1, 
         load_rows(o1_raw, o1)
         load_rows(o3_raw, o3)
         nc.sync.dma_start(out=o2_codes[:], in_=o2_words[0].rearrange("p c i -> p (c i)").bitcast(I32))
-        for q in range(QUADS):
-            nc.gpsimd.dma_start(out=o2_sc[32 * q : 32 * q + 4, :].bitcast(I32),
-                                in_=o2_scales[0, 4 * q : 4 * q + 4, :].bitcast(I32))
+        for r in range(4):
+            nc.gpsimd.dma_start(out=o2_sc[r:P:32, :].bitcast(I32),
+                                in_=o2_scales[0].bitcast(I32).rearrange("(q r) c -> r q c", r=4)[r])
         for n in range(1, NT):
             load_state(n)
 
@@ -148,8 +146,7 @@ def tile_list_fader_balance_mix_kernel(tc, tab_words, tab_scales, offs, gT, w1, 
             first = a * H + t * P
             return w3_codes[:, first : first + P].bitcast(FP8X4), w_sc[LOW:P, first : first + P]
 
-        planes_e4m3 = (v_sc[:], v_sc[LOW:P, :])
-        planes_e2m1 = (v_sc[:], v_sc_raised[:])
+        planes_e4m3 = planes_e2m1 = (v_sc[:], v_sc_raised[:])
 
         def first_product(dst, side, planes, t, entries):
             for a in range(PASSES):

@@ -62,7 +62,7 @@ def tile_list_fader_balance_mix_kernel(tc, tab_words, tab_scales, offs, gT, w1, 
         w3_raw = shared([P, PASSES * H], I32, "w3_raw", "w3_slot")
         w2_raw = held([P, PASSES * 2 * H], U8, "w2_raw")
         w1_raw = [held([P, PACK, H], F32, f"w1_raw{a}") for a in range(PASSES)]
-        o1_raw = held([P, PACK, N], F32, "o1_raw")
+        o1_raw = shared([P, PACK, N], F32, "o1_raw", "o1_slot")
         o3_raw = shared([P, PACK, N], F32, "o3_raw", "o3_slot")
         o2_codes = held([P, N], I32, "o2_codes")
         state = [held([P, T], F32, f"state{n}") for n in range(NT)]
@@ -102,13 +102,17 @@ def tile_list_fader_balance_mix_kernel(tc, tab_words, tab_scales, offs, gT, w1, 
                           in_=w3_words.rearrange("a p c i -> p a (c i)").bitcast(I32))
         load_state(0)
         load_rows(o1_raw, o1)
+        load_state(1)
         load_rows(o3_raw, o3)
         nc.sync.dma_start(out=o2_codes[:], in_=o2_words[0].rearrange("p c i -> p (c i)").bitcast(I32))
         for r in range(4):
             nc.gpsimd.dma_start(out=o2_sc[r:P:32, :].bitcast(I32),
                                 in_=o2_scales[0].bitcast(I32).rearrange("(q r) c -> r q c", r=4)[r])
-        for n in range(1, NT):
+        for n in range(2, NT):
             load_state(n)
+
+        warm = held([P, 1], F32, "warm")
+        nc.scalar.activation(warm[:], b3_t[:, 0:1], ACT.Sigmoid)
 
         v_w = [held([P, S], U32, f"v_w{a}") for a in range(PASSES)]
         for a in range(PASSES):
@@ -158,14 +162,12 @@ def tile_list_fader_balance_mix_kernel(tc, tab_words, tab_scales, offs, gT, w1, 
         for i, raw in enumerate((o1_raw, o3_raw)):
             nc.gpsimd.tensor_scalar(o_bf[:, i, :].rearrange("p (c j) -> p c j", j=PACK),
                                     raw[:].rearrange("p j c -> p c j"), 1.0, 0.0, ALU.mult, ALU.add)
-        late_codes = shared([P, 2 * N + 3 * S], U32, "late_codes", "o3_slot")
+        late_codes = shared([P, 2 * N + 2 * S], U32, "late_codes", "o3_slot")
         o_sc = held([P, 2 * N], U8, "o_sc")
-        nc.vector.quantize_mx(out=late_codes[:, 0 : 2 * N].bitcast(FP8X4), scales=o_sc[:],
-                              in_=o_bf[:].rearrange("p i c -> p (i c)"))
         o_sides = ((late_codes[:, 0:N], o_sc[:, 0:N]), (o2_codes, o2_sc),
                    (late_codes[:, N : 2 * N], o_sc[:, N : 2 * N]))
-        h3_codes = late_codes[:, 2 * N : 2 * N + S]
-        h21_codes = late_codes[:, 2 * N + S : 2 * N + 3 * S]
+        h3_codes = shared([P, S], U32, "h3_codes", "o1_slot")[:]
+        h21_codes = late_codes[:, 2 * N : 2 * N + 2 * S]
         h3_sc = held([P, S], U8, "h3_sc")
         h21_sc = held([P, 2 * S], U8, "h21_sc")
 
@@ -190,11 +192,18 @@ def tile_list_fader_balance_mix_kernel(tc, tab_words, tab_scales, offs, gT, w1, 
             slices = shared([P, PACK, CH], BF16, "slices", f"{name}_slot{c}")
             for t in range(PACK):
                 nc.scalar.activation(slices[:, t, :], act[:, t, :], ACT.Copy, scale=gain[:, t : t + 1])
-            nc.scalar.copy(dst.rearrange("p (c i t) -> p c t i", i=RUN, t=PACK),
-                           slices[:].rearrange("p t (c i) -> p c t i", i=RUN))
+            if c == 1:
+                nc.gpsimd.tensor_scalar(dst.rearrange("p (c t) -> p c t", t=PACK),
+                                        slices[:].rearrange("p t c -> p c t"), 1.0, 0.0, ALU.mult, ALU.add)
+            else:
+                nc.scalar.copy(dst.rearrange("p (c i t) -> p c t i", i=RUN, t=PACK),
+                               slices[:].rearrange("p t (c i) -> p c t i", i=RUN))
 
         def gated(c):
-            h_bf = work.tile([P, 2, CH * PACK], BF16, name="h_bf", align_bytes=64)
+            if c == 1:
+                h_bf = shared([P, 2, CH * PACK], BF16, "h_bf", "w1_slot")
+            else:
+                h_bf = work.tile([P, 2, CH * PACK], BF16, name="h_bf", align_bytes=64)
             gated_branch("h2", c, w2_side, planes_e2m1, P, ACT.Sigmoid, gain2_t, h_bf[:, 0, :])
             gated_branch("h1", c, w1_side, planes_e4m3, CH, ACT.Tanh, gain1_t, h_bf[:, 1, :])
             cols = slice(2 * c * CH, 2 * (c + 1) * CH)
@@ -212,7 +221,22 @@ def tile_list_fader_balance_mix_kernel(tc, tab_words, tab_scales, offs, gT, w1, 
                                         bank[:].rearrange("p t n -> p n t"),
                                         b3_t[:].unsqueeze(1).to_broadcast([P, P, PACK]), ALU.add)
 
-        picked = [held([P, S], F32, f"picked{n}") for n in range(NT)]
+        def quantize_h3(entries, values):
+            nc.vector.quantize_mx(out=h3_codes[:, entries].bitcast(FP8X4), scales=h3_sc[:, entries], in_=values)
+
+        def affine_on_scalar(c):
+            slices = held([P, PACK, CH], BF16, "h3_slices")
+            for pair in range(PACK // 2):
+                bank = psum.tile([P, 2, CH], F32, name="x_bank", bufs=3)
+                for e in range(2):
+                    first_product(bank[:, e, :], w3_side, planes_e4m3, 2 * pair + e, chunk(c))
+                for e in range(2):
+                    t = 2 * pair + e
+                    nc.scalar.activation(slices[:, t, :], bank[:, e, :], ACT.Identity, bias=b3_t[:, t : t + 1])
+            woven = held([P, CH * PACK], BF16, "h3_last")
+            nc.scalar.copy(woven[:].rearrange("p (c i t) -> p c t i", i=RUN, t=PACK),
+                           slices[:].rearrange("p t (c i) -> p c t i", i=RUN))
+            quantize_h3(chunk(c), woven[:])
 
         def second_stage(tiles, entries, slot):
             width = entries.stop - entries.start
@@ -230,20 +254,31 @@ def tile_list_fader_balance_mix_kernel(tc, tab_words, tab_scales, offs, gT, w1, 
                                             rhs_scale=scales, start=(b == 0), stop=(b == 2))
             nc.scalar.copy(y[:], bank[:])
             for e, n in enumerate(tiles):
-                if entries.start == 0:
-                    nc.vector.tensor_copy(picked[n][:], state[n][:].indirect(offsets[:]))
                 nc.vector.tensor_tensor(state[n][:].indirect(listed(entries)), y[:, e, :], picked[n][:, entries],
                                         ALU.mult)
                 if entries.stop == S:
                     nc.sync.dma_start(out=out[n * P : (n + 1) * P, :], in_=state[n][:])
 
+        picked = [held([P, S], F32, f"picked{n}") for n in range(NT)]
+
+        def pick(n):
+            nc.vector.tensor_copy(picked[n][:], state[n][:].indirect(offsets[:]))
+
+        pick(0)
+        nc.vector.quantize_mx(out=late_codes[:, 0 : 2 * N].bitcast(FP8X4), scales=o_sc[:],
+                              in_=o_bf[:].rearrange("p i c -> p (i c)"))
         gated(0)
-        for c in range(CHUNKS):
+        for c in range(CHUNKS - 1):
             affine(c)
-        nc.vector.quantize_mx(out=h3_codes.bitcast(FP8X4), scales=h3_sc[:], in_=h3_bf[:])
+        quantize_h3(slice(0, 2 * CH), h3_bf[:, 0 : 2 * CH * PACK])
+        quantize_h3(chunk(2), h3_bf[:, 2 * CH * PACK : 3 * CH * PACK])
+        for n in range(1, NT):
+            pick(n)
 
         upper, lower = (0, 1), (2, 3)
         for c in range(CHUNKS - 1):
+            if c == 1:
+                affine_on_scalar(CHUNKS - 1)
             gated(c + 1)
             second_stage(upper, chunk(c), f"h1_slot{c + 1}")
             if c < CHUNKS - 2:

@@ -19,23 +19,23 @@ ACT = mybir.ActivationFunctionType
 P = 128
 PACK = 4
 PASSES = K // (P * PACK)
-QUADS = 4
-LOW = 4
+ROWS = 4
 GROUP = 16
 CH = 256
 CHUNKS = S // CH
-NT = N // P
-BRANCHES = ("h1", "h2", "h3")
+PAIR = 2
+HALVES = N // (P * PAIR)
 RUN = 4
+W1_SPLIT = 88
+RING = 4
 
 
 def tile_list_fader_balance_mix_kernel(tc, tab_words, tab_scales, offs, gT, w1, w2_words, w2_scales,
-                                                 w3_words, w3_scales, gain1, gain2, b3, o1, o2_words, o2_scales,
-                                                 o3, out):
+                                                     w3_words, w3_scales, gain1, gain2, b3, o1, o2_words, o2_scales,
+                                                     o3, out):
     nc = tc.nc
     with ExitStack() as ctx:
         keep = ctx.enter_context(tc.tile_pool(name="keep", bufs=1))
-        work = ctx.enter_context(tc.tile_pool(name="work", bufs=2))
         psum = ctx.enter_context(tc.psum_pool(name="psum", bufs=1))
 
         def held(shape, dtype, name):
@@ -44,245 +44,346 @@ def tile_list_fader_balance_mix_kernel(tc, tab_words, tab_scales, offs, gT, w1, 
         def shared(shape, dtype, name, slot):
             return keep.tile(shape, dtype, name=name, tag=slot, align_bytes=64)
 
+        turns = []
+
+        def ring_bank(shape):
+            turns.append(shape)
+            return psum.tile(shape, F32, name="ring", tag=f"ring{len(turns) % RING}")
+
         def listed(entries):
             return offsets[:, entries.start // GROUP : entries.stop // GROUP]
+
+        def chunk(c):
+            return slice(c * CH, (c + 1) * CH)
 
         offsets = keep.tile([P, S // GROUP], U16, name="offsets")
         nc.sync.dma_start(offsets[:], offs)
 
         tab_sc = held([P, T], U8, "tab_sc")
-        w_sc_raw = held([P, PASSES * H], U8, "w_sc_raw")
+        w2_sc_raw = shared([P, PASSES * H], U8, "w2_sc_raw", "w2_sc_slot")
+        w3_sc_raw = held([P, PASSES * H], U8, "w3_sc_raw")
         v_sc_raised = held([P, S], U8, "v_sc_raised")
         o2_sc = held([P, N], U8, "o2_sc")
-        for plane in (tab_sc, w_sc_raw, v_sc_raised, o2_sc):
+        for plane in (tab_sc, w3_sc_raw, w2_sc_raw, v_sc_raised, o2_sc):
             nc.vector.memset(plane[:].bitcast(I32), 0)
 
         b3_t, gain2_t, gain1_t = (held([P, PACK], F32, name) for name in ("b3_t", "gain2_t", "gain1_t"))
-        tab_w = [held([P, T], I32, f"tab_w{a}") for a in range(PASSES)]
-        w3_raw = shared([P, PASSES * H], I32, "w3_raw", "w3_slot")
+        tab_w = [shared([P, T], I32, "tab_w", f"tab_slot{a}") for a in range(PASSES)]
+        w3_raw = held([P, PASSES * H], I32, "w3_raw")
         w2_raw = held([P, PASSES * 2 * H], U8, "w2_raw")
         w1_raw = [held([P, PACK, H], F32, f"w1_raw{a}") for a in range(PASSES)]
-        o1_raw = shared([P, PACK, N], F32, "o1_raw", "o1_slot")
-        o3_raw = shared([P, PACK, N], F32, "o3_raw", "o3_slot")
-        o2_codes = held([P, N], I32, "o2_codes")
-        state = [held([P, T], F32, f"state{n}") for n in range(NT)]
+        o_raw = [held([P, 2, PACK, P * PAIR], F32, f"o_raw{half}") for half in range(HALVES)]
+        o2_codes = [held([P, P * PAIR], I32, f"o2_codes{half}") for half in range(HALVES)]
+        state = [held([P, T], F32, f"state{n}") for n in range(HALVES * PAIR)]
 
-        def load_w_scales(queue, scales, first, rows):
-            for r in rows:
-                queue.dma_start(out=w_sc_raw[first + r : P : 32, :].bitcast(I32).rearrange("q (a c) -> q a c", a=PASSES),
-                                in_=scales.bitcast(I32).rearrange("a (q r) c -> r q a c", r=4)[r])
+        def load_w_scales(queue, plane, scales):
+            for r in range(ROWS):
+                queue.dma_start(out=plane[r:P:32, :].bitcast(I32).rearrange("q (a c) -> q a c", a=PASSES),
+                                in_=scales.bitcast(I32).rearrange("a (q r) c -> r q a c", r=ROWS)[r])
 
         def load_rows(tile, rows):
-            nc.sync.dma_start(out=tile[:], in_=rows.rearrange("(p j) c -> p j c", j=PACK))
+            nc.sync.dma_start(out=tile, in_=rows.rearrange("(p j) c -> p j c", j=PACK))
 
         def load_state(n):
             nc.sync.dma_start(out=state[n][:], in_=gT[n * P : (n + 1) * P, :])
 
-        for tile, vec in ((b3_t, b3), (gain2_t, gain2), (gain1_t, gain1)):
-            nc.gpsimd.dma_start(out=tile[:], in_=vec.rearrange("(p t) -> p t", t=PACK))
-        load_w_scales(nc.scalar, w2_scales, 0, range(QUADS // 2))
-        for r in range(4):
+        def load_o(half):
+            for i, rows in enumerate((o1, o3)):
+                load_rows(o_raw[half][:, i], rows[:, half * P * PAIR : (half + 1) * P * PAIR])
+            nc.sync.dma_start(out=o2_codes[half][:], in_=o2_words[0].rearrange("p c i -> p (c i)").bitcast(I32)[
+                :, half * P * PAIR : (half + 1) * P * PAIR])
+
+        def load_vector(queue, tile, vec):
+            queue.dma_start(out=tile[:], in_=vec.rearrange("(p t) -> p t", t=PACK))
+
+        load_vector(nc.sync, b3_t, b3)
+        load_vector(nc.sync, gain2_t, gain2)
+        for r in range(ROWS):
             nc.sync.dma_start(out=tab_sc[r:P:16, :].bitcast(I32),
-                              in_=tab_scales.bitcast(I32).rearrange("a (q r) t -> r q a t", r=4)[r])
+                              in_=tab_scales.bitcast(I32).rearrange("a (q r) t -> r q a t", r=ROWS)[r])
+        load_w_scales(nc.gpsimd, w3_sc_raw, w3_scales)
+        load_vector(nc.gpsimd, gain1_t, gain1)
+        for r in range(ROWS):
+            nc.gpsimd.dma_start(out=o2_sc[r:P:32, :].bitcast(I32),
+                                in_=o2_scales[0].bitcast(I32).rearrange("(q r) c -> r q c", r=ROWS)[r])
         for a in range(PASSES):
             nc.sync.dma_start(out=tab_w[a][:], in_=tab_words[a].rearrange("p t i -> p (t i)").bitcast(I32))
-        load_w_scales(nc.sync, w2_scales, 0, range(QUADS // 2, QUADS))
-        load_w_scales(nc.sync, w3_scales, LOW, range(QUADS))
-        for a in range(PASSES):
-            load_rows(w1_raw[a], w1[a * P * PACK : (a + 1) * P * PACK, :])
         nc.sync.dma_start(out=w2_raw[:].bitcast(I32).rearrange("p (a c) -> p a c", a=PASSES),
                           in_=w2_words.bitcast(I32).rearrange("a p c -> p a c"))
+        load_w_scales(nc.sync, w2_sc_raw, w2_scales)
+        nc.sync.dma_start(out=w3_raw[:].rearrange("p (a c) -> p a c", a=PASSES),
+                          in_=w3_words.rearrange("a p c i -> p a (c i)").bitcast(I32))
 
         v_sc = held([P, S], U8, "v_sc")
         nc.vector.tensor_copy(v_sc[:], tab_sc[:].indirect(offsets[:]))
-        for r in range(4):
+        for r in range(ROWS):
             nc.sync.dma_start(out=v_sc_raised[r:P:32, :].bitcast(I32), in_=v_sc[16 + r : P : 32, :].bitcast(I32))
 
-        nc.sync.dma_start(out=w3_raw[:].rearrange("p (a c) -> p a c", a=PASSES),
-                          in_=w3_words.rearrange("a p c i -> p a (c i)").bitcast(I32))
+        for a in range(PASSES):
+            load_rows(w1_raw[a][:], w1[a * P * PACK : (a + 1) * P * PACK, :])
+        load_state(2)
+        load_state(3)
+        load_o(0)
         load_state(0)
-        load_rows(o1_raw, o1)
         load_state(1)
-        load_rows(o3_raw, o3)
-        nc.sync.dma_start(out=o2_codes[:], in_=o2_words[0].rearrange("p c i -> p (c i)").bitcast(I32))
-        for r in range(4):
-            nc.gpsimd.dma_start(out=o2_sc[r:P:32, :].bitcast(I32),
-                                in_=o2_scales[0].bitcast(I32).rearrange("(q r) c -> r q c", r=4)[r])
-        for n in range(2, NT):
-            load_state(n)
+        load_o(1)
 
         warm = held([P, 1], F32, "warm")
         nc.scalar.activation(warm[:], b3_t[:, 0:1], ACT.Sigmoid)
 
-        v_w = [held([P, S], U32, f"v_w{a}") for a in range(PASSES)]
-        for a in range(PASSES):
-            nc.vector.tensor_copy(v_w[a][:], tab_w[a][:].bitcast(U32).indirect(offsets[:]))
+        v_planes = (v_sc, v_sc_raised)
+        v_parts = []
 
-        def reorder(dst, src, walk):
-            nc.vector.tensor_copy(dst.rearrange(f"p (a t m) -> p {walk}", a=PASSES, t=PACK),
-                                  src.rearrange(f"p (a m t) -> p {walk}", a=PASSES, t=PACK))
+        def gather_words(a, entries, slot):
+            part = shared([P, entries.stop - entries.start], U32, "v_w", slot)
+            nc.vector.tensor_copy(part[:], tab_w[a][:].bitcast(U32).indirect(listed(entries)))
+            v_parts.append((a, entries, part))
 
-        w3_codes = held([P, PASSES * H], I32, "w3_codes")
+        def v_words(a, entries):
+            for b, whole, part in v_parts:
+                if a == b and whole.start <= entries.start < whole.stop:
+                    return part[:, entries.start - whole.start : entries.stop - whole.start]
+
+        def reorder(copy, dst, src, walk):
+            copy(dst.rearrange(f"p (a t m) -> p {walk}", a=PASSES, t=PACK),
+                 src.rearrange(f"p (a m t) -> p {walk}", a=PASSES, t=PACK))
+
+        w3_codes = held([P, PASSES * H], U32, "w3_codes")
         w2_codes = held([P, PASSES * 2 * H], U8, "w2_codes")
-        w_sc = held([P, PASSES * H], U8, "w_sc")
-        reorder(w_sc[:], w_sc_raw[:], "a t m")
-        reorder(w3_codes[:], w3_raw[:], "a m t")
-        reorder(w2_codes[:].bitcast(U16), w2_raw[:].bitcast(U16), "a t m")
+        w2_sc = held([P, PASSES * H], U8, "w2_sc")
+        reorder(nc.scalar.copy, w2_codes[:].bitcast(U16), w2_raw[:].bitcast(U16), "a m t")
+        reorder(nc.scalar.copy, w3_codes[:], w3_raw[:].bitcast(U32), "a m t")
+        gather_words(0, slice(0, S), "v_slot0")
+        gather_words(1, slice(0, S // 2), "v_slot1")
+        reorder(nc.vector.tensor_copy, w2_sc[:], w2_sc_raw[:], "a t m")
+        gather_words(1, slice(S // 2, S), "w2_sc_slot")
+        w3_sc = shared([P, PASSES * H], U8, "w3_sc", "tab_slot1")
+        reorder(nc.vector.tensor_copy, w3_sc[:], w3_sc_raw[:], "a t m")
 
-        w1_bf = shared([P, PASSES * PACK * H], BF16, "w1_bf", "w1_slot")
-        for a in range(PASSES):
-            dst = w1_bf[:, a * PACK * H : (a + 1) * PACK * H]
-            nc.scalar.copy(dst.rearrange("p (t m j) -> p m j t", t=PACK, j=PACK),
-                           w1_raw[a][:].rearrange("p j (m t) -> p m j t", t=PACK))
-        w1_codes = shared([P, PASSES * H], U32, "w1_codes", "w3_slot")
+        def gpsimd_cast(dst, src):
+            nc.gpsimd.tensor_scalar(dst, src, 1.0, 0.0, ALU.mult, ALU.add)
+
+        w1_codes = held([P, PASSES * H], U32, "w1_codes")
         w1_sc = held([P, PASSES * H], U8, "w1_sc")
-        nc.vector.quantize_mx(out=w1_codes[:].bitcast(FP8X4), scales=w1_sc[:], in_=w1_bf[:])
+        w1_bf = shared([P, PASSES, PACK * H], BF16, "w1_bf", "w1_slot")[:]
 
-        def w1_side(a, t):
-            first = a * H + t * P
+        def cast_w1(cast, a, columns, walk):
+            cast(w1_bf[:, a, :].rearrange("p (t m j) -> p m t j", t=PACK, j=PACK)[:, columns].rearrange(f"p m t j -> p {walk}"),
+                 w1_raw[a][:].rearrange("p j (m t) -> p m t j", t=PACK)[:, columns].rearrange(f"p m t j -> p {walk}"))
+
+        def w1_side(first):
             return w1_codes[:, first : first + P].bitcast(FP8X4), w1_sc[:, first : first + P]
 
-        def w2_side(a, t):
-            first = a * H + t * P
-            return w2_codes[:, 2 * first : 2 * (first + P)].bitcast(FP4X4), w_sc[:, first : first + P]
+        def w2_side(first):
+            return w2_codes[:, 2 * first : 2 * (first + P)].bitcast(FP4X4), w2_sc[:, first : first + P]
 
-        def w3_side(a, t):
-            first = a * H + t * P
-            return w3_codes[:, first : first + P].bitcast(FP8X4), w_sc[LOW:P, first : first + P]
+        def w3_side(first):
+            return w3_codes[:, first : first + P].bitcast(FP8X4), w3_sc[:, first : first + P]
 
-        planes_e4m3 = planes_e2m1 = (v_sc[:], v_sc_raised[:])
-
-        def first_product(dst, side, planes, t, entries):
+        def first_product(bank, side, first, entries):
+            count = bank.shape[1]
             for a in range(PASSES):
-                codes, scales = side(a, t)
-                nc.tensor.matmul_mx(out=dst, lhsT=codes, lhsT_scale=scales, rhs=v_w[a][:, entries].bitcast(FP8X4),
-                                    rhs_scale=planes[a][:, entries], start=(a == 0), stop=(a == PASSES - 1))
+                for e in range(count):
+                    codes, scales = side(a * H + (first + e) * P)
+                    nc.tensor.matmul_mx(out=bank[:, e, :], lhsT=codes, lhsT_scale=scales,
+                                        rhs=v_words(a, entries).bitcast(FP8X4), rhs_scale=v_planes[a][:, entries],
+                                        start=(a == 0 and e == 0), stop=(a == PASSES - 1 and e == count - 1))
 
-        o_bf = shared([P, 2, N * PACK], BF16, "o_bf", "w1_slot")
-        for i, raw in enumerate((o1_raw, o3_raw)):
-            nc.gpsimd.tensor_scalar(o_bf[:, i, :].rearrange("p (c j) -> p c j", j=PACK),
-                                    raw[:].rearrange("p j c -> p c j"), 1.0, 0.0, ALU.mult, ALU.add)
-        late_codes = shared([P, 2 * N + 2 * S], U32, "late_codes", "o3_slot")
-        o_sc = held([P, 2 * N], U8, "o_sc")
-        o_sides = ((late_codes[:, 0:N], o_sc[:, 0:N]), (o2_codes, o2_sc),
-                   (late_codes[:, N : 2 * N], o_sc[:, N : 2 * N]))
-        h3_codes = shared([P, S], U32, "h3_codes", "o1_slot")[:]
-        h21_codes = late_codes[:, 2 * N : 2 * N + 2 * S]
-        h3_sc = held([P, S], U8, "h3_sc")
+        def along_r(vec):
+            return vec[:].unsqueeze(1).to_broadcast([P, P, PACK])
+
+        def woven(values):
+            return values.rearrange("p (n t) -> p n t", t=PACK)
+
+        def weave(copy, dst, slices):
+            copy(dst.rearrange("p (c i t) -> p c t i", i=RUN, t=PACK), slices.rearrange("p t (c i) -> p c t i", i=RUN))
+
+        branches = {"h1": (w1_side, ACT.Tanh, gain1_t), "h2": (w2_side, ACT.Sigmoid, gain2_t)}
+
+        def activate_woven(name, c, act):
+            side, func = branches[name][:2]
+            for s in range(CH // P):
+                bank = ring_bank([P, PACK, P])
+                first_product(bank, side, 0, slice(c * CH + s * P, c * CH + (s + 1) * P))
+                nc.scalar.activation(woven(act[:, s * P * PACK : (s + 1) * P * PACK]),
+                                     bank[:].rearrange("p t n -> p n t"), func)
+            return act
+
+        def gain_on_gpsimd(name, act, dst):
+            for s in range(CH // P):
+                part = slice(s * P * PACK, (s + 1) * P * PACK)
+                nc.gpsimd.tensor_tensor(woven(dst[:, part]), woven(act[:, part]), along_r(branches[name][2]), ALU.mult)
+
+        def activate(name, c, pairs):
+            side, func = branches[name][:2]
+            for pair, act in enumerate(pairs):
+                bank = ring_bank([P, 2, CH])
+                first_product(bank, side, 2 * pair, chunk(c))
+                nc.scalar.activation(act, bank[:], func)
+
+        def gain_on_scalar(name, pairs, slot):
+            gain = branches[name][2]
+            slices = shared([P, PACK, CH], BF16, "slices", slot)
+            for t in range(PACK):
+                nc.scalar.activation(slices[:, t, :], pairs[t // 2][:, t % 2, :], ACT.Copy, scale=gain[:, t : t + 1])
+            return slices[:]
+
+        h3_place = {}
+        h21_codes = held([P, 2 * S], U32, "h21_codes")
         h21_sc = held([P, 2 * S], U8, "h21_sc")
 
-        def h_side(name, c):
-            if name == "h3":
-                return h3_codes[:, chunk(c)], h3_sc[:, chunk(c)]
-            cols = chunk(2 * c + (name == "h1"))
-            return h21_codes[:, cols], h21_sc[:, cols]
+        def quantize_h3(chunks, values, slot):
+            codes = shared([P, len(chunks) * CH], U32, "h3_codes", slot)
+            plane = held([P, len(chunks) * CH], U8, f"h3_sc{chunks[0]}")
+            nc.vector.quantize_mx(out=codes[:].bitcast(FP8X4), scales=plane[:], in_=values)
+            for e, c in enumerate(chunks):
+                h3_place[c] = codes[:, chunk(e)], plane[:, chunk(e)]
 
-        def chunk(c):
-            return slice(c * CH, (c + 1) * CH)
+        def affine_by_vector(c, dst):
+            for s in range(CH // P):
+                bank = psum.tile([P, PACK, P], F32, name="x3_bank", bufs=8 - RING)
+                first_product(bank, w3_side, 0, slice(c * CH + s * P, c * CH + (s + 1) * P))
+                nc.vector.tensor_tensor(woven(dst[:, s * P * PACK : (s + 1) * P * PACK]),
+                                        bank[:].rearrange("p t n -> p n t"), along_r(b3_t), ALU.add)
 
-        def gated_branch(name, c, side, planes, width, func, gain, dst):
-            act = work.tile([P, PACK, CH], F32, name="act")
+        def affine_by_scalar(c, dst, slices):
             for pair in range(PACK // 2):
-                bank = psum.tile([P, 2, CH], F32, name="x_bank", bufs=3)
-                for e in range(2):
-                    for s in range(0, CH, width):
-                        first_product(bank[:, e, s : s + width], side, planes, 2 * pair + e,
-                                      slice(c * CH + s, c * CH + s + width))
-                nc.scalar.activation(act[:, 2 * pair : 2 * pair + 2, :], bank[:], func)
-            slices = shared([P, PACK, CH], BF16, "slices", f"{name}_slot{c}")
-            for t in range(PACK):
-                nc.scalar.activation(slices[:, t, :], act[:, t, :], ACT.Copy, scale=gain[:, t : t + 1])
-            if c == 1:
-                nc.gpsimd.tensor_scalar(dst.rearrange("p (c t) -> p c t", t=PACK),
-                                        slices[:].rearrange("p t c -> p c t"), 1.0, 0.0, ALU.mult, ALU.add)
-            else:
-                nc.scalar.copy(dst.rearrange("p (c i t) -> p c t i", i=RUN, t=PACK),
-                               slices[:].rearrange("p t (c i) -> p c t i", i=RUN))
-
-        def gated(c):
-            if c == 1:
-                h_bf = shared([P, 2, CH * PACK], BF16, "h_bf", "w1_slot")
-            else:
-                h_bf = work.tile([P, 2, CH * PACK], BF16, name="h_bf", align_bytes=64)
-            gated_branch("h2", c, w2_side, planes_e2m1, P, ACT.Sigmoid, gain2_t, h_bf[:, 0, :])
-            gated_branch("h1", c, w1_side, planes_e4m3, CH, ACT.Tanh, gain1_t, h_bf[:, 1, :])
-            cols = slice(2 * c * CH, 2 * (c + 1) * CH)
-            nc.vector.quantize_mx(out=h21_codes[:, cols].bitcast(FP8X4), scales=h21_sc[:, cols],
-                                  in_=h_bf[:].rearrange("p b c -> p (b c)"))
-
-        h3_bf = held([P, S * PACK], BF16, "h3_bf")
-
-        def affine(c):
-            for s in range(c * CH, (c + 1) * CH, P):
-                bank = psum.tile([P, PACK, P], F32, name="x3_bank", bufs=4)
-                for t in range(PACK):
-                    first_product(bank[:, t, :], w3_side, planes_e4m3, t, slice(s, s + P))
-                nc.vector.tensor_tensor(h3_bf[:, s * PACK : (s + P) * PACK].rearrange("p (n t) -> p n t", t=PACK),
-                                        bank[:].rearrange("p t n -> p n t"),
-                                        b3_t[:].unsqueeze(1).to_broadcast([P, P, PACK]), ALU.add)
-
-        def quantize_h3(entries, values):
-            nc.vector.quantize_mx(out=h3_codes[:, entries].bitcast(FP8X4), scales=h3_sc[:, entries], in_=values)
-
-        def affine_on_scalar(c):
-            slices = held([P, PACK, CH], BF16, "h3_slices")
-            for pair in range(PACK // 2):
-                bank = psum.tile([P, 2, CH], F32, name="x_bank", bufs=3)
-                for e in range(2):
-                    first_product(bank[:, e, :], w3_side, planes_e4m3, 2 * pair + e, chunk(c))
+                bank = ring_bank([P, 2, CH])
+                first_product(bank, w3_side, 2 * pair, chunk(c))
                 for e in range(2):
                     t = 2 * pair + e
                     nc.scalar.activation(slices[:, t, :], bank[:, e, :], ACT.Identity, bias=b3_t[:, t : t + 1])
-            woven = held([P, CH * PACK], BF16, "h3_last")
-            nc.scalar.copy(woven[:].rearrange("p (c i t) -> p c t i", i=RUN, t=PACK),
-                           slices[:].rearrange("p t (c i) -> p c t i", i=RUN))
-            quantize_h3(chunk(c), woven[:])
+            weave(nc.scalar.copy, dst, slices)
 
-        def second_stage(tiles, entries, slot):
-            width = entries.stop - entries.start
-            y = shared([P, len(tiles), width], F32, "y", slot)
-            bank = psum.tile([P, len(tiles), width], F32, name="y_bank")
-            for e, n in enumerate(tiles):
-                cols = slice(n * P, (n + 1) * P)
-                for c in range(entries.start // CH, entries.stop // CH):
-                    first = c * CH - entries.start
-                    for b, name in enumerate(BRANCHES):
-                        codes, scales = h_side(name, c)
-                        nc.tensor.matmul_mx(out=bank[:, e, first : first + CH],
-                                            lhsT=o_sides[b][0][:, cols].bitcast(FP8X4),
-                                            lhsT_scale=o_sides[b][1][:, cols], rhs=codes.bitcast(FP8X4),
-                                            rhs_scale=scales, start=(b == 0), stop=(b == 2))
-            nc.scalar.copy(y[:], bank[:])
-            for e, n in enumerate(tiles):
-                nc.vector.tensor_tensor(state[n][:].indirect(listed(entries)), y[:, e, :], picked[n][:, entries],
-                                        ALU.mult)
-                if entries.stop == S:
-                    nc.sync.dma_start(out=out[n * P : (n + 1) * P, :], in_=state[n][:])
+        h_place = {}
 
-        picked = [held([P, S], F32, f"picked{n}") for n in range(NT)]
+        def quantize_h21(c, names, h_bf):
+            cols = slice(2 * c * CH, 2 * (c + 1) * CH)
+            nc.vector.quantize_mx(out=h21_codes[:, cols].bitcast(FP8X4), scales=h21_sc[:, cols],
+                                  in_=h_bf.rearrange("p b c -> p (b c)"))
+            for b, name in enumerate(names):
+                h_place[name, c] = chunk(2 * c + b)
+
+        o_codes = [held([P, 2, P * PAIR], U32, f"o_codes{half}") for half in range(HALVES)]
+        o_sc = [held([P, 2, P * PAIR], U8, f"o_sc{half}") for half in range(HALVES)]
+
+        def quantize_o(half, o_bf):
+            nc.vector.quantize_mx(out=o_codes[half][:].rearrange("p i c -> p (i c)").bitcast(FP8X4),
+                                  scales=o_sc[half][:].rearrange("p i c -> p (i c)"),
+                                  in_=o_bf.rearrange("p i c -> p (i c)"))
+
+        picked = [held([P, PAIR, S], F32, f"picked{half}") for half in range(HALVES)]
 
         def pick(n):
-            nc.vector.tensor_copy(picked[n][:], state[n][:].indirect(offsets[:]))
+            nc.vector.tensor_copy(picked[n // PAIR][:, n % PAIR, :], state[n][:].indirect(offsets[:]))
 
-        pick(0)
-        nc.vector.quantize_mx(out=late_codes[:, 0 : 2 * N].bitcast(FP8X4), scales=o_sc[:],
-                              in_=o_bf[:].rearrange("p i c -> p (i c)"))
-        gated(0)
-        for c in range(CHUNKS - 1):
-            affine(c)
-        quantize_h3(slice(0, 2 * CH), h3_bf[:, 0 : 2 * CH * PACK])
-        quantize_h3(chunk(2), h3_bf[:, 2 * CH * PACK : 3 * CH * PACK])
-        for n in range(1, NT):
-            pick(n)
+        def second_product(dst, n, c):
+            half, own, cols = n // PAIR, slice(n % PAIR * P, (n % PAIR + 1) * P), slice(n * P, (n + 1) * P)
+            sides = ((o_codes[half][:, 0, own], o_sc[half][:, 0, own], h21_codes[:, h_place["h1", c]],
+                      h21_sc[:, h_place["h1", c]]),
+                     (o2_codes[half][:, own], o2_sc[:, cols], h21_codes[:, h_place["h2", c]], h21_sc[:, h_place["h2", c]]),
+                     (o_codes[half][:, 1, own], o_sc[half][:, 1, own], *h3_place[c]))
+            for b, (o_words, o_plane, h_words, h_plane) in enumerate(sides):
+                nc.tensor.matmul_mx(out=dst, lhsT=o_words.bitcast(FP8X4), lhsT_scale=o_plane,
+                                    rhs=h_words.bitcast(FP8X4), rhs_scale=h_plane, start=(b == 0), stop=(b == 2))
+
+        def second_stage(tiles, entries, y):
+            width = entries.stop - entries.start
+            bank = ring_bank([P, len(tiles), width])
+            for e, n in enumerate(tiles):
+                for c in range(entries.start // CH, entries.stop // CH):
+                    second_product(bank[:, e, c * CH - entries.start : (c + 1) * CH - entries.start], n, c)
+            y = y.rearrange("p (e c) -> p e c", e=len(tiles))
+            nc.scalar.copy(y, bank[:])
+            return {n: y[:, e, :] for e, n in enumerate(tiles)}
+
+        def scatter(n, entries, y):
+            nc.vector.tensor_tensor(state[n][:].indirect(listed(entries)), y[n],
+                                    picked[n // PAIR][:, n % PAIR, entries], ALU.mult)
+            if entries.stop == S:
+                nc.sync.dma_start(out=out[n * P : (n + 1) * P, :], in_=state[n][:])
+
+        def finish(tiles, entries, y):
+            y = second_stage(tiles, entries, y)
+            for n in tiles:
+                scatter(n, entries, y)
+
+        def y_tile(slot):
+            return shared([P, PAIR * CH], F32, "y", slot)[:]
+
+        def halves(act):
+            return act[:, 0:2, :], act[:, 2:4, :]
 
         upper, lower = (0, 1), (2, 3)
+        h_bf0, h_bf3 = (held([P, 2, CH * PACK], BF16, f"h_bf{c}")[:] for c in (0, 3))
+        mixed = held([P, 4, CH * PACK], BF16, "mixed")
+        h_bf2, h_bf1, o_bf0 = mixed[:, 0:2, :], mixed[:, 1:3, :], mixed[:, 2:4, :]
+        o_bf1 = shared([P, 2, P * PAIR * PACK], BF16, "o_bf1", "o_bf1_slot")[:]
+        h3_bf = held([P, S * PACK], BF16, "h3_bf")
+
+        def act_tile(slot):
+            return shared([P, CH * PACK], F32, "act", slot)[:]
+
+        def flat(rows):
+            return rows.rearrange("p j c -> p (j c)")
+
+        def h3_part(first, last):
+            return h3_bf[:, first * CH * PACK : last * CH * PACK]
+
+        gain_on_gpsimd("h2", activate_woven("h2", 0, act_tile("act_a")), h_bf0[:, 0, :])
+        cast_w1(nc.scalar.copy, 0, slice(0, P), "m j t")
+        cast_w1(nc.scalar.copy, 1, slice(0, W1_SPLIT), "m j t")
+        cast_w1(gpsimd_cast, 1, slice(W1_SPLIT, P), "t m j")
         for c in range(CHUNKS - 1):
-            if c == 1:
-                affine_on_scalar(CHUNKS - 1)
-            gated(c + 1)
-            second_stage(upper, chunk(c), f"h1_slot{c + 1}")
-            if c < CHUNKS - 2:
-                second_stage(lower, chunk(c), f"y_lower{c}")
-        second_stage(upper, chunk(CHUNKS - 1), "y_upper_last")
+            affine_by_vector(c, h3_part(c, c + 1))
+        act = halves(w1_raw[1][:, :, 0:CH])
+        activate("h2", 1, act)
+        nc.vector.quantize_mx(out=w1_codes[:].bitcast(FP8X4), scales=w1_sc[:], in_=w1_bf.rearrange("p a c -> p (a c)"))
+        quantize_h3((0, 1), h3_part(0, 2), "w1_slot")
+        quantize_h3((2,), h3_part(2, 3), "h3_slot2")
+        slices = gain_on_scalar("h2", act, "slices_a")
+        gain_on_gpsimd("h1", activate_woven("h1", 0, act_tile("act_b")), h_bf0[:, 1, :])
+        weave(nc.scalar.copy, h_bf1[:, 0, :], slices)
+        act = activate_woven("h1", 1, act_tile("act_a"))
+        pick(2)
+        pick(3)
+        gpsimd_cast(woven(o_bf0[:, 0, :]), o_raw[0][:, 0].rearrange("p j c -> p c j"))
+        weave(nc.scalar.copy, o_bf0[:, 1, :], o_raw[0][:, 1])
+        quantize_h21(0, ("h2", "h1"), h_bf0)
+        quantize_o(0, o_bf0)
+        pick(0)
+        gain_on_gpsimd("h1", act, h_bf1[:, 1, :])
+        affine_by_scalar(3, h3_part(3, 4),
+                         flat(o_raw[0][:, 1, 0:2, :]).bitcast(BF16).rearrange("p (t c) -> p t c", t=PACK))
+        y = second_stage(upper, chunk(0), y_tile("y_a"))
+        scatter(0, chunk(0), y)
+        woven_act = activate_woven("h2", 2, flat(o_raw[0][:, 1]))
+        quantize_h21(1, ("h2", "h1"), h_bf1)
+        gain_on_gpsimd("h2", woven_act, h_bf2[:, 1, :])
+        pick(1)
+        scatter(1, chunk(0), y)
+        act = halves(o_raw[0][:, 0])
+        activate("h1", 2, act)
+        for i in range(2):
+            weave(nc.scalar.copy, o_bf1[:, i, :], o_raw[1][:, i])
+        quantize_o(1, o_bf1)
+        quantize_h3((3,), h3_part(3, 4), "o_bf1_slot")
+        finish(upper, chunk(1), flat(o_raw[1][:, 1, 0:2, :]))
+        weave(nc.scalar.copy, h_bf2[:, 0, :], gain_on_scalar("h1", act, "slices_b"))
+        quantize_h21(2, ("h1", "h2"), h_bf2)
+        act = o_raw[1][:, 1, 2:4, :], o_raw[1][:, 0, 0:2, :]
+        activate("h2", 3, act)
+        finish(lower[:1], slice(0, 2 * CH), y_tile("slices_b"))
+        slices = gain_on_scalar("h2", act, "slices_a")
+        finish(lower[1:], slice(0, 2 * CH), flat(o_raw[1][:, 0, 0:2, :]))
+        weave(nc.scalar.copy, h_bf3[:, 0, :], slices)
+        act = halves(w1_raw[0][:, :, 0:CH])
+        activate("h1", 3, act)
+        finish(upper[:1], chunk(2), y_tile("slices_a")[:, 0:CH])
+        weave(nc.scalar.copy, h_bf3[:, 1, :], gain_on_scalar("h1", act, "slices_c"))
+        quantize_h21(3, ("h2", "h1"), h_bf3)
+        finish(upper[1:], chunk(2), y_tile("slices_c")[:, 0:CH])
+        for n in upper:
+            finish((n,), chunk(3), y_tile(f"y_last{n}")[:, 0:CH])
         for n in lower:
-            second_stage((n,), slice((CHUNKS - 2) * CH, S), f"y_last{n}")
+            finish((n,), slice(2 * CH, S), y_tile(f"y_last{n}"))

@@ -53,6 +53,9 @@ def tile_list_fader_balance_mix_kernel(tc, tab_words, tab_scales, offs, gT, w1, 
         def listed(entries):
             return offsets[:, entries.start // GROUP : entries.stop // GROUP]
 
+        def flat(rows):
+            return rows.rearrange("p j c -> p (j c)")
+
         def chunk(c):
             return slice(c * CH, (c + 1) * CH)
 
@@ -221,16 +224,13 @@ def tile_list_fader_balance_mix_kernel(tc, tab_words, tab_scales, offs, gT, w1, 
                 first_product(bank, side, 2 * pair, chunk(c))
                 nc.scalar.activation(act, bank[:], func)
 
-        def gain_on_scalar(name, pairs, slot):
+        def gain_on_scalar(name, pairs, slices):
             gain = branches[name][2]
-            slices = shared([P, PACK, CH], BF16, "slices", slot)
             for t in range(PACK):
                 nc.scalar.activation(slices[:, t, :], pairs[t // 2][:, t % 2, :], ACT.Copy, scale=gain[:, t : t + 1])
-            return slices[:]
+            return slices
 
         h3_place = {}
-        h21_codes = held([P, 2 * S], U32, "h21_codes")
-        h21_sc = held([P, 2 * S], U8, "h21_sc")
 
         def quantize_h3(chunks, values, slot):
             codes = shared([P, len(chunks) * CH], U32, "h3_codes", slot)
@@ -257,12 +257,12 @@ def tile_list_fader_balance_mix_kernel(tc, tab_words, tab_scales, offs, gT, w1, 
 
         h_place = {}
 
-        def quantize_h21(c, names, h_bf):
-            cols = slice(2 * c * CH, 2 * (c + 1) * CH)
-            nc.vector.quantize_mx(out=h21_codes[:, cols].bitcast(FP8X4), scales=h21_sc[:, cols],
-                                  in_=h_bf.rearrange("p b c -> p (b c)"))
+        def quantize_h21(c, names, h_bf, slot):
+            codes = shared([P, 2, CH], U32, "h_codes", slot)
+            plane = held([P, 2, CH], U8, f"h_sc{c}")
+            nc.vector.quantize_mx(out=flat(codes[:]).bitcast(FP8X4), scales=flat(plane[:]), in_=flat(h_bf))
             for b, name in enumerate(names):
-                h_place[name, c] = chunk(2 * c + b)
+                h_place[name, c] = codes[:, b, :], plane[:, b, :]
 
         o_codes = [held([P, 2, P * PAIR], U32, f"o_codes{half}") for half in range(HALVES)]
         o_sc = [held([P, 2, P * PAIR], U8, f"o_sc{half}") for half in range(HALVES)]
@@ -272,16 +272,16 @@ def tile_list_fader_balance_mix_kernel(tc, tab_words, tab_scales, offs, gT, w1, 
                                   scales=o_sc[half][:].rearrange("p i c -> p (i c)"),
                                   in_=o_bf.rearrange("p i c -> p (i c)"))
 
-        picked = [held([P, PAIR, S], F32, f"picked{half}") for half in range(HALVES)]
+        picked = {}
 
-        def pick(n):
-            nc.vector.tensor_copy(picked[n // PAIR][:, n % PAIR, :], state[n][:].indirect(offsets[:]))
+        def pick(n, slot):
+            picked[n] = shared([P, S], F32, "picked", slot)
+            nc.vector.tensor_copy(picked[n][:], state[n][:].indirect(offsets[:]))
 
         def second_product(dst, n, c):
             half, own, cols = n // PAIR, slice(n % PAIR * P, (n % PAIR + 1) * P), slice(n * P, (n + 1) * P)
-            sides = ((o_codes[half][:, 0, own], o_sc[half][:, 0, own], h21_codes[:, h_place["h1", c]],
-                      h21_sc[:, h_place["h1", c]]),
-                     (o2_codes[half][:, own], o2_sc[:, cols], h21_codes[:, h_place["h2", c]], h21_sc[:, h_place["h2", c]]),
+            sides = ((o_codes[half][:, 0, own], o_sc[half][:, 0, own], *h_place["h1", c]),
+                     (o2_codes[half][:, own], o2_sc[:, cols], *h_place["h2", c]),
                      (o_codes[half][:, 1, own], o_sc[half][:, 1, own], *h3_place[c]))
             for b, (o_words, o_plane, h_words, h_plane) in enumerate(sides):
                 nc.tensor.matmul_mx(out=dst, lhsT=o_words.bitcast(FP8X4), lhsT_scale=o_plane,
@@ -299,7 +299,7 @@ def tile_list_fader_balance_mix_kernel(tc, tab_words, tab_scales, offs, gT, w1, 
 
         def scatter(n, entries, y):
             nc.vector.tensor_tensor(state[n][:].indirect(listed(entries)), y[n],
-                                    picked[n // PAIR][:, n % PAIR, entries], ALU.mult)
+                                    picked[n][:, entries], ALU.mult)
             if entries.stop == S:
                 nc.sync.dma_start(out=out[n * P : (n + 1) * P, :], in_=state[n][:])
 
@@ -319,69 +319,66 @@ def tile_list_fader_balance_mix_kernel(tc, tab_words, tab_scales, offs, gT, w1, 
         mixed = held([P, 4, CH * PACK], BF16, "mixed")
         h_bf2, h_bf1, o_bf0 = mixed[:, 0:2, :], mixed[:, 1:3, :], mixed[:, 2:4, :]
         o_bf1 = shared([P, 2, P * PAIR * PACK], BF16, "o_bf1", "o_bf1_slot")[:]
-        h3_bf = held([P, S * PACK], BF16, "h3_bf")
+        h3_bf = [shared([P, size * CH * PACK], BF16, "h3_bf", f"h3_bf_slot{e}")[:] for e, size in enumerate((2, 1, 1))]
 
         def act_tile(slot):
             return shared([P, CH * PACK], F32, "act", slot)[:]
 
-        def flat(rows):
-            return rows.rearrange("p j c -> p (j c)")
+        def slices_tile(slot):
+            return shared([P, PACK, CH], BF16, "slices", slot)[:]
 
-        def h3_part(first, last):
-            return h3_bf[:, first * CH * PACK : last * CH * PACK]
+        def as_slices(rows):
+            return flat(rows).bitcast(BF16).rearrange("p (t c) -> p t c", t=PACK)
 
         gain_on_gpsimd("h2", activate_woven("h2", 0, act_tile("act_a")), h_bf0[:, 0, :])
         cast_w1(nc.scalar.copy, 0, slice(0, P), "m j t")
         cast_w1(nc.scalar.copy, 1, slice(0, W1_SPLIT), "m j t")
         cast_w1(gpsimd_cast, 1, slice(W1_SPLIT, P), "t m j")
-        for c in range(CHUNKS - 1):
-            affine_by_vector(c, h3_part(c, c + 1))
+        for c, dst in enumerate((h3_bf[0][:, : CH * PACK], h3_bf[0][:, CH * PACK :], h3_bf[1])):
+            affine_by_vector(c, dst)
         act = halves(w1_raw[1][:, :, 0:CH])
         activate("h2", 1, act)
         nc.vector.quantize_mx(out=w1_codes[:].bitcast(FP8X4), scales=w1_sc[:], in_=w1_bf.rearrange("p a c -> p (a c)"))
-        quantize_h3((0, 1), h3_part(0, 2), "w1_slot")
-        quantize_h3((2,), h3_part(2, 3), "h3_slot2")
-        slices = gain_on_scalar("h2", act, "slices_a")
+        quantize_h3((0, 1), h3_bf[0], "w1_slot")
+        quantize_h3((2,), h3_bf[1], "h3_slot2")
+        slices = gain_on_scalar("h2", act, slices_tile("slices_a"))
         gain_on_gpsimd("h1", activate_woven("h1", 0, act_tile("act_b")), h_bf0[:, 1, :])
         weave(nc.scalar.copy, h_bf1[:, 0, :], slices)
         act = activate_woven("h1", 1, act_tile("act_a"))
-        pick(2)
-        pick(3)
+        pick(2, "h3_bf_slot0")
+        pick(3, "picked3")
         gpsimd_cast(woven(o_bf0[:, 0, :]), o_raw[0][:, 0].rearrange("p j c -> p c j"))
         weave(nc.scalar.copy, o_bf0[:, 1, :], o_raw[0][:, 1])
-        quantize_h21(0, ("h2", "h1"), h_bf0)
+        quantize_h21(0, ("h2", "h1"), h_bf0, "codes0")
         quantize_o(0, o_bf0)
-        pick(0)
+        pick(0, "picked0")
         gain_on_gpsimd("h1", act, h_bf1[:, 1, :])
-        affine_by_scalar(3, h3_part(3, 4),
-                         flat(o_raw[0][:, 1, 0:2, :]).bitcast(BF16).rearrange("p (t c) -> p t c", t=PACK))
-        y = second_stage(upper, chunk(0), y_tile("y_a"))
-        scatter(0, chunk(0), y)
+        affine_by_scalar(3, h3_bf[2], as_slices(o_raw[0][:, 1, 0:2, :]))
+        finish(upper[:1], chunk(0), y_tile("y_first0")[:, 0:CH])
+        y = second_stage(upper[1:], chunk(0), y_tile("y_first1")[:, 0:CH])
         woven_act = activate_woven("h2", 2, flat(o_raw[0][:, 1]))
-        quantize_h21(1, ("h2", "h1"), h_bf1)
+        quantize_h21(1, ("h2", "h1"), h_bf1, "y_first0")
         gain_on_gpsimd("h2", woven_act, h_bf2[:, 1, :])
-        pick(1)
+        pick(1, "picked1")
         scatter(1, chunk(0), y)
         act = halves(o_raw[0][:, 0])
         activate("h1", 2, act)
         for i in range(2):
             weave(nc.scalar.copy, o_bf1[:, i, :], o_raw[1][:, i])
         quantize_o(1, o_bf1)
-        quantize_h3((3,), h3_part(3, 4), "o_bf1_slot")
+        quantize_h3((3,), h3_bf[2], "o_bf1_slot")
         finish(upper, chunk(1), flat(o_raw[1][:, 1, 0:2, :]))
-        weave(nc.scalar.copy, h_bf2[:, 0, :], gain_on_scalar("h1", act, "slices_b"))
-        quantize_h21(2, ("h1", "h2"), h_bf2)
-        act = o_raw[1][:, 1, 2:4, :], o_raw[1][:, 0, 0:2, :]
+        weave(nc.scalar.copy, h_bf2[:, 0, :], gain_on_scalar("h1", act, as_slices(o_raw[1][:, 1, 2:4, :])))
+        quantize_h21(2, ("h1", "h2"), h_bf2, "codes2")
         activate("h2", 3, act)
-        finish(lower[:1], slice(0, 2 * CH), y_tile("slices_b"))
-        slices = gain_on_scalar("h2", act, "slices_a")
+        finish(lower[:1], slice(0, 2 * CH), flat(o_raw[1][:, 1, 2:4, :]))
+        slices = gain_on_scalar("h2", act, slices_tile("slices_a"))
         finish(lower[1:], slice(0, 2 * CH), flat(o_raw[1][:, 0, 0:2, :]))
         weave(nc.scalar.copy, h_bf3[:, 0, :], slices)
-        act = halves(w1_raw[0][:, :, 0:CH])
         activate("h1", 3, act)
         finish(upper[:1], chunk(2), y_tile("slices_a")[:, 0:CH])
-        weave(nc.scalar.copy, h_bf3[:, 1, :], gain_on_scalar("h1", act, "slices_c"))
-        quantize_h21(3, ("h2", "h1"), h_bf3)
+        weave(nc.scalar.copy, h_bf3[:, 1, :], gain_on_scalar("h1", act, slices_tile("slices_c")))
+        quantize_h21(3, ("h2", "h1"), h_bf3, "codes3")
         finish(upper[1:], chunk(2), y_tile("slices_c")[:, 0:CH])
         for n in upper:
             finish((n,), chunk(3), y_tile(f"y_last{n}")[:, 0:CH])

@@ -20,13 +20,14 @@ P = 128
 PACK = 4
 PASSES = K // (P * PACK)
 ROWS = 4
+LOW = 4
 GROUP = 16
 CH = 256
 CHUNKS = S // CH
 PAIR = 2
 HALVES = N // (P * PAIR)
 RUN = 4
-W1_SPLIT = 88
+REGION = 8192
 RING = 4
 
 
@@ -36,6 +37,7 @@ def tile_list_fader_balance_mix_kernel(tc, tab_words, tab_scales, offs, gT, w1, 
     nc = tc.nc
     with ExitStack() as ctx:
         keep = ctx.enter_context(tc.tile_pool(name="keep", bufs=1))
+        placed = ctx.enter_context(tc.tile_pool(name="placed", bufs=1))
         psum = ctx.enter_context(tc.psum_pool(name="psum", bufs=1))
 
         def held(shape, dtype, name):
@@ -43,6 +45,9 @@ def tile_list_fader_balance_mix_kernel(tc, tab_words, tab_scales, offs, gT, w1, 
 
         def shared(shape, dtype, name, slot):
             return keep.tile(shape, dtype, name=name, tag=slot, align_bytes=64)
+
+        def placed_at(region, part, shape, dtype, name):
+            return placed.tile(shape, dtype, name=name, offset=region * REGION + part * REGION // 4, align_bytes=64)
 
         turns = []
 
@@ -63,11 +68,10 @@ def tile_list_fader_balance_mix_kernel(tc, tab_words, tab_scales, offs, gT, w1, 
         nc.sync.dma_start(offsets[:], offs)
 
         tab_sc = held([P, T], U8, "tab_sc")
-        w2_sc_raw = shared([P, PASSES * H], U8, "w2_sc_raw", "w2_sc_slot")
-        w3_sc_raw = held([P, PASSES * H], U8, "w3_sc_raw")
+        w_sc_raw = held([P, PASSES * H], U8, "w_sc_raw")
         v_sc_raised = held([P, S], U8, "v_sc_raised")
         o2_sc = held([P, N], U8, "o2_sc")
-        for plane in (tab_sc, w3_sc_raw, w2_sc_raw, v_sc_raised, o2_sc):
+        for plane in (tab_sc, w_sc_raw, v_sc_raised, o2_sc):
             nc.vector.memset(plane[:].bitcast(I32), 0)
 
         b3_t, gain2_t, gain1_t = (held([P, PACK], F32, name) for name in ("b3_t", "gain2_t", "gain1_t"))
@@ -75,17 +79,20 @@ def tile_list_fader_balance_mix_kernel(tc, tab_words, tab_scales, offs, gT, w1, 
         w3_raw = held([P, PASSES * H], I32, "w3_raw")
         w2_raw = held([P, PASSES * 2 * H], U8, "w2_raw")
         w1_raw = [held([P, PACK, H], F32, f"w1_raw{a}") for a in range(PASSES)]
-        o_raw = [held([P, 2, PACK, P * PAIR], F32, f"o_raw{half}") for half in range(HALVES)]
+        o_raw = [placed_at(half, 0, [P, 2, PACK, P * PAIR], F32, f"o_raw{half}") for half in range(HALVES)]
         o2_codes = [held([P, P * PAIR], I32, f"o2_codes{half}") for half in range(HALVES)]
         state = [held([P, T], F32, f"state{n}") for n in range(HALVES * PAIR)]
 
-        def load_w_scales(queue, plane, scales):
-            for r in range(ROWS):
-                queue.dma_start(out=plane[r:P:32, :].bitcast(I32).rearrange("q (a c) -> q a c", a=PASSES),
+        def load_w_scales(queue, first, scales, rows):
+            for r in rows:
+                queue.dma_start(out=w_sc_raw[first + r : P : 32, :].bitcast(I32).rearrange("q (a c) -> q a c", a=PASSES),
                                 in_=scales.bitcast(I32).rearrange("a (q r) c -> r q a c", r=ROWS)[r])
 
         def load_rows(tile, rows):
             nc.sync.dma_start(out=tile, in_=rows.rearrange("(p j) c -> p j c", j=PACK))
+
+        def load_table(a):
+            nc.sync.dma_start(out=tab_w[a][:], in_=tab_words[a].rearrange("p t i -> p (t i)").bitcast(I32))
 
         def load_state(n):
             nc.sync.dma_start(out=state[n][:], in_=gT[n * P : (n + 1) * P, :])
@@ -100,22 +107,23 @@ def tile_list_fader_balance_mix_kernel(tc, tab_words, tab_scales, offs, gT, w1, 
             queue.dma_start(out=tile[:], in_=vec.rearrange("(p t) -> p t", t=PACK))
 
         load_vector(nc.sync, b3_t, b3)
-        load_vector(nc.sync, gain2_t, gain2)
         for r in range(ROWS):
             nc.sync.dma_start(out=tab_sc[r:P:16, :].bitcast(I32),
                               in_=tab_scales.bitcast(I32).rearrange("a (q r) t -> r q a t", r=ROWS)[r])
-        load_w_scales(nc.gpsimd, w3_sc_raw, w3_scales)
+        load_vector(nc.gpsimd, gain2_t, gain2)
         load_vector(nc.gpsimd, gain1_t, gain1)
+        load_w_scales(nc.gpsimd, LOW, w3_scales, (2, 3))
         for r in range(ROWS):
             nc.gpsimd.dma_start(out=o2_sc[r:P:32, :].bitcast(I32),
                                 in_=o2_scales[0].bitcast(I32).rearrange("(q r) c -> r q c", r=ROWS)[r])
-        for a in range(PASSES):
-            nc.sync.dma_start(out=tab_w[a][:], in_=tab_words[a].rearrange("p t i -> p (t i)").bitcast(I32))
+        load_table(0)
         nc.sync.dma_start(out=w2_raw[:].bitcast(I32).rearrange("p (a c) -> p a c", a=PASSES),
                           in_=w2_words.bitcast(I32).rearrange("a p c -> p a c"))
-        load_w_scales(nc.sync, w2_sc_raw, w2_scales)
+        load_w_scales(nc.sync, 0, w2_scales, range(ROWS))
         nc.sync.dma_start(out=w3_raw[:].rearrange("p (a c) -> p a c", a=PASSES),
                           in_=w3_words.rearrange("a p c i -> p a (c i)").bitcast(I32))
+        load_w_scales(nc.sync, LOW, w3_scales, (0, 1))
+        load_table(1)
 
         v_sc = held([P, S], U8, "v_sc")
         nc.vector.tensor_copy(v_sc[:], tab_sc[:].indirect(offsets[:]))
@@ -153,44 +161,44 @@ def tile_list_fader_balance_mix_kernel(tc, tab_words, tab_scales, offs, gT, w1, 
 
         w3_codes = held([P, PASSES * H], U32, "w3_codes")
         w2_codes = held([P, PASSES * 2 * H], U8, "w2_codes")
-        w2_sc = held([P, PASSES * H], U8, "w2_sc")
+        w_sc = held([P, PASSES * H], U8, "w_sc")
         reorder(nc.scalar.copy, w2_codes[:].bitcast(U16), w2_raw[:].bitcast(U16), "a m t")
         reorder(nc.scalar.copy, w3_codes[:], w3_raw[:].bitcast(U32), "a m t")
         gather_words(0, slice(0, S), "v_slot0")
+        reorder(nc.vector.tensor_copy, w_sc[:], w_sc_raw[:], "a t m")
         gather_words(1, slice(0, S // 2), "v_slot1")
-        reorder(nc.vector.tensor_copy, w2_sc[:], w2_sc_raw[:], "a t m")
-        gather_words(1, slice(S // 2, S), "w2_sc_slot")
-        w3_sc = shared([P, PASSES * H], U8, "w3_sc", "tab_slot1")
-        reorder(nc.vector.tensor_copy, w3_sc[:], w3_sc_raw[:], "a t m")
-
-        def gpsimd_cast(dst, src):
-            nc.gpsimd.tensor_scalar(dst, src, 1.0, 0.0, ALU.mult, ALU.add)
+        gather_words(1, slice(S // 2, S), "v_slot2")
 
         w1_codes = held([P, PASSES * H], U32, "w1_codes")
         w1_sc = held([P, PASSES * H], U8, "w1_sc")
-        w1_bf = shared([P, PASSES, PACK * H], BF16, "w1_bf", "w1_slot")[:]
+        w1_bf = [shared([P, PACK * H], BF16, "w1_bf", f"w1_slot{a}") for a in range(PASSES)]
 
-        def cast_w1(cast, a, columns, walk):
-            cast(w1_bf[:, a, :].rearrange("p (t m j) -> p m t j", t=PACK, j=PACK)[:, columns].rearrange(f"p m t j -> p {walk}"),
-                 w1_raw[a][:].rearrange("p j (m t) -> p m t j", t=PACK)[:, columns].rearrange(f"p m t j -> p {walk}"))
+        def cast_w1(a):
+            nc.scalar.copy(w1_bf[a][:].rearrange("p (t m j) -> p m j t", t=PACK, j=PACK),
+                           w1_raw[a][:].rearrange("p j (m t) -> p m j t", t=PACK))
+
+        def quantize_w1(a):
+            cols = slice(a * H, (a + 1) * H)
+            nc.vector.quantize_mx(out=w1_codes[:, cols].bitcast(FP8X4), scales=w1_sc[:, cols], in_=w1_bf[a][:])
 
         def w1_side(first):
             return w1_codes[:, first : first + P].bitcast(FP8X4), w1_sc[:, first : first + P]
 
         def w2_side(first):
-            return w2_codes[:, 2 * first : 2 * (first + P)].bitcast(FP4X4), w2_sc[:, first : first + P]
+            return w2_codes[:, 2 * first : 2 * (first + P)].bitcast(FP4X4), w_sc[:, first : first + P]
 
         def w3_side(first):
-            return w3_codes[:, first : first + P].bitcast(FP8X4), w3_sc[:, first : first + P]
+            return w3_codes[:, first : first + P].bitcast(FP8X4), w_sc[LOW:P, first : first + P]
 
-        def first_product(bank, side, first, entries):
+        def first_product(bank, side, first, entries, order, passes=range(PASSES)):
             count = bank.shape[1]
-            for a in range(PASSES):
+            for step in passes:
+                a = order[step]
                 for e in range(count):
                     codes, scales = side(a * H + (first + e) * P)
                     nc.tensor.matmul_mx(out=bank[:, e, :], lhsT=codes, lhsT_scale=scales,
                                         rhs=v_words(a, entries).bitcast(FP8X4), rhs_scale=v_planes[a][:, entries],
-                                        start=(a == 0 and e == 0), stop=(a == PASSES - 1 and e == count - 1))
+                                        start=(step == 0 and e == 0), stop=(step == PASSES - 1 and e == count - 1))
 
         def along_r(vec):
             return vec[:].unsqueeze(1).to_broadcast([P, P, PACK])
@@ -205,23 +213,24 @@ def tile_list_fader_balance_mix_kernel(tc, tab_words, tab_scales, offs, gT, w1, 
 
         def activate_woven(name, c, act):
             side, func = branches[name][:2]
-            for s in range(CH // P):
-                bank = ring_bank([P, PACK, P])
-                first_product(bank, side, 0, slice(c * CH + s * P, c * CH + (s + 1) * P))
-                nc.scalar.activation(woven(act[:, s * P * PACK : (s + 1) * P * PACK]),
-                                     bank[:].rearrange("p t n -> p n t"), func)
+            banks = [ring_bank([P, PACK, P]) for s in range(CH // P)]
+            for s, bank in enumerate(banks):
+                first_product(bank, side, 0, slice(c * CH + s * P, c * CH + (s + 1) * P), (0, 1), range(PASSES - 1))
+            for s, bank in enumerate(banks):
+                first_product(bank, side, 0, slice(c * CH + s * P, c * CH + (s + 1) * P), (0, 1), (PASSES - 1,))
+                nc.scalar.activation(woven(act[s]), bank[:].rearrange("p t n -> p n t"), func)
             return act
 
         def gain_on_gpsimd(name, act, dst):
             for s in range(CH // P):
                 part = slice(s * P * PACK, (s + 1) * P * PACK)
-                nc.gpsimd.tensor_tensor(woven(dst[:, part]), woven(act[:, part]), along_r(branches[name][2]), ALU.mult)
+                nc.gpsimd.tensor_tensor(woven(dst[:, part]), woven(act[s]), along_r(branches[name][2]), ALU.mult)
 
         def activate(name, c, pairs):
             side, func = branches[name][:2]
             for pair, act in enumerate(pairs):
                 bank = ring_bank([P, 2, CH])
-                first_product(bank, side, 2 * pair, chunk(c))
+                first_product(bank, side, 2 * pair, chunk(c), (0, 1))
                 nc.scalar.activation(act, bank[:], func)
 
         def gain_on_scalar(name, pairs, slices):
@@ -242,18 +251,16 @@ def tile_list_fader_balance_mix_kernel(tc, tab_words, tab_scales, offs, gT, w1, 
         def affine_by_vector(c, dst):
             for s in range(CH // P):
                 bank = psum.tile([P, PACK, P], F32, name="x3_bank", bufs=8 - RING)
-                first_product(bank, w3_side, 0, slice(c * CH + s * P, c * CH + (s + 1) * P))
+                first_product(bank, w3_side, 0, slice(c * CH + s * P, c * CH + (s + 1) * P), (1, 0))
                 nc.vector.tensor_tensor(woven(dst[:, s * P * PACK : (s + 1) * P * PACK]),
                                         bank[:].rearrange("p t n -> p n t"), along_r(b3_t), ALU.add)
 
-        def affine_by_scalar(c, dst, slices):
-            for pair in range(PACK // 2):
-                bank = ring_bank([P, 2, CH])
-                first_product(bank, w3_side, 2 * pair, chunk(c))
-                for e in range(2):
-                    t = 2 * pair + e
-                    nc.scalar.activation(slices[:, t, :], bank[:, e, :], ACT.Identity, bias=b3_t[:, t : t + 1])
-            weave(nc.scalar.copy, dst, slices)
+        def affine_by_scalar(entries, slices):
+            for t in range(PACK):
+                bank = ring_bank([P, 1, entries.stop - entries.start])
+                first_product(bank, w3_side, t, entries, (1, 0))
+                nc.scalar.activation(slices[:, t, :], bank[:, 0, :], ACT.Identity, bias=b3_t[:, t : t + 1])
+            return slices
 
         h_place = {}
 
@@ -267,6 +274,10 @@ def tile_list_fader_balance_mix_kernel(tc, tab_words, tab_scales, offs, gT, w1, 
         o_codes = [held([P, 2, P * PAIR], U32, f"o_codes{half}") for half in range(HALVES)]
         o_sc = [held([P, 2, P * PAIR], U8, f"o_sc{half}") for half in range(HALVES)]
 
+        def cast_o(half, o_bf):
+            for i in range(2):
+                weave(nc.scalar.copy, o_bf[:, i, :], o_raw[half][:, i])
+
         def quantize_o(half, o_bf):
             nc.vector.quantize_mx(out=o_codes[half][:].rearrange("p i c -> p (i c)").bitcast(FP8X4),
                                   scales=o_sc[half][:].rearrange("p i c -> p (i c)"),
@@ -274,9 +285,9 @@ def tile_list_fader_balance_mix_kernel(tc, tab_words, tab_scales, offs, gT, w1, 
 
         picked = {}
 
-        def pick(n, slot):
-            picked[n] = shared([P, S], F32, "picked", slot)
-            nc.vector.tensor_copy(picked[n][:], state[n][:].indirect(offsets[:]))
+        def pick(n, tile):
+            picked[n] = tile
+            nc.vector.tensor_copy(tile[:], state[n][:].indirect(offsets[:]))
 
         def second_product(dst, n, c):
             half, own, cols = n // PAIR, slice(n % PAIR * P, (n % PAIR + 1) * P), slice(n * P, (n + 1) * P)
@@ -316,64 +327,64 @@ def tile_list_fader_balance_mix_kernel(tc, tab_words, tab_scales, offs, gT, w1, 
 
         upper, lower = (0, 1), (2, 3)
         h_bf0, h_bf3 = (held([P, 2, CH * PACK], BF16, f"h_bf{c}")[:] for c in (0, 3))
-        mixed = held([P, 4, CH * PACK], BF16, "mixed")
-        h_bf2, h_bf1, o_bf0 = mixed[:, 0:2, :], mixed[:, 1:3, :], mixed[:, 2:4, :]
+        o_bf0 = placed_at(2, 0, [P, 2, CH * PACK], BF16, "o_bf0")[:]
         o_bf1 = shared([P, 2, P * PAIR * PACK], BF16, "o_bf1", "o_bf1_slot")[:]
-        h3_bf = [shared([P, size * CH * PACK], BF16, "h3_bf", f"h3_bf_slot{e}")[:] for e, size in enumerate((2, 1, 1))]
+        h3_bf = [shared([P, size * CH * PACK], BF16, "h3_bf", f"h3_bf_slot{e}")[:] for e, size in enumerate((2, 2))]
 
         def act_tile(slot):
-            return shared([P, CH * PACK], F32, "act", slot)[:]
+            return shared([P, PACK, CH], F32, "act", slot)[:]
+
+        def flat_halves(act):
+            return [flat(half) for half in halves(act)]
 
         def slices_tile(slot):
             return shared([P, PACK, CH], BF16, "slices", slot)[:]
 
-        def as_slices(rows):
-            return flat(rows).bitcast(BF16).rearrange("p (t c) -> p t c", t=PACK)
-
-        gain_on_gpsimd("h2", activate_woven("h2", 0, act_tile("act_a")), h_bf0[:, 0, :])
-        cast_w1(nc.scalar.copy, 0, slice(0, P), "m j t")
-        cast_w1(nc.scalar.copy, 1, slice(0, W1_SPLIT), "m j t")
-        cast_w1(gpsimd_cast, 1, slice(W1_SPLIT, P), "t m j")
-        for c, dst in enumerate((h3_bf[0][:, : CH * PACK], h3_bf[0][:, CH * PACK :], h3_bf[1])):
-            affine_by_vector(c, dst)
+        gain_on_gpsimd("h2", activate_woven("h2", 0, flat_halves(act_tile("act_a"))), h_bf0[:, 0, :])
+        for a in range(PASSES):
+            cast_w1(a)
+        for c in range(2):
+            affine_by_vector(c, h3_bf[0][:, c * CH * PACK : (c + 1) * CH * PACK])
+        quantize_h3((0, 1), h3_bf[0], "h3_slot0")
+        quantize_w1(0)
+        quantize_w1(1)
         act = halves(w1_raw[1][:, :, 0:CH])
         activate("h2", 1, act)
-        nc.vector.quantize_mx(out=w1_codes[:].bitcast(FP8X4), scales=w1_sc[:], in_=w1_bf.rearrange("p a c -> p (a c)"))
-        quantize_h3((0, 1), h3_bf[0], "w1_slot")
-        quantize_h3((2,), h3_bf[1], "h3_slot2")
         slices = gain_on_scalar("h2", act, slices_tile("slices_a"))
-        gain_on_gpsimd("h1", activate_woven("h1", 0, act_tile("act_b")), h_bf0[:, 1, :])
-        weave(nc.scalar.copy, h_bf1[:, 0, :], slices)
-        act = activate_woven("h1", 1, act_tile("act_a"))
-        pick(2, "h3_bf_slot0")
-        pick(3, "picked3")
-        gpsimd_cast(woven(o_bf0[:, 0, :]), o_raw[0][:, 0].rearrange("p j c -> p c j"))
-        weave(nc.scalar.copy, o_bf0[:, 1, :], o_raw[0][:, 1])
+        gain_on_gpsimd("h1", activate_woven("h1", 0, flat_halves(act_tile("act_b"))), h_bf0[:, 1, :])
+        pick(2, shared([P, S], F32, "picked2", "w1_slot1"))
+        pick(3, held([P, S], F32, "picked3"))
+        cast_o(0, o_bf0)
         quantize_h21(0, ("h2", "h1"), h_bf0, "codes0")
         quantize_o(0, o_bf0)
-        pick(0, "picked0")
-        gain_on_gpsimd("h1", act, h_bf1[:, 1, :])
-        affine_by_scalar(3, h3_bf[2], as_slices(o_raw[0][:, 1, 0:2, :]))
+        pick(0, held([P, S], F32, "picked0"))
+        woven_act = flat_halves(placed_at(0, 0, [P, PACK, CH], F32, "act1"))
+        h_bf1 = placed_at(2, 0, [P, 4, CH * PACK], BF16, "h_bf1")[:, 0:2, :]
+        gain_on_gpsimd("h1", activate_woven("h1", 1, woven_act), h_bf1[:, 1, :])
+        woven_act = activate_woven("h2", 2, flat_halves(placed_at(0, 2, [P, PACK, CH], F32, "act2")))
+        weave(nc.scalar.copy, h_bf1[:, 0, :], slices)
         finish(upper[:1], chunk(0), y_tile("y_first0")[:, 0:CH])
         y = second_stage(upper[1:], chunk(0), y_tile("y_first1")[:, 0:CH])
-        woven_act = activate_woven("h2", 2, flat(o_raw[0][:, 1]))
         quantize_h21(1, ("h2", "h1"), h_bf1, "y_first0")
+        h_bf2 = placed_at(2, 2, [P, 2, CH * PACK], BF16, "h_bf2")[:]
         gain_on_gpsimd("h2", woven_act, h_bf2[:, 1, :])
-        pick(1, "picked1")
+        pick(1, placed_at(2, 0, [P, S], F32, "picked1"))
         scatter(1, chunk(0), y)
-        act = halves(o_raw[0][:, 0])
+        act = halves(act_tile("act_b"))
         activate("h1", 2, act)
-        for i in range(2):
-            weave(nc.scalar.copy, o_bf1[:, i, :], o_raw[1][:, i])
+        weave(nc.scalar.copy, h_bf2[:, 0, :], gain_on_scalar("h1", act, slices_tile("slices_b")))
+        cast_o(1, o_bf1)
         quantize_o(1, o_bf1)
-        quantize_h3((3,), h3_bf[2], "o_bf1_slot")
-        finish(upper, chunk(1), flat(o_raw[1][:, 1, 0:2, :]))
-        weave(nc.scalar.copy, h_bf2[:, 0, :], gain_on_scalar("h1", act, as_slices(o_raw[1][:, 1, 2:4, :])))
-        quantize_h21(2, ("h1", "h2"), h_bf2, "codes2")
+        finish(upper, chunk(1), placed_at(1, 0, [P, PAIR * CH], F32, "y1")[:])
+        quantize_h21(2, ("h1", "h2"), h_bf2, "o_bf1_slot")
+        slices = affine_by_scalar(slice(2 * CH, S), placed_at(1, 1, [P, PACK, 2 * CH], BF16, "slices3")[:])
+        finish(lower[:1], slice(0, 2 * CH), y_tile("y2"))
+        weave(nc.scalar.copy, h3_bf[1], slices)
+        quantize_h3((2, 3), h3_bf[1], "h3_slot2")
+        finish(lower[1:], slice(0, 2 * CH), placed_at(1, 1, [P, PAIR * CH], F32, "y3")[:])
+        act = halves(placed_at(1, 2, [P, PACK, CH], F32, "act3"))
         activate("h2", 3, act)
-        finish(lower[:1], slice(0, 2 * CH), flat(o_raw[1][:, 1, 2:4, :]))
         slices = gain_on_scalar("h2", act, slices_tile("slices_a"))
-        finish(lower[1:], slice(0, 2 * CH), flat(o_raw[1][:, 0, 0:2, :]))
         weave(nc.scalar.copy, h_bf3[:, 0, :], slices)
         activate("h1", 3, act)
         finish(upper[:1], chunk(2), y_tile("slices_a")[:, 0:CH])

@@ -25,7 +25,7 @@ GROUP = 16
 CH = 256
 CHUNKS = S // CH
 PAIR = 2
-HALVES = N // (P * PAIR)
+O_PARTS = ((0,), (1,), (2, 3))
 RUN = 4
 REGION = 8192
 RING = 4
@@ -79,9 +79,10 @@ def tile_list_fader_balance_mix_kernel(tc, tab_words, tab_scales, offs, gT, w1, 
         w3_raw = held([P, PASSES * H], I32, "w3_raw")
         w2_raw = held([P, PASSES * 2 * H], U8, "w2_raw")
         w1_raw = [held([P, PACK, H], F32, f"w1_raw{a}") for a in range(PASSES)]
-        o_raw = [placed_at(half, 0, [P, 2, PACK, P * PAIR], F32, f"o_raw{half}") for half in range(HALVES)]
-        o2_codes = [held([P, P * PAIR], I32, f"o2_codes{half}") for half in range(HALVES)]
-        state = [held([P, T], F32, f"state{n}") for n in range(HALVES * PAIR)]
+        o_raw = [placed_at(region, 0, [P, 2, PACK, P * PAIR], F32, f"o_raw{region}")[:, :, :, : P * len(tiles)]
+                 for region, tiles in zip((0, 3, 1), O_PARTS)]
+        o2_codes = [held([P, P * len(tiles)], I32, f"o2_codes{part}") for part, tiles in enumerate(O_PARTS)]
+        state = [held([P, T], F32, f"state{n}") for n in range(N // P)]
 
         def load_w_scales(queue, first, scales, rows):
             for r in rows:
@@ -97,11 +98,11 @@ def tile_list_fader_balance_mix_kernel(tc, tab_words, tab_scales, offs, gT, w1, 
         def load_state(n):
             nc.sync.dma_start(out=state[n][:], in_=gT[n * P : (n + 1) * P, :])
 
-        def load_o(half):
+        def load_o(part):
+            cols = slice(O_PARTS[part][0] * P, (O_PARTS[part][-1] + 1) * P)
             for i, rows in enumerate((o1, o3)):
-                load_rows(o_raw[half][:, i], rows[:, half * P * PAIR : (half + 1) * P * PAIR])
-            nc.sync.dma_start(out=o2_codes[half][:], in_=o2_words[0].rearrange("p c i -> p (c i)").bitcast(I32)[
-                :, half * P * PAIR : (half + 1) * P * PAIR])
+                load_rows(o_raw[part][:, i], rows[:, cols])
+            nc.sync.dma_start(out=o2_codes[part][:], in_=o2_words[0].rearrange("p c i -> p (c i)").bitcast(I32)[:, cols])
 
         def load_vector(queue, tile, vec):
             queue.dma_start(out=tile[:], in_=vec.rearrange("(p t) -> p t", t=PACK))
@@ -138,6 +139,7 @@ def tile_list_fader_balance_mix_kernel(tc, tab_words, tab_scales, offs, gT, w1, 
         load_state(0)
         load_state(1)
         load_o(1)
+        load_o(2)
 
         warm = held([P, 1], F32, "warm")
         nc.scalar.activation(warm[:], b3_t[:, 0:1], ACT.Sigmoid)
@@ -271,11 +273,11 @@ def tile_list_fader_balance_mix_kernel(tc, tab_words, tab_scales, offs, gT, w1, 
             for b, name in enumerate(names):
                 h_place[name, c] = codes[:, b, :], plane[:, b, :]
 
-        o_codes = [held([P, 2, P * PAIR], U32, f"o_codes{half}") for half in range(HALVES)]
-        o_sc = [held([P, 2, P * PAIR], U8, f"o_sc{half}") for half in range(HALVES)]
+        o_codes = [held([P, 2, P * len(tiles)], U32, f"o_codes{part}") for part, tiles in enumerate(O_PARTS)]
+        o_sc = [held([P, 2, P * len(tiles)], U8, f"o_sc{part}") for part, tiles in enumerate(O_PARTS)]
 
-        def cast_o(half, o_bf):
-            for i in range(2):
+        def cast_o(half, o_bf, parts=(0, 1)):
+            for i in parts:
                 weave(nc.scalar.copy, o_bf[:, i, :], o_raw[half][:, i])
 
         def quantize_o(half, o_bf):
@@ -290,7 +292,8 @@ def tile_list_fader_balance_mix_kernel(tc, tab_words, tab_scales, offs, gT, w1, 
             nc.vector.tensor_copy(tile[:], state[n][:].indirect(offsets[:]))
 
         def second_product(dst, n, c):
-            half, own, cols = n // PAIR, slice(n % PAIR * P, (n % PAIR + 1) * P), slice(n * P, (n + 1) * P)
+            half = min(n, len(O_PARTS) - 1)
+            own, cols = slice((n - O_PARTS[half][0]) * P, (n - O_PARTS[half][0] + 1) * P), slice(n * P, (n + 1) * P)
             sides = ((o_codes[half][:, 0, own], o_sc[half][:, 0, own], *h_place["h1", c]),
                      (o2_codes[half][:, own], o2_sc[:, cols], *h_place["h2", c]),
                      (o_codes[half][:, 1, own], o_sc[half][:, 1, own], *h3_place[c]))
@@ -327,9 +330,9 @@ def tile_list_fader_balance_mix_kernel(tc, tab_words, tab_scales, offs, gT, w1, 
 
         upper, lower = (0, 1), (2, 3)
         h_bf0, h_bf3 = (held([P, 2, CH * PACK], BF16, f"h_bf{c}")[:] for c in (0, 3))
-        o_bf0 = placed_at(2, 0, [P, 2, CH * PACK], BF16, "o_bf0")[:]
+        o_bf0 = placed_at(2, 0, [P, 2, P * PACK], BF16, "o_bf0")[:]
         o_bf1 = shared([P, 2, P * PAIR * PACK], BF16, "o_bf1", "o_bf1_slot")[:]
-        h3_bf = [shared([P, size * CH * PACK], BF16, "h3_bf", f"h3_bf_slot{e}")[:] for e, size in enumerate((2, 2))]
+        h3_bf = [shared([P, size * CH * PACK], BF16, "h3_bf", f"h3_bf_slot{e}")[:] for e, size in enumerate((2, 1))]
 
         def act_tile(slot):
             return shared([P, PACK, CH], F32, "act", slot)[:]
@@ -346,7 +349,9 @@ def tile_list_fader_balance_mix_kernel(tc, tab_words, tab_scales, offs, gT, w1, 
         for c in range(2):
             affine_by_vector(c, h3_bf[0][:, c * CH * PACK : (c + 1) * CH * PACK])
         quantize_h3((0, 1), h3_bf[0], "h3_slot0")
+        affine_by_vector(2, h3_bf[1])
         quantize_w1(0)
+        quantize_h3((2,), h3_bf[1], "h3_slot1")
         quantize_w1(1)
         act = halves(w1_raw[1][:, :, 0:CH])
         activate("h2", 1, act)
@@ -364,30 +369,35 @@ def tile_list_fader_balance_mix_kernel(tc, tab_words, tab_scales, offs, gT, w1, 
         woven_act = activate_woven("h2", 2, flat_halves(placed_at(0, 2, [P, PACK, CH], F32, "act2")))
         weave(nc.scalar.copy, h_bf1[:, 0, :], slices)
         finish(upper[:1], chunk(0), y_tile("y_first0")[:, 0:CH])
-        y = second_stage(upper[1:], chunk(0), y_tile("y_first1")[:, 0:CH])
         quantize_h21(1, ("h2", "h1"), h_bf1, "y_first0")
         h_bf2 = placed_at(2, 2, [P, 2, CH * PACK], BF16, "h_bf2")[:]
         gain_on_gpsimd("h2", woven_act, h_bf2[:, 1, :])
         pick(1, placed_at(2, 0, [P, S], F32, "picked1"))
-        scatter(1, chunk(0), y)
         act = halves(act_tile("act_b"))
         activate("h1", 2, act)
         weave(nc.scalar.copy, h_bf2[:, 0, :], gain_on_scalar("h1", act, slices_tile("slices_b")))
-        cast_o(1, o_bf1)
-        quantize_o(1, o_bf1)
-        finish(upper, chunk(1), placed_at(1, 0, [P, PAIR * CH], F32, "y1")[:])
-        quantize_h21(2, ("h1", "h2"), h_bf2, "o_bf1_slot")
-        slices = affine_by_scalar(slice(2 * CH, S), placed_at(1, 1, [P, PACK, 2 * CH], BF16, "slices3")[:])
-        finish(lower[:1], slice(0, 2 * CH), y_tile("y2"))
-        weave(nc.scalar.copy, h3_bf[1], slices)
-        quantize_h3((2, 3), h3_bf[1], "h3_slot2")
-        finish(lower[1:], slice(0, 2 * CH), placed_at(1, 1, [P, PAIR * CH], F32, "y3")[:])
+        o_bf_second = shared([P, 2, P * PACK], BF16, "o_bf_second", "o_second_slot")[:]
+        cast_o(1, o_bf_second)
+        quantize_o(1, o_bf_second)
+        quantize_h21(2, ("h1", "h2"), h_bf2, "o_second_slot")
+        finish(upper[:1], chunk(1), placed_at(3, 0, [P, CH], F32, "y1")[:])
+        slices = affine_by_scalar(chunk(3), placed_at(3, 1, [P, PACK, CH], BF16, "slices3")[:])
+        cast_o(2, o_bf1, (0,))
+        finish(upper[1:], chunk(0), y_tile("y2")[:, 0:CH])
+        cast_o(2, o_bf1, (1,))
+        quantize_o(2, o_bf1)
+        finish(upper[1:], chunk(1), placed_at(1, 0, [P, CH], F32, "y3")[:])
+        h3_last = placed_at(1, 1, [P, CH * PACK], BF16, "h3_last")[:]
+        weave(nc.scalar.copy, h3_last, slices)
+        quantize_h3((3,), h3_last, "h3_slot2")
+        finish(upper[:1], chunk(2), placed_at(3, 1, [P, CH], F32, "y6")[:])
         act = halves(placed_at(1, 2, [P, PACK, CH], F32, "act3"))
         activate("h2", 3, act)
+        finish(lower[:1], slice(0, 2 * CH), y_tile("y4"))
         slices = gain_on_scalar("h2", act, slices_tile("slices_a"))
+        finish(lower[1:], slice(0, 2 * CH), y_tile("y5"))
         weave(nc.scalar.copy, h_bf3[:, 0, :], slices)
         activate("h1", 3, act)
-        finish(upper[:1], chunk(2), y_tile("slices_a")[:, 0:CH])
         weave(nc.scalar.copy, h_bf3[:, 1, :], gain_on_scalar("h1", act, slices_tile("slices_c")))
         quantize_h21(3, ("h2", "h1"), h_bf3, "codes3")
         finish(upper[1:], chunk(2), y_tile("slices_c")[:, 0:CH])

from contextlib import ExitStack

import concourse.mybir as mybir

T, S, K, H, N = 2048, 1024, 1024, 512, 512
FLOPS = 2 * S * (3 * K * H + 3 * H * N)

F32 = mybir.dt.float32
BF16 = mybir.dt.bfloat16
I32 = mybir.dt.int32
U32 = mybir.dt.uint32
U16 = mybir.dt.uint16
U8 = mybir.dt.uint8
FP8X4 = mybir.dt.float8_e4m3fn_x4
FP4X4 = mybir.dt.float4_e2m1fn_x4
ALU = mybir.AluOpType
ACT = mybir.ActivationFunctionType

P = 128
PACK = 4
PASSES = K // (P * PACK)
ROWS = 4
LOW = 4
GROUP = 16
CH = 256
CHUNKS = S // CH
PAIR = 2
O_PARTS = ((0,), (1,), (2, 3))
RUN = 4
REGION = 8192
RING = 4


def tile_list_fader_balance_mix_kernel(tc, tab_words, tab_scales, offs, gT, w1, w2_words, w2_scales,
                                                     w3_words, w3_scales, gain1, gain2, b3, o1, o2_words, o2_scales,
                                                     o3, out):
    nc = tc.nc
    with ExitStack() as ctx:
        keep = ctx.enter_context(tc.tile_pool(name="keep", bufs=1))
        placed = ctx.enter_context(tc.tile_pool(name="placed", bufs=1))
        psum = ctx.enter_context(tc.psum_pool(name="psum", bufs=1))

        def held(shape, dtype, name):
            return keep.tile(shape, dtype, name=name, align_bytes=64)

        def shared(shape, dtype, name, slot):
            return keep.tile(shape, dtype, name=name, tag=slot, align_bytes=64)

        def placed_at(region, part, shape, dtype, name):
            return placed.tile(shape, dtype, name=name, offset=region * REGION + part * REGION // 4, align_bytes=64)

        turns = []

        def ring_bank(shape):
            turns.append(shape)
            return psum.tile(shape, F32, name="ring", tag=f"ring{len(turns) % RING}")

        def listed(entries):
            return offsets[:, entries.start // GROUP : entries.stop // GROUP]

        def flat(rows):
            return rows.rearrange("p j c -> p (j c)")

        def chunk(c):
            return slice(c * CH, (c + 1) * CH)

        offsets = keep.tile([P, S // GROUP], U16, name="offsets")
        nc.sync.dma_start(offsets[:], offs)

        tab_sc = held([P, T], U8, "tab_sc")
        w_sc_raw = held([P, PASSES * H], U8, "w_sc_raw")
        v_sc_raised = held([P, S], U8, "v_sc_raised")
        o2_sc = held([P, N], U8, "o2_sc")
        for plane in (tab_sc, w_sc_raw, v_sc_raised, o2_sc):
            nc.vector.memset(plane[:].bitcast(I32), 0)

        b3_t, gain2_t, gain1_t = (held([P, PACK], F32, name) for name in ("b3_t", "gain2_t", "gain1_t"))
        tab_w = [shared([P, T], I32, "tab_w", f"tab_slot{a}") for a in range(PASSES)]
        w3_raw = held([P, PASSES * H], I32, "w3_raw")
        w2_raw = held([P, PASSES * 2 * H], U8, "w2_raw")
        w1_raw = [held([P, PACK, H], F32, f"w1_raw{a}") for a in range(PASSES)]
        o_raw = [placed_at(region, 0, [P, 2, PACK, P * PAIR], F32, f"o_raw{region}")[:, :, :, : P * len(tiles)]
                 for region, tiles in zip((0, 3, 1), O_PARTS)]
        o2_codes = [held([P, P * len(tiles)], I32, f"o2_codes{part}") for part, tiles in enumerate(O_PARTS)]
        state = [held([P, T], F32, f"state{n}") for n in range(N // P)]

        def load_w_scales(queue, first, scales, rows):
            for r in rows:
                queue.dma_start(out=w_sc_raw[first + r : P : 32, :].bitcast(I32).rearrange("q (a c) -> q a c", a=PASSES),
                                in_=scales.bitcast(I32).rearrange("a (q r) c -> r q a c", r=ROWS)[r])

        def load_rows(tile, rows):
            nc.sync.dma_start(out=tile, in_=rows.rearrange("(p j) c -> p j c", j=PACK))

        def load_table(a):
            nc.sync.dma_start(out=tab_w[a][:], in_=tab_words[a].rearrange("p t i -> p (t i)").bitcast(I32))

        def load_state(n):
            nc.sync.dma_start(out=state[n][:], in_=gT[n * P : (n + 1) * P, :])

        def load_o(part):
            cols = slice(O_PARTS[part][0] * P, (O_PARTS[part][-1] + 1) * P)
            for i, rows in enumerate((o1, o3)):
                load_rows(o_raw[part][:, i], rows[:, cols])
            nc.sync.dma_start(out=o2_codes[part][:], in_=o2_words[0].rearrange("p c i -> p (c i)").bitcast(I32)[:, cols])

        def load_vector(queue, tile, vec):
            queue.dma_start(out=tile[:], in_=vec.rearrange("(p t) -> p t", t=PACK))

        load_vector(nc.sync, b3_t, b3)
        for r in range(ROWS):
            nc.sync.dma_start(out=tab_sc[r:P:16, :].bitcast(I32),
                              in_=tab_scales.bitcast(I32).rearrange("a (q r) t -> r q a t", r=ROWS)[r])
        load_vector(nc.gpsimd, gain2_t, gain2)
        load_vector(nc.gpsimd, gain1_t, gain1)
        load_w_scales(nc.gpsimd, LOW, w3_scales, (2, 3))
        for r in range(ROWS):
            nc.gpsimd.dma_start(out=o2_sc[r:P:32, :].bitcast(I32),
                                in_=o2_scales[0].bitcast(I32).rearrange("(q r) c -> r q c", r=ROWS)[r])
        load_table(0)
        nc.sync.dma_start(out=w2_raw[:].bitcast(I32).rearrange("p (a c) -> p a c", a=PASSES),
                          in_=w2_words.bitcast(I32).rearrange("a p c -> p a c"))
        load_w_scales(nc.sync, 0, w2_scales, range(ROWS))
        nc.sync.dma_start(out=w3_raw[:].rearrange("p (a c) -> p a c", a=PASSES),
                          in_=w3_words.rearrange("a p c i -> p a (c i)").bitcast(I32))
        load_w_scales(nc.sync, LOW, w3_scales, (0, 1))
        load_table(1)

        v_sc = held([P, S], U8, "v_sc")
        nc.vector.tensor_copy(v_sc[:], tab_sc[:].indirect(offsets[:]))
        for r in range(ROWS):
            nc.sync.dma_start(out=v_sc_raised[r:P:32, :].bitcast(I32), in_=v_sc[16 + r : P : 32, :].bitcast(I32))

        for a in range(PASSES):
            load_rows(w1_raw[a][:], w1[a * P * PACK : (a + 1) * P * PACK, :])
        load_state(2)
        load_state(3)
        load_o(0)
        load_state(0)
        load_state(1)
        load_o(1)
        load_o(2)

        warm = held([P, 1], F32, "warm")
        nc.scalar.activation(warm[:], b3_t[:, 0:1], ACT.Sigmoid)

        v_planes = (v_sc, v_sc_raised)
        v_parts = []

        def gather_words(a, entries, slot):
            part = shared([P, entries.stop - entries.start], U32, "v_w", slot)
            nc.vector.tensor_copy(part[:], tab_w[a][:].bitcast(U32).indirect(listed(entries)))
            v_parts.append((a, entries, part))

        def v_words(a, entries):
            for b, whole, part in v_parts:
                if a == b and whole.start <= entries.start < whole.stop:
                    return part[:, entries.start - whole.start : entries.stop - whole.start]

        def reorder(copy, dst, src, walk):
            copy(dst.rearrange(f"p (a t m) -> p {walk}", a=PASSES, t=PACK),
                 src.rearrange(f"p (a m t) -> p {walk}", a=PASSES, t=PACK))

        w3_codes = held([P, PASSES * H], U32, "w3_codes")
        w2_codes = held([P, PASSES * 2 * H], U8, "w2_codes")
        w_sc = held([P, PASSES * H], U8, "w_sc")
        reorder(nc.scalar.copy, w2_codes[:].bitcast(U16), w2_raw[:].bitcast(U16), "a m t")
        reorder(nc.scalar.copy, w3_codes[:], w3_raw[:].bitcast(U32), "a m t")
        gather_words(0, slice(0, S), "v_slot0")
        reorder(nc.vector.tensor_copy, w_sc[:], w_sc_raw[:], "a t m")
        gather_words(1, slice(0, S // 2), "v_slot1")
        gather_words(1, slice(S // 2, S), "v_slot2")

        w1_codes = held([P, PASSES * H], U32, "w1_codes")
        w1_sc = held([P, PASSES * H], U8, "w1_sc")
        w1_bf = [shared([P, PACK * H], BF16, "w1_bf", f"w1_slot{a}") for a in range(PASSES)]

        def cast_w1(a):
            nc.scalar.copy(w1_bf[a][:].rearrange("p (t m j) -> p m j t", t=PACK, j=PACK),
                           w1_raw[a][:].rearrange("p j (m t) -> p m j t", t=PACK))

        def quantize_w1(a):
            cols = slice(a * H, (a + 1) * H)
            nc.vector.quantize_mx(out=w1_codes[:, cols].bitcast(FP8X4), scales=w1_sc[:, cols], in_=w1_bf[a][:])

        def w1_side(first):
            return w1_codes[:, first : first + P].bitcast(FP8X4), w1_sc[:, first : first + P]

        def w2_side(first):
            return w2_codes[:, 2 * first : 2 * (first + P)].bitcast(FP4X4), w_sc[:, first : first + P]

        def w3_side(first):
            return w3_codes[:, first : first + P].bitcast(FP8X4), w_sc[LOW:P, first : first + P]

        def first_product(bank, side, first, entries, order, passes=range(PASSES)):
            count = bank.shape[1]
            for step in passes:
                a = order[step]
                for e in range(count):
                    codes, scales = side(a * H + (first + e) * P)
                    nc.tensor.matmul_mx(out=bank[:, e, :], lhsT=codes, lhsT_scale=scales,
                                        rhs=v_words(a, entries).bitcast(FP8X4), rhs_scale=v_planes[a][:, entries],
                                        start=(step == 0 and e == 0), stop=(step == PASSES - 1 and e == count - 1))

        def along_r(vec):
            return vec[:].unsqueeze(1).to_broadcast([P, P, PACK])

        def woven(values):
            return values.rearrange("p (n t) -> p n t", t=PACK)

        def weave(copy, dst, slices):
            copy(dst.rearrange("p (c i t) -> p c t i", i=RUN, t=PACK), slices.rearrange("p t (c i) -> p c t i", i=RUN))

        branches = {"h1": (w1_side, ACT.Tanh, gain1_t), "h2": (w2_side, ACT.Sigmoid, gain2_t)}

        def activate_woven(name, c, act):
            side, func = branches[name][:2]
            banks = [ring_bank([P, PACK, P]) for s in range(CH // P)]
            for s, bank in enumerate(banks):
                first_product(bank, side, 0, slice(c * CH + s * P, c * CH + (s + 1) * P), (0, 1), range(PASSES - 1))
            for s, bank in enumerate(banks):
                first_product(bank, side, 0, slice(c * CH + s * P, c * CH + (s + 1) * P), (0, 1), (PASSES - 1,))
                nc.scalar.activation(woven(act[s]), bank[:].rearrange("p t n -> p n t"), func)
            return act

        def gain_on_gpsimd(name, act, dst):
            for s in range(CH // P):
                part = slice(s * P * PACK, (s + 1) * P * PACK)
                nc.gpsimd.tensor_tensor(woven(dst[:, part]), woven(act[s]), along_r(branches[name][2]), ALU.mult)

        def activate(name, c, pairs):
            side, func = branches[name][:2]
            for pair, act in enumerate(pairs):
                bank = ring_bank([P, 2, CH])
                first_product(bank, side, 2 * pair, chunk(c), (0, 1))
                nc.scalar.activation(act, bank[:], func)

        def gain_on_scalar(name, pairs, slices):
            gain = branches[name][2]
            for t in range(PACK):
                nc.scalar.activation(slices[:, t, :], pairs[t // 2][:, t % 2, :], ACT.Copy, scale=gain[:, t : t + 1])
            return slices

        h3_place = {}

        def quantize_h3(chunks, values, slot):
            codes = shared([P, len(chunks) * CH], U32, "h3_codes", slot)
            plane = held([P, len(chunks) * CH], U8, f"h3_sc{chunks[0]}")
            nc.vector.quantize_mx(out=codes[:].bitcast(FP8X4), scales=plane[:], in_=values)
            for e, c in enumerate(chunks):
                h3_place[c] = codes[:, chunk(e)], plane[:, chunk(e)]

        def affine_by_vector(c, dst):
            for s in range(CH // P):
                bank = psum.tile([P, PACK, P], F32, name="x3_bank", bufs=8 - RING)
                first_product(bank, w3_side, 0, slice(c * CH + s * P, c * CH + (s + 1) * P), (1, 0))
                nc.vector.tensor_tensor(woven(dst[:, s * P * PACK : (s + 1) * P * PACK]),
                                        bank[:].rearrange("p t n -> p n t"), along_r(b3_t), ALU.add)

        def affine_by_scalar(entries, slices):
            for t in range(PACK):
                bank = ring_bank([P, 1, entries.stop - entries.start])
                first_product(bank, w3_side, t, entries, (1, 0))
                nc.scalar.activation(slices[:, t, :], bank[:, 0, :], ACT.Identity, bias=b3_t[:, t : t + 1])
            return slices

        h_place = {}

        def quantize_h21(c, names, h_bf, slot):
            codes = shared([P, 2, CH], U32, "h_codes", slot)
            plane = held([P, 2, CH], U8, f"h_sc{c}")
            nc.vector.quantize_mx(out=flat(codes[:]).bitcast(FP8X4), scales=flat(plane[:]), in_=flat(h_bf))
            for b, name in enumerate(names):
                h_place[name, c] = codes[:, b, :], plane[:, b, :]

        o_codes = [held([P, 2, P * len(tiles)], U32, f"o_codes{part}") for part, tiles in enumerate(O_PARTS)]
        o_sc = [held([P, 2, P * len(tiles)], U8, f"o_sc{part}") for part, tiles in enumerate(O_PARTS)]

        def cast_o(half, o_bf, parts=(0, 1)):
            for i in parts:
                weave(nc.scalar.copy, o_bf[:, i, :], o_raw[half][:, i])

        def quantize_o(half, o_bf):
            nc.vector.quantize_mx(out=o_codes[half][:].rearrange("p i c -> p (i c)").bitcast(FP8X4),
                                  scales=o_sc[half][:].rearrange("p i c -> p (i c)"),
                                  in_=o_bf.rearrange("p i c -> p (i c)"))

        picked = {}

        def pick(n, tile):
            picked[n] = tile
            nc.vector.tensor_copy(tile[:], state[n][:].indirect(offsets[:]))

        def second_product(dst, n, c):
            half = min(n, len(O_PARTS) - 1)
            own, cols = slice((n - O_PARTS[half][0]) * P, (n - O_PARTS[half][0] + 1) * P), slice(n * P, (n + 1) * P)
            sides = ((o_codes[half][:, 0, own], o_sc[half][:, 0, own], *h_place["h1", c]),
                     (o2_codes[half][:, own], o2_sc[:, cols], *h_place["h2", c]),
                     (o_codes[half][:, 1, own], o_sc[half][:, 1, own], *h3_place[c]))
            for b, (o_words, o_plane, h_words, h_plane) in enumerate(sides):
                nc.tensor.matmul_mx(out=dst, lhsT=o_words.bitcast(FP8X4), lhsT_scale=o_plane,
                                    rhs=h_words.bitcast(FP8X4), rhs_scale=h_plane, start=(b == 0), stop=(b == 2))

        def second_stage(tiles, entries, y):
            width = entries.stop - entries.start
            bank = ring_bank([P, len(tiles), width])
            for e, n in enumerate(tiles):
                for c in range(entries.start // CH, entries.stop // CH):
                    second_product(bank[:, e, c * CH - entries.start : (c + 1) * CH - entries.start], n, c)
            y = y.rearrange("p (e c) -> p e c", e=len(tiles))
            nc.scalar.copy(y, bank[:])
            return {n: y[:, e, :] for e, n in enumerate(tiles)}

        def scatter(n, entries, y):
            nc.vector.tensor_tensor(state[n][:].indirect(listed(entries)), y[n],
                                    picked[n][:, entries], ALU.mult)
            if entries.stop == S:
                nc.sync.dma_start(out=out[n * P : (n + 1) * P, :], in_=state[n][:])

        def finish(tiles, entries, y):
            y = second_stage(tiles, entries, y)
            for n in tiles:
                scatter(n, entries, y)

        def y_tile(slot):
            return shared([P, PAIR * CH], F32, "y", slot)[:]

        def halves(act):
            return act[:, 0:2, :], act[:, 2:4, :]

        upper, lower = (0, 1), (2, 3)
        h_bf0, h_bf3 = (held([P, 2, CH * PACK], BF16, f"h_bf{c}")[:] for c in (0, 3))
        o_bf0 = placed_at(2, 0, [P, 2, P * PACK], BF16, "o_bf0")[:]
        o_bf1 = shared([P, 2, P * PAIR * PACK], BF16, "o_bf1", "o_bf1_slot")[:]
        h3_bf = [shared([P, size * CH * PACK], BF16, "h3_bf", f"h3_bf_slot{e}")[:] for e, size in enumerate((2, 1))]

        def act_tile(slot):
            return shared([P, PACK, CH], F32, "act", slot)[:]

        def flat_halves(act):
            return [flat(half) for half in halves(act)]

        def slices_tile(slot):
            return shared([P, PACK, CH], BF16, "slices", slot)[:]

        gain_on_gpsimd("h2", activate_woven("h2", 0, flat_halves(act_tile("act_a"))), h_bf0[:, 0, :])
        for a in range(PASSES):
            cast_w1(a)
        for c in range(2):
            affine_by_vector(c, h3_bf[0][:, c * CH * PACK : (c + 1) * CH * PACK])
        quantize_h3((0, 1), h3_bf[0], "h3_slot0")
        affine_by_vector(2, h3_bf[1])
        quantize_w1(0)
        quantize_h3((2,), h3_bf[1], "h3_slot1")
        quantize_w1(1)
        act = halves(w1_raw[1][:, :, 0:CH])
        activate("h2", 1, act)
        slices = gain_on_scalar("h2", act, slices_tile("slices_a"))
        gain_on_gpsimd("h1", activate_woven("h1", 0, flat_halves(act_tile("act_b"))), h_bf0[:, 1, :])
        pick(2, shared([P, S], F32, "picked2", "w1_slot1"))
        pick(3, held([P, S], F32, "picked3"))
        cast_o(0, o_bf0)
        quantize_h21(0, ("h2", "h1"), h_bf0, "codes0")
        quantize_o(0, o_bf0)
        pick(0, held([P, S], F32, "picked0"))
        woven_act = flat_halves(placed_at(0, 0, [P, PACK, CH], F32, "act1"))
        h_bf1 = placed_at(2, 0, [P, 4, CH * PACK], BF16, "h_bf1")[:, 0:2, :]
        gain_on_gpsimd("h1", activate_woven("h1", 1, woven_act), h_bf1[:, 1, :])
        woven_act = activate_woven("h2", 2, flat_halves(placed_at(0, 2, [P, PACK, CH], F32, "act2")))
        weave(nc.scalar.copy, h_bf1[:, 0, :], slices)
        finish(upper[:1], chunk(0), y_tile("y_first0")[:, 0:CH])
        quantize_h21(1, ("h2", "h1"), h_bf1, "y_first0")
        h_bf2 = placed_at(2, 2, [P, 2, CH * PACK], BF16, "h_bf2")[:]
        gain_on_gpsimd("h2", woven_act, h_bf2[:, 1, :])
        pick(1, placed_at(2, 0, [P, S], F32, "picked1"))
        act = halves(act_tile("act_b"))
        activate("h1", 2, act)
        weave(nc.scalar.copy, h_bf2[:, 0, :], gain_on_scalar("h1", act, slices_tile("slices_b")))
        o_bf_second = shared([P, 2, P * PACK], BF16, "o_bf_second", "o_second_slot")[:]
        cast_o(1, o_bf_second)
        quantize_o(1, o_bf_second)
        quantize_h21(2, ("h1", "h2"), h_bf2, "o_second_slot")
        finish(upper[:1], chunk(1), placed_at(3, 0, [P, CH], F32, "y1")[:])
        slices = affine_by_scalar(chunk(3), placed_at(3, 1, [P, PACK, CH], BF16, "slices3")[:])
        cast_o(2, o_bf1, (0,))
        finish(upper[1:], chunk(0), y_tile("y2")[:, 0:CH])
        cast_o(2, o_bf1, (1,))
        quantize_o(2, o_bf1)
        finish(upper[1:], chunk(1), placed_at(1, 0, [P, CH], F32, "y3")[:])
        h3_last = placed_at(1, 1, [P, CH * PACK], BF16, "h3_last")[:]
        weave(nc.scalar.copy, h3_last, slices)
        quantize_h3((3,), h3_last, "h3_slot2")
        finish(upper[:1], chunk(2), placed_at(3, 1, [P, CH], F32, "y6")[:])
        act = halves(placed_at(1, 2, [P, PACK, CH], F32, "act3"))
        activate("h2", 3, act)
        finish(lower[:1], slice(0, 2 * CH), y_tile("y4"))
        slices = gain_on_scalar("h2", act, slices_tile("slices_a"))
        finish(lower[1:], slice(0, 2 * CH), y_tile("y5"))
        weave(nc.scalar.copy, h_bf3[:, 0, :], slices)
        activate("h1", 3, act)
        weave(nc.scalar.copy, h_bf3[:, 1, :], gain_on_scalar("h1", act, slices_tile("slices_c")))
        quantize_h21(3, ("h2", "h1"), h_bf3, "codes3")
        finish(upper[1:], chunk(2), y_tile("slices_c")[:, 0:CH])
        for n in upper:
            finish((n,), chunk(3), y_tile(f"y_last{n}")[:, 0:CH])
        for n in lower:
            finish((n,), slice(2 * CH, S), y_tile(f"y_last{n}"))
